import numpy as np
import ml_dtypes


def mxq(x, axis, fmt="e4m3"):
    dtype, down = {"e4m3": (ml_dtypes.float8_e4m3fn, 7), "e5m2": (ml_dtypes.float8_e5m2, 14)}[fmt]
    v = np.moveaxis(np.asarray(x, np.float32).astype(ml_dtypes.bfloat16).astype(np.float64), axis, -1)
    blocks = v.reshape(v.shape[:-1] + (-1, 32))
    amax = np.abs(blocks).max(-1, keepdims=True)
    byte = np.maximum(np.where(amax > 0, np.frexp(amax)[1] - 1 + 127, 0) - down, 1)
    scale = np.exp2(byte - 127.0)
    codes = (blocks / scale).astype(np.float32).astype(dtype).astype(np.float64)
    return np.moveaxis((codes * scale).reshape(v.shape), -1, axis)


WIDE = False


def mx_kscale(k):
    if not WIDE:
        return np.ones(k)
    levels = np.array([10, -10, 5, -5, 0])
    if k % 512:
        return np.exp2(np.random.permutation(np.resize(levels, k // 32))).repeat(32)
    a = np.empty((k // 512, 16))
    for p in range(k // 512):
        a[p, :8] = np.random.permutation(np.resize(levels, 8))
        for g in range(8):
            far = levels[np.abs(levels - a[p, g]) >= 10]
            a[p, g + 8] = far[np.random.randint(len(far))]
    return np.exp2(a.ravel()).repeat(32)


def f64(x):
    return np.asarray(x).astype(np.float64)


def striped(idx):
    return np.tile(idx.reshape(-1, 16).T, (8, 1)).astype(np.uint16)


def unstriped(offs):
    return offs[:16].T.reshape(-1).astype(np.int64)


E2M1 = np.array([0.0, 0.5, 1.0, 1.5, 2.0, 3.0, 4.0, 6.0, -0.0, -0.5, -1.0, -1.5, -2.0, -3.0, -4.0, -6.0])


def pack_weight(w, fmt):
    k, n = w.shape
    w = f64(np.asarray(w, np.float32).astype(ml_dtypes.bfloat16)).reshape(k // 32, 32, n)
    amax = np.abs(w).max(1)
    if fmt == "e4m3":
        byte = np.frexp(amax)[1] - 1 + 127 - 7
    else:
        mant, ex = np.frexp(amax / 6.0)
        byte = np.where(mant > 0.5, ex, ex - 1) + 127
    byte = np.clip(np.where(amax > 0, byte, 1), 1, 254)
    scaled = (w * np.exp2(127.0 - byte)[:, None, :]).reshape(k, n).astype(np.float32)
    by_word = np.ascontiguousarray(scaled.reshape(k // 512, 128, 4, n).transpose(0, 1, 3, 2))
    if fmt == "e4m3":
        words = by_word.astype(ml_dtypes.float8_e4m3fn).view(np.uint8)
    else:
        c = by_word.astype(ml_dtypes.float4_e2m1fn).view(np.uint8) & 0xF
        words = (c[..., 0::2] | (c[..., 1::2] << 4)).reshape(k // 512, 128, 2 * n)
    return np.ascontiguousarray(words), np.ascontiguousarray(byte.astype(np.uint8).reshape(k // 512, 16, n))


def unpack_weight(words, scales, fmt):
    g, _, n = scales.shape
    words = np.ascontiguousarray(words).reshape(g, 128, n, -1)
    if fmt == "e4m3":
        vals = words.view(ml_dtypes.float8_e4m3fn).astype(np.float64)
    else:
        nib = np.empty((g, 128, n, 4), np.uint8)
        nib[..., 0::2] = words & 0xF
        nib[..., 1::2] = words >> 4
        vals = E2M1[nib]
    vals = vals * np.repeat(np.exp2(scales.astype(np.float64) - 127.0), 8, axis=1)[..., None]
    return vals.transpose(0, 1, 3, 2).reshape(g * 512, n)


def gelu(v):
    return 0.5 * v * (1.0 + np.tanh(np.sqrt(2.0 / np.pi) * (v + 0.044715 * v**3)))


def bf(x):
    return np.asarray(x, np.float32).astype(ml_dtypes.bfloat16)


def planes(Y):
    n, m = Y.shape
    b = f64(bf(Y)).reshape(n // 32, 32, m)
    amax = np.abs(b).max(1)
    byte = np.clip(np.where(amax > 0, np.frexp(amax)[1] - 1 + 127 - 7, 1), 1, 254)
    codes = (b * np.exp2(127.0 - byte)[:, None, :]).reshape(n, m).astype(np.float32).astype(ml_dtypes.float8_e4m3fn).view(np.uint8)
    words = codes.reshape(n // 512, 128, 4, m).transpose(0, 1, 3, 2)
    return np.ascontiguousarray(words), np.ascontiguousarray(byte.astype(np.uint8).reshape(n // 512, 16, m))


K, T, S, T2, H, N = 1024, 2048, 1024, 2048, 512, 384

def setup_inputs():
    n = np.random.standard_normal
    s = mx_kscale(K)[:, None]
    u = mx_kscale(H)[:, None]
    tab_words, tab_scales = pack_weight(n((K, T)) * s, "e4m3")
    wc_words, wc_scales = pack_weight(0.5 * n((H, N)) / np.sqrt(H) / u, "e2m1")
    return {
        "tab_words": tab_words, "tab_scales": tab_scales,
        "offs": striped(np.random.permutation(T)[:S]),
        "w1": (1.25 * n((K, H)) / np.sqrt(K) / s).astype(np.float32),
        "gain": (np.random.uniform(0.5, 1.5, H) * u[:, 0]).astype(np.float32),
        "page0": (n((H, T2)) * u).astype(np.float32),
        "wgs": np.exp(0.3 * n((128, S))).astype(np.float32),
        "offs2": striped(np.random.permutation(T2)[:S]),
        "wc_words": wc_words, "wc_scales": wc_scales,
        "wd": (n((H, N)) / np.sqrt(H) / u).astype(np.float32),
    }

def reference(tab_words, tab_scales, offs, w1, gain, page0, wgs, offs2, wc_words, wc_scales, wd):
    v = unpack_weight(tab_words, tab_scales, "e4m3")[:, unstriped(offs)]
    a = mxq(f64(w1), 0, "e4m3").T @ v
    h = f64(gain)[:, None] / (1.0 + np.square(a))
    page = f64(page0).copy()
    page[:, unstriped(offs2)] = np.tile(f64(wgs), (H // 128, 1)) * h
    words, scales = planes(page)
    pq = mxq(page, 0, "e4m3")
    phase = unpack_weight(wc_words, wc_scales, "e2m1").T @ pq
    value = mxq(f64(wd), 0, "e4m3").T @ pq
    y = np.cos(phase) * value
    return y, page, words, scales

@@ -1,0 +1,256 @@
+import math
+from contextlib import ExitStack
+
+import concourse.mybir as mybir
+
+K, T, S, T2, H, N = 1024, 2048, 1024, 2048, 512, 384
+FLOPS = 2 * K * H * S + 2 * 2 * H * N * T2
+
+F32 = mybir.dt.float32
+BF16 = mybir.dt.bfloat16
+I32 = mybir.dt.int32
+U32 = mybir.dt.uint32
+U16 = mybir.dt.uint16
+U8 = mybir.dt.uint8
+FP8X4 = mybir.dt.float8_e4m3fn_x4
+FP4X4 = mybir.dt.float4_e2m1fn_x4
+ACT = mybir.ActivationFunctionType
+ALU = mybir.AluOpType
+
+P = 128
+PACK = 4
+QUADS = 4
+BANK = 512
+PASSES = K // (P * PACK)
+HALVES = S // BANK
+CHUNKS = T2 // BANK
+NT = N // P
+
+
+def tile_list_rod_checkpoint_kernel(
+    tc, tab_words, tab_scales, offs, w1, gain, page0, wgs, offs2, wc_words, wc_scales, wd,
+    out_0, out_1, out_2, out_3,
+):
+    nc = tc.nc
+    with ExitStack() as ctx:
+        lists = ctx.enter_context(tc.tile_pool(name="lists", bufs=1))
+        keep = ctx.enter_context(tc.tile_pool(name="keep", bufs=1))
+        work = ctx.enter_context(tc.tile_pool(name="work", bufs=3))
+        psum = ctx.enter_context(tc.psum_pool(name="psum", bufs=1))
+
+        pick = lists.tile([P, S // 16], U16, name="pick")
+        put = lists.tile([P, S // 16], U16, name="put")
+
+        one = keep.tile([P, 8], F32, name="one")
+        warm = keep.tile([P, 8], F32, name="warm")
+        nc.vector.memset(one[:], 1.0)
+        nc.scalar.activation(warm[:], one[:], ACT.Abs_reciprocal_sqrt)
+
+        tab_sc = keep.tile([P, T], U8, name="tab_sc", align_bytes=64)
+        nc.vector.memset(tab_sc[:].bitcast(I32), 0)
+        wc_sc = keep.tile([P, N], U8, name="wc_sc", align_bytes=64)
+        nc.vector.memset(wc_sc[:].bitcast(I32), 0)
+
+        tab = [keep.tile([P, T], U32, name=f"tab{a}", align_bytes=64) for a in range(PASSES)]
+        w1_raw = [keep.tile([P, PACK, H], F32, name=f"w1_raw{a}") for a in range(PASSES)]
+        w1_rows = w1.rearrange("(a p j) c -> a p j c", p=P, j=PACK)
+
+        def tab_src(a):
+            return tab_words[a].rearrange("p t i -> p (t i)").bitcast(I32)
+
+        nc.sync.dma_start(pick[:], offs)
+        nc.sync.dma_start(tab[0][:].bitcast(I32), tab_src(0))
+        for q in range(QUADS):
+            nc.sync.dma_start(
+                tab_sc[32 * q : 32 * q + 4 * PASSES, :].bitcast(I32),
+                tab_scales[:, 4 * q : 4 * q + 4, :].bitcast(I32),
+            )
+        gains = keep.tile([P, 8], F32, name="gains")
+        nc.sync.dma_start(gains[:, 0:PACK], gain.rearrange("(p t) -> p t", t=PACK))
+        for a in range(PASSES):
+            nc.sync.dma_start(w1_raw[a][:], w1_rows[a])
+        nc.sync.dma_start(tab[1][:].bitcast(I32), tab_src(1))
+
+        wgs_rows = wgs.rearrange("(q t) j -> q t j", t=PACK)
+        wgs_first = keep.tile([P, S], F32, name="wgs_first")
+        wgs_rest = keep.tile([P, PACK - 1, S], F32, name="wgs_rest")
+        for q in (0, 2, 1, 3):
+            nc.sync.dma_start(wgs_first[32 * q : 32 * q + 32, :], wgs_rows[:, 0, :])
+        page = [keep.tile([P, T2], F32, name=f"page{t}") for t in range(PACK)]
+        page_src = page0.rearrange("(p t) m -> t p m", t=PACK)
+        page_dst = out_1.rearrange("(p t) m -> t p m", t=PACK)
+        nc.sync.dma_start(page[0][:], page_src[0])
+        nc.sync.dma_start(put[:], offs2)
+        for q in (0, 2, 1, 3):
+            nc.sync.dma_start(wgs_rest[32 * q : 32 * q + 32, :, :], wgs_rows[:, 1:PACK, :])
+        for t in range(1, PACK - 1):
+            nc.sync.dma_start(page[t][:], page_src[t])
+        wc = keep.tile([P, 2 * N], U8, name="wc", align_bytes=64)
+        nc.sync.dma_start(wc[:].bitcast(I32), wc_words[0].bitcast(I32))
+        for q in range(QUADS):
+            nc.sync.dma_start(
+                wc_sc[32 * q : 32 * q + 4, :].bitcast(I32),
+                wc_scales[0, 4 * q : 4 * q + 4, :].bitcast(I32),
+            )
+        wd_raw = keep.tile([P, PACK, N], F32, name="wd_raw")
+        nc.sync.dma_start(page[PACK - 1][:], page_src[PACK - 1])
+        nc.sync.dma_start(wd_raw[:], wd.rearrange("(p j) n -> p j n", j=PACK))
+
+        v = [keep.tile([P, S], U32, name=f"v{a}", align_bytes=64) for a in range(PASSES)]
+        v_sc = keep.tile([P, S], U8, name="v_sc", align_bytes=64)
+        nc.vector.tensor_copy(v[0][:], tab[0][:].indirect(pick[:]))
+        nc.vector.tensor_copy(v_sc[:], tab_sc[:].indirect(pick[:]))
+
+        w1_q = [keep.tile([P, H], U32, name=f"w1_q{a}", align_bytes=64) for a in range(PASSES)]
+        w1_sc = [keep.tile([P, H], U8, name=f"w1_sc{a}", align_bytes=64) for a in range(PASSES)]
+        for a, engine_copy in enumerate((nc.scalar.copy, nc.vector.tensor_copy)):
+            w1_bf = keep.tile([P, PACK, P, PACK], BF16, name=f"w1_bf{a}", align_bytes=64)
+            engine_copy(
+                w1_bf[:].rearrange("p t m j -> p m j t"),
+                w1_raw[a][:].rearrange("p j (m t) -> p m j t", t=PACK),
+            )
+            nc.vector.quantize_mx(
+                out=w1_q[a][:].bitcast(FP8X4),
+                scales=w1_sc[a][:],
+                in_=w1_bf[:].rearrange("p t m j -> p (t m j)"),
+            )
+        for half in range(HALVES):
+            nc.vector.tensor_copy(
+                v[1][:, half * BANK : (half + 1) * BANK],
+                tab[1][:].indirect(pick[:, half * (BANK // 16) : (half + 1) * (BANK // 16)]),
+            )
+
+        pairs = [keep.tile([P, 2, 2 * BANK, 2], BF16, name=f"pairs{g}", align_bytes=64) for g in range(HALVES)]
+
+        def pair_words(g):
+            return pairs[g][:].rearrange("p u m e -> p u (m e)").bitcast(F32)
+
+        def round_page(t, m0, m1, engine_copy):
+            g, base = divmod(m0, 2 * BANK)
+            engine_copy(pairs[g][:, t // 2, base : base + m1 - m0, t % 2], page[t][:, m0:m1])
+
+        wd_bf = keep.tile([P, N, PACK], BF16, name="wd_bf", align_bytes=64)
+        wd_q = keep.tile([P, N], U32, name="wd_q", align_bytes=64)
+        wd_sc = keep.tile([P, N], U8, name="wd_sc", align_bytes=64)
+        clock = keep.tile([P, 2, 8], F32, name="clock")
+
+        factors = [keep.tile([P, S], F32, name=f"factor{t}") for t in range(PACK)]
+        for t in range(PACK):
+            h = wgs_first[:] if t == 0 else wgs_rest[:, t - 1, :]
+            factor = factors[t]
+            for half in range(HALVES):
+                cols = slice(half * BANK, (half + 1) * BANK)
+                nc.scalar.activation(factor[:, cols], h[:, cols], ACT.Copy, scale=gains[:, t : t + 1])
+                acc = psum.tile([P, BANK], F32, name="acc", bufs=2)
+                for a in range(PASSES):
+                    nc.tensor.matmul_mx(
+                        out=acc[:],
+                        lhsT=w1_q[a][:, t * P : (t + 1) * P].bitcast(FP8X4),
+                        lhsT_scale=w1_sc[a][:, t * P : (t + 1) * P],
+                        rhs=v[a][:, cols].bitcast(FP8X4),
+                        rhs_scale=v_sc[4 * a : P, cols],
+                        start=(a == 0),
+                        stop=(a == PASSES - 1),
+                    )
+                sq = h[:, cols]
+                root = factors[t + 1][:, cols] if t + 1 < PACK else pair_words(half)[:, 0, 0:BANK]
+                nc.scalar.activation(sq, acc[:], ACT.Square)
+                nc.scalar.activation(root, sq, ACT.Abs_reciprocal_sqrt, bias=1.0)
+                nc.scalar.activation(h[:, cols], root, ACT.Square)
+                if t == 0 and half == 0:
+                    nc.gpsimd.tensor_copy(clock[:, 1, 0:1], h[:, 0:1])
+                if t == 0:
+                    nc.vector.tensor_tensor(
+                        page[t][:].indirect(put[:, half * (BANK // 16) : (half + 1) * (BANK // 16)]),
+                        h[:, cols], factor[:, cols], ALU.mult,
+                    )
+            if t > 0:
+                nc.vector.tensor_tensor(page[t][:].indirect(put[:]), h, factor[:], ALU.mult)
+            nc.sync.dma_start(page_dst[t], page[t][:])
+        nc.scalar.activation(warm[:, 0:1], wgs_rest[:, PACK - 2, S - 1 : S], ACT.Sin, scale=0.0)
+
+        nc.scalar.copy(
+            wd_bf[:].rearrange("p (c i) j -> p c j i", i=4),
+            wd_raw[:].rearrange("p j (c i) -> p c j i", i=4),
+        )
+        for t in range(2):
+            for g in range(HALVES):
+                round_page(t, 2 * g * BANK, (2 * g + 2) * BANK, nc.scalar.copy)
+
+        words = keep.tile([P, T2], U32, name="words", align_bytes=64)
+        scales = keep.tile([P, T2], U8, name="scales", align_bytes=64)
+        words_dst = out_2[0].rearrange("p m t -> p (m t)").bitcast(I32)
+
+        def quantise_page(m0, m1):
+            cols = slice(m0, m1)
+            g, base = divmod(m0, 2 * BANK)
+            for t in (2, 3):
+                round_page(t, m0, m1, nc.vector.tensor_copy)
+            grouped = work.tile([P, m1 - m0, 2], F32, name="grouped", align_bytes=64)
+            nc.vector.tensor_copy(
+                grouped[:], pair_words(g)[:, :, base : base + m1 - m0].rearrange("p u m -> p m u")
+            )
+            nc.vector.quantize_mx(
+                out=words[:, cols].bitcast(FP8X4),
+                scales=scales[:, cols],
+                in_=grouped[:].rearrange("p m u -> p (m u)").bitcast(BF16),
+            )
+            nc.sync.dma_start(words_dst[:, cols], words[:, cols].bitcast(I32))
+
+        def products(m0, m1):
+            cols = slice(m0, m1)
+            width = m1 - m0
+            for n in range(NT):
+                phase = psum.tile([P, width], F32, name="phase", tag="acc", bufs=2)
+                nc.tensor.matmul_mx(
+                    out=phase[:],
+                    lhsT=wc[:, 2 * n * P : 2 * (n + 1) * P].bitcast(FP4X4),
+                    lhsT_scale=wc_sc[:, n * P : (n + 1) * P],
+                    rhs=words[:, cols].bitcast(FP8X4),
+                    rhs_scale=scales[:, cols],
+                    start=True,
+                    stop=True,
+                )
+                value = psum.tile([P, width], F32, name="value", bufs=6)
+                nc.tensor.matmul_mx(
+                    out=value[:],
+                    lhsT=wd_q[:, n * P : (n + 1) * P].bitcast(FP8X4),
+                    lhsT_scale=wd_sc[:, n * P : (n + 1) * P],
+                    rhs=words[:, cols].bitcast(FP8X4),
+                    rhs_scale=scales[:, cols],
+                    start=True,
+                    stop=True,
+                )
+                half_cos = work.tile([P, width], F32, name="half_cos")
+                nc.scalar.activation(half_cos[:], phase[:], ACT.Sin, scale=0.5, bias=math.pi / 2)
+                if n == 0 and m0 == 0:
+                    nc.gpsimd.tensor_copy(clock[:, 0, 0:1], half_cos[:, 0:1])
+                cos_tile = work.tile([P, width], F32, name="cos_tile", bufs=6)
+                cos_up = cos_tile[:]
+                if m1 == T2 and n > 0:
+                    nc.vector.scalar_tensor_tensor(cos_up, half_cos[:], 2.0, half_cos[:], ALU.mult, ALU.mult)
+                else:
+                    nc.scalar.activation(cos_up, half_cos[:], ACT.Square, scale=math.sqrt(2.0))
+                y = work.tile([P, width], F32, name="y", bufs=12)
+                nc.vector.scalar_tensor_tensor(y[:], cos_up, -1.0, value[:], ALU.add, ALU.mult)
+                nc.sync.dma_start(out_0[n * P : (n + 1) * P, cols], y[:])
+
+        edges = [BANK * c for c in range(CHUNKS + 1)]
+        spans = list(zip(edges[:-1], edges[1:]))
+        quantise_page(*spans[0])
+        for n0, n1 in ((0, P), (P, N)):
+            nc.vector.quantize_mx(
+                out=wd_q[:, n0:n1].bitcast(FP8X4),
+                scales=wd_sc[:, n0:n1],
+                in_=wd_bf[:].rearrange("p n j -> p (n j)")[:, n0 * PACK : n1 * PACK],
+            )
+        for i, span in enumerate(spans):
+            if i + 1 < len(spans):
+                quantise_page(*spans[i + 1])
+            else:
+                for q in range(QUADS):
+                    nc.sync.dma_start(
+                        out_3[0, 4 * q : 4 * q + 4, :].bitcast(I32),
+                        scales[32 * q : 32 * q + 4, :].bitcast(I32),
+                    )
+            products(*span)

@@ -72,19 +72,22 @@ def tile_list_rod_checkpoint_kernel(
         nc.sync.dma_start(tab[1][:].bitcast(I32), tab_src(1))
 
         wgs_rows = wgs.rearrange("(q t) j -> q t j", t=PACK)
-        wgs_first = keep.tile([P, S], F32, name="wgs_first")
-        wgs_rest = keep.tile([P, PACK - 1, S], F32, name="wgs_rest")
-        for q in (0, 2, 1, 3):
-            nc.sync.dma_start(wgs_first[32 * q : 32 * q + 32, :], wgs_rows[:, 0, :])
+        resp = [keep.tile([P, S], F32, name=f"resp{t}") for t in range(PACK)]
+
+        def load_wgs(t):
+            for q in (0, 2, 1, 3):
+                nc.sync.dma_start(resp[t][32 * q : 32 * q + 32, :], wgs_rows[:, t, :])
+
+        load_wgs(0)
         page = [keep.tile([P, T2], F32, name=f"page{t}") for t in range(PACK)]
         page_src = page0.rearrange("(p t) m -> t p m", t=PACK)
         page_dst = out_1.rearrange("(p t) m -> t p m", t=PACK)
         nc.sync.dma_start(page[0][:], page_src[0])
         nc.sync.dma_start(put[:], offs2)
-        for q in (0, 2, 1, 3):
-            nc.sync.dma_start(wgs_rest[32 * q : 32 * q + 32, :, :], wgs_rows[:, 1:PACK, :])
         for t in range(1, PACK - 1):
+            load_wgs(t)
             nc.sync.dma_start(page[t][:], page_src[t])
+        load_wgs(PACK - 1)
         wc = keep.tile([P, 2 * N], U8, name="wc", align_bytes=64)
         nc.sync.dma_start(wc[:].bitcast(I32), wc_words[0].bitcast(I32))
         for q in range(QUADS):
@@ -101,19 +104,19 @@ def tile_list_rod_checkpoint_kernel(
         nc.vector.tensor_copy(v[0][:], tab[0][:].indirect(pick[:]))
         nc.vector.tensor_copy(v_sc[:], tab_sc[:].indirect(pick[:]))
 
-        w1_q = [keep.tile([P, H], U32, name=f"w1_q{a}", align_bytes=64) for a in range(PASSES)]
-        w1_sc = [keep.tile([P, H], U8, name=f"w1_sc{a}", align_bytes=64) for a in range(PASSES)]
+        w1_q = keep.tile([P, PASSES * H], U32, name="w1_q", align_bytes=64)
+        w1_sc = keep.tile([P, PASSES * H], U8, name="w1_sc", align_bytes=64)
+        w1_bf = keep.tile([P, PASSES, PACK, P, PACK], BF16, name="w1_bf", align_bytes=64)
         for a, engine_copy in enumerate((nc.scalar.copy, nc.vector.tensor_copy)):
-            w1_bf = keep.tile([P, PACK, P, PACK], BF16, name=f"w1_bf{a}", align_bytes=64)
             engine_copy(
-                w1_bf[:].rearrange("p t m j -> p m j t"),
+                w1_bf[:, a, :, :, :].rearrange("p t m j -> p m j t"),
                 w1_raw[a][:].rearrange("p j (m t) -> p m j t", t=PACK),
             )
-            nc.vector.quantize_mx(
-                out=w1_q[a][:].bitcast(FP8X4),
-                scales=w1_sc[a][:],
-                in_=w1_bf[:].rearrange("p t m j -> p (t m j)"),
-            )
+        nc.vector.quantize_mx(
+            out=w1_q[:].bitcast(FP8X4),
+            scales=w1_sc[:],
+            in_=w1_bf[:].rearrange("p a t m j -> p (a t m j)"),
+        )
         for half in range(HALVES):
             nc.vector.tensor_copy(
                 v[1][:, half * BANK : (half + 1) * BANK],
@@ -132,11 +135,10 @@ def tile_list_rod_checkpoint_kernel(
         wd_bf = keep.tile([P, N, PACK], BF16, name="wd_bf", align_bytes=64)
         wd_q = keep.tile([P, N], U32, name="wd_q", align_bytes=64)
         wd_sc = keep.tile([P, N], U8, name="wd_sc", align_bytes=64)
-        clock = keep.tile([P, 2, 8], F32, name="clock")
 
         factors = [keep.tile([P, S], F32, name=f"factor{t}") for t in range(PACK)]
         for t in range(PACK):
-            h = wgs_first[:] if t == 0 else wgs_rest[:, t - 1, :]
+            h = resp[t][:]
             factor = factors[t]
             for half in range(HALVES):
                 cols = slice(half * BANK, (half + 1) * BANK)
@@ -145,29 +147,27 @@ def tile_list_rod_checkpoint_kernel(
                 for a in range(PASSES):
                     nc.tensor.matmul_mx(
                         out=acc[:],
-                        lhsT=w1_q[a][:, t * P : (t + 1) * P].bitcast(FP8X4),
-                        lhsT_scale=w1_sc[a][:, t * P : (t + 1) * P],
+                        lhsT=w1_q[:, a * H + t * P : a * H + (t + 1) * P].bitcast(FP8X4),
+                        lhsT_scale=w1_sc[:, a * H + t * P : a * H + (t + 1) * P],
                         rhs=v[a][:, cols].bitcast(FP8X4),
                         rhs_scale=v_sc[4 * a : P, cols],
                         start=(a == 0),
                         stop=(a == PASSES - 1),
                     )
-                sq = h[:, cols]
+                sq = factors[1][:, 0:BANK] if (t, half) == (0, 1) else h[:, cols]
                 root = factors[t + 1][:, cols] if t + 1 < PACK else pair_words(half)[:, 0, 0:BANK]
                 nc.scalar.activation(sq, acc[:], ACT.Square)
                 nc.scalar.activation(root, sq, ACT.Abs_reciprocal_sqrt, bias=1.0)
                 nc.scalar.activation(h[:, cols], root, ACT.Square)
-                if t == 0 and half == 0:
-                    nc.gpsimd.tensor_copy(clock[:, 1, 0:1], h[:, 0:1])
-                if t == 0:
+                if t < 2:
                     nc.vector.tensor_tensor(
                         page[t][:].indirect(put[:, half * (BANK // 16) : (half + 1) * (BANK // 16)]),
                         h[:, cols], factor[:, cols], ALU.mult,
                     )
-            if t > 0:
+            if t >= 2:
                 nc.vector.tensor_tensor(page[t][:].indirect(put[:]), h, factor[:], ALU.mult)
             nc.sync.dma_start(page_dst[t], page[t][:])
-        nc.scalar.activation(warm[:, 0:1], wgs_rest[:, PACK - 2, S - 1 : S], ACT.Sin, scale=0.0)
+        nc.scalar.activation(warm[:, 0:1], resp[PACK - 1][:, S - 1 : S], ACT.Sin, scale=0.0)
 
         nc.scalar.copy(
             wd_bf[:].rearrange("p (c i) j -> p c j i", i=4),
@@ -197,21 +197,25 @@ def tile_list_rod_checkpoint_kernel(
             )
             nc.sync.dma_start(words_dst[:, cols], words[:, cols].bitcast(I32))
 
-        def products(m0, m1):
-            cols = slice(m0, m1)
-            width = m1 - m0
+        def products(c, pieces):
+            cols = slice(c * BANK, (c + 1) * BANK)
             for n in range(NT):
-                phase = psum.tile([P, width], F32, name="phase", tag="acc", bufs=2)
-                nc.tensor.matmul_mx(
-                    out=phase[:],
-                    lhsT=wc[:, 2 * n * P : 2 * (n + 1) * P].bitcast(FP4X4),
-                    lhsT_scale=wc_sc[:, n * P : (n + 1) * P],
-                    rhs=words[:, cols].bitcast(FP8X4),
-                    rhs_scale=scales[:, cols],
-                    start=True,
-                    stop=True,
-                )
-                value = psum.tile([P, width], F32, name="value", bufs=6)
+                half_cos = work.tile([P, BANK], F32, name="half_cos")
+                for m0, m1 in pieces:
+                    phase = psum.tile([P, m1 - m0], F32, name="phase", tag="acc", bufs=2)
+                    nc.tensor.matmul_mx(
+                        out=phase[:],
+                        lhsT=wc[:, 2 * n * P : 2 * (n + 1) * P].bitcast(FP4X4),
+                        lhsT_scale=wc_sc[:, n * P : (n + 1) * P],
+                        rhs=words[:, m0:m1].bitcast(FP8X4),
+                        rhs_scale=scales[:, m0:m1],
+                        start=True,
+                        stop=True,
+                    )
+                    nc.scalar.activation(
+                        half_cos[:, m0 - c * BANK : m1 - c * BANK], phase[:], ACT.Sin, scale=0.5, bias=math.pi / 2
+                    )
+                value = psum.tile([P, BANK], F32, name="value", bufs=6)
                 nc.tensor.matmul_mx(
                     out=value[:],
                     lhsT=wd_q[:, n * P : (n + 1) * P].bitcast(FP8X4),
@@ -221,36 +225,32 @@ def tile_list_rod_checkpoint_kernel(
                     start=True,
                     stop=True,
                 )
-                half_cos = work.tile([P, width], F32, name="half_cos")
-                nc.scalar.activation(half_cos[:], phase[:], ACT.Sin, scale=0.5, bias=math.pi / 2)
-                if n == 0 and m0 == 0:
-                    nc.gpsimd.tensor_copy(clock[:, 0, 0:1], half_cos[:, 0:1])
-                cos_tile = work.tile([P, width], F32, name="cos_tile", bufs=6)
-                cos_up = cos_tile[:]
-                if m1 == T2 and n > 0:
-                    nc.vector.scalar_tensor_tensor(cos_up, half_cos[:], 2.0, half_cos[:], ALU.mult, ALU.mult)
+                cos_up = work.tile([P, BANK], F32, name="cos_up", bufs=6)
+                if c == CHUNKS - 1 and n == NT - 1:
+                    nc.vector.scalar_tensor_tensor(cos_up[:], half_cos[:], 2.0, half_cos[:], ALU.mult, ALU.mult)
                 else:
-                    nc.scalar.activation(cos_up, half_cos[:], ACT.Square, scale=math.sqrt(2.0))
-                y = work.tile([P, width], F32, name="y", bufs=12)
-                nc.vector.scalar_tensor_tensor(y[:], cos_up, -1.0, value[:], ALU.add, ALU.mult)
+                    nc.scalar.activation(cos_up[:], half_cos[:], ACT.Square, scale=math.sqrt(2.0))
+                y = work.tile([P, BANK], F32, name="y", bufs=12)
+                nc.vector.scalar_tensor_tensor(y[:], cos_up[:], -1.0, value[:], ALU.add, ALU.mult)
                 nc.sync.dma_start(out_0[n * P : (n + 1) * P, cols], y[:])
 
-        edges = [BANK * c for c in range(CHUNKS + 1)]
-        spans = list(zip(edges[:-1], edges[1:]))
-        quantise_page(*spans[0])
+        pieces = [[(c * BANK, (c + 1) * BANK)] for c in range(CHUNKS)]
+        pieces[0] = [(0, BANK // 2), (BANK // 2, BANK)]
+        for piece in pieces[0]:
+            quantise_page(*piece)
         for n0, n1 in ((0, P), (P, N)):
             nc.vector.quantize_mx(
                 out=wd_q[:, n0:n1].bitcast(FP8X4),
                 scales=wd_sc[:, n0:n1],
                 in_=wd_bf[:].rearrange("p n j -> p (n j)")[:, n0 * PACK : n1 * PACK],
             )
-        for i, span in enumerate(spans):
-            if i + 1 < len(spans):
-                quantise_page(*spans[i + 1])
+        for c in range(CHUNKS):
+            if c + 1 < CHUNKS:
+                quantise_page(*pieces[c + 1][0])
             else:
                 for q in range(QUADS):
                     nc.sync.dma_start(
                         out_3[0, 4 * q : 4 * q + 4, :].bitcast(I32),
                         scales[32 * q : 32 * q + 4, :].bitcast(I32),
                     )
-            products(*span)
+            products(c, pieces[c])

@@ -52,7 +52,8 @@ def tile_list_rod_checkpoint_kernel(
         nc.vector.memset(wc_sc[:].bitcast(I32), 0)
 
         tab = [keep.tile([P, T], U32, name=f"tab{a}", align_bytes=64) for a in range(PASSES)]
-        w1_raw = [keep.tile([P, PACK, H], F32, name=f"w1_raw{a}") for a in range(PASSES)]
+        w1_first = keep.tile([P, PACK, H], F32, name="w1_first")
+        w1_last = [keep.tile([P, PACK, H // 2], F32, name=f"w1_last{u}") for u in range(2)]
         w1_rows = w1.rearrange("(a p j) c -> a p j c", p=P, j=PACK)
 
         def tab_src(a):
@@ -67,27 +68,29 @@ def tile_list_rod_checkpoint_kernel(
             )
         gains = keep.tile([P, 8], F32, name="gains")
         nc.sync.dma_start(gains[:, 0:PACK], gain.rearrange("(p t) -> p t", t=PACK))
-        for a in range(PASSES):
-            nc.sync.dma_start(w1_raw[a][:], w1_rows[a])
+        nc.sync.dma_start(w1_first[:], w1_rows[0])
         nc.sync.dma_start(tab[1][:].bitcast(I32), tab_src(1))
+        for u in range(2):
+            nc.sync.dma_start(w1_last[u][:], w1_rows[1][:, :, u * (H // 2) : (u + 1) * (H // 2)])
 
         wgs_rows = wgs.rearrange("(q t) j -> q t j", t=PACK)
         resp = [keep.tile([P, S], F32, name=f"resp{t}") for t in range(PACK)]
 
-        def load_wgs(t):
+        def load_wgs(t, j0, j1):
             for q in (0, 2, 1, 3):
-                nc.sync.dma_start(resp[t][32 * q : 32 * q + 32, :], wgs_rows[:, t, :])
+                nc.sync.dma_start(resp[t][32 * q : 32 * q + 32, j0:j1], wgs_rows[:, t, j0:j1])
 
-        load_wgs(0)
+        load_wgs(0, 0, BANK)
         page = [keep.tile([P, T2], F32, name=f"page{t}") for t in range(PACK)]
         page_src = page0.rearrange("(p t) m -> t p m", t=PACK)
         page_dst = out_1.rearrange("(p t) m -> t p m", t=PACK)
         nc.sync.dma_start(page[0][:], page_src[0])
         nc.sync.dma_start(put[:], offs2)
+        load_wgs(0, BANK, S)
         for t in range(1, PACK - 1):
-            load_wgs(t)
+            load_wgs(t, 0, S)
             nc.sync.dma_start(page[t][:], page_src[t])
-        load_wgs(PACK - 1)
+        load_wgs(PACK - 1, 0, S)
         wc = keep.tile([P, 2 * N], U8, name="wc", align_bytes=64)
         nc.sync.dma_start(wc[:].bitcast(I32), wc_words[0].bitcast(I32))
         for q in range(QUADS):
@@ -96,47 +99,51 @@ def tile_list_rod_checkpoint_kernel(
                 wc_scales[0, 4 * q : 4 * q + 4, :].bitcast(I32),
             )
         wd_raw = keep.tile([P, PACK, N], F32, name="wd_raw")
-        nc.sync.dma_start(page[PACK - 1][:], page_src[PACK - 1])
         nc.sync.dma_start(wd_raw[:], wd.rearrange("(p j) n -> p j n", j=PACK))
+        nc.sync.dma_start(page[PACK - 1][:], page_src[PACK - 1])
 
         v = [keep.tile([P, S], U32, name=f"v{a}", align_bytes=64) for a in range(PASSES)]
         v_sc = keep.tile([P, S], U8, name="v_sc", align_bytes=64)
         nc.vector.tensor_copy(v[0][:], tab[0][:].indirect(pick[:]))
         nc.vector.tensor_copy(v_sc[:], tab_sc[:].indirect(pick[:]))
 
-        w1_q = keep.tile([P, PASSES * H], U32, name="w1_q", align_bytes=64)
-        w1_sc = keep.tile([P, PASSES * H], U8, name="w1_sc", align_bytes=64)
-        w1_bf = keep.tile([P, PASSES, PACK, P, PACK], BF16, name="w1_bf", align_bytes=64)
-        for a, engine_copy in enumerate((nc.scalar.copy, nc.vector.tensor_copy)):
-            engine_copy(
-                w1_bf[:, a, :, :, :].rearrange("p t m j -> p m j t"),
-                w1_raw[a][:].rearrange("p j (m t) -> p m j t", t=PACK),
-            )
-        nc.vector.quantize_mx(
-            out=w1_q[:].bitcast(FP8X4),
-            scales=w1_sc[:],
-            in_=w1_bf[:].rearrange("p a t m j -> p (a t m j)"),
-        )
         for half in range(HALVES):
             nc.vector.tensor_copy(
                 v[1][:, half * BANK : (half + 1) * BANK],
                 tab[1][:].indirect(pick[:, half * (BANK // 16) : (half + 1) * (BANK // 16)]),
             )
 
-        pairs = [keep.tile([P, 2, 2 * BANK, 2], BF16, name=f"pairs{g}", align_bytes=64) for g in range(HALVES)]
+        w1_q = keep.tile([P, PASSES * H], U32, name="w1_q", align_bytes=64)
+        w1_sc = keep.tile([P, PASSES * H], U8, name="w1_sc", align_bytes=64)
+        w1_bf = keep.tile([P, PACK, PASSES, P, PACK], BF16, name="w1_bf", align_bytes=64)
 
-        def pair_words(g):
-            return pairs[g][:].rearrange("p u m e -> p u (m e)").bitcast(F32)
+        def round_w1(engine_copy, raw, a, m0, m1):
+            engine_copy(
+                w1_bf[:, :, a, m0:m1, :].rearrange("p t m j -> p m j t"),
+                raw.rearrange("p j (m t) -> p m j t", t=PACK),
+            )
 
-        def round_page(t, m0, m1, engine_copy):
+        round_w1(nc.scalar.copy, w1_first[:], 0, 0, P)
+        round_w1(nc.scalar.copy, w1_last[0][:], 1, 0, P // 2)
+        round_w1(nc.vector.tensor_copy, w1_last[1][:], 1, P // 2, P)
+        w1_flat = w1_bf[:].rearrange("p t a m j -> p (t a m j)")
+        for t0, t1 in ((0, 1), (1, 2), (2, 4)):
+            c0, c1 = t0 * PASSES * P, t1 * PASSES * P
+            nc.vector.quantize_mx(
+                out=w1_q[:, c0:c1].bitcast(FP8X4),
+                scales=w1_sc[:, c0:c1],
+                in_=w1_flat[:, c0 * PACK : c1 * PACK],
+            )
+
+        rounded = [keep.tile([P, PACK, 2 * BANK], BF16, name=f"rounded{g}", align_bytes=64) for g in range(HALVES)]
+
+        def round_page(t, m0, m1):
             g, base = divmod(m0, 2 * BANK)
-            engine_copy(pairs[g][:, t // 2, base : base + m1 - m0, t % 2], page[t][:, m0:m1])
+            nc.scalar.copy(rounded[g][:, t, base : base + m1 - m0], page[t][:, m0:m1])
 
         wd_bf = keep.tile([P, N, PACK], BF16, name="wd_bf", align_bytes=64)
-        wd_q = keep.tile([P, N], U32, name="wd_q", align_bytes=64)
-        wd_sc = keep.tile([P, N], U8, name="wd_sc", align_bytes=64)
 
-        factors = [keep.tile([P, S], F32, name=f"factor{t}") for t in range(PACK)]
+        factors = [keep.tile([P, S], F32, name=f"factor{t}", align_bytes=64) for t in range(PACK)]
         for t in range(PACK):
             h = resp[t][:]
             factor = factors[t]
@@ -147,18 +154,23 @@ def tile_list_rod_checkpoint_kernel(
                 for a in range(PASSES):
                     nc.tensor.matmul_mx(
                         out=acc[:],
-                        lhsT=w1_q[:, a * H + t * P : a * H + (t + 1) * P].bitcast(FP8X4),
-                        lhsT_scale=w1_sc[:, a * H + t * P : a * H + (t + 1) * P],
+                        lhsT=w1_q[:, (t * PASSES + a) * P : (t * PASSES + a + 1) * P].bitcast(FP8X4),
+                        lhsT_scale=w1_sc[:, (t * PASSES + a) * P : (t * PASSES + a + 1) * P],
                         rhs=v[a][:, cols].bitcast(FP8X4),
                         rhs_scale=v_sc[4 * a : P, cols],
                         start=(a == 0),
                         stop=(a == PASSES - 1),
                     )
                 sq = factors[1][:, 0:BANK] if (t, half) == (0, 1) else h[:, cols]
-                root = factors[t + 1][:, cols] if t + 1 < PACK else pair_words(half)[:, 0, 0:BANK]
+                if t + 1 < PACK:
+                    root = factors[t + 1][:, cols].rearrange("p (u m) -> p u m", u=PACK)
+                else:
+                    root = rounded[half][:].bitcast(F32)[:, :, 0 : BANK // PACK]
                 nc.scalar.activation(sq, acc[:], ACT.Square)
-                nc.scalar.activation(root, sq, ACT.Abs_reciprocal_sqrt, bias=1.0)
-                nc.scalar.activation(h[:, cols], root, ACT.Square)
+                nc.scalar.activation(
+                    root, sq.rearrange("p (u m) -> p u m", u=PACK), ACT.Abs_reciprocal_sqrt, bias=1.0
+                )
+                nc.scalar.activation(h[:, cols].rearrange("p (u m) -> p u m", u=PACK), root, ACT.Square)
                 if t < 2:
                     nc.vector.tensor_tensor(
                         page[t][:].indirect(put[:, half * (BANK // 16) : (half + 1) * (BANK // 16)]),
@@ -173,9 +185,9 @@ def tile_list_rod_checkpoint_kernel(
             wd_bf[:].rearrange("p (c i) j -> p c j i", i=4),
             wd_raw[:].rearrange("p j (c i) -> p c j i", i=4),
         )
-        for t in range(2):
+        for t in range(PACK - 1):
             for g in range(HALVES):
-                round_page(t, 2 * g * BANK, (2 * g + 2) * BANK, nc.scalar.copy)
+                round_page(t, 2 * g * BANK, (2 * g + 2) * BANK)
 
         words = keep.tile([P, T2], U32, name="words", align_bytes=64)
         scales = keep.tile([P, T2], U8, name="scales", align_bytes=64)
@@ -184,16 +196,16 @@ def tile_list_rod_checkpoint_kernel(
         def quantise_page(m0, m1):
             cols = slice(m0, m1)
             g, base = divmod(m0, 2 * BANK)
-            for t in (2, 3):
-                round_page(t, m0, m1, nc.vector.tensor_copy)
-            grouped = work.tile([P, m1 - m0, 2], F32, name="grouped", align_bytes=64)
+            round_page(PACK - 1, m0, m1)
+            grouped = work.tile([P, m1 - m0, PACK], BF16, name="grouped", align_bytes=64)
             nc.vector.tensor_copy(
-                grouped[:], pair_words(g)[:, :, base : base + m1 - m0].rearrange("p u m -> p m u")
+                grouped[:].rearrange("p (c i) t -> p c t i", i=4),
+                rounded[g][:, :, base : base + m1 - m0].rearrange("p t (c i) -> p c t i", i=4),
             )
             nc.vector.quantize_mx(
                 out=words[:, cols].bitcast(FP8X4),
                 scales=scales[:, cols],
-                in_=grouped[:].rearrange("p m u -> p (m u)").bitcast(BF16),
+                in_=grouped[:].rearrange("p m t -> p (m t)"),
             )
             nc.sync.dma_start(words_dst[:, cols], words[:, cols].bitcast(I32))
 
@@ -226,10 +238,7 @@ def tile_list_rod_checkpoint_kernel(
                     stop=True,
                 )
                 cos_up = work.tile([P, BANK], F32, name="cos_up", bufs=6)
-                if c == CHUNKS - 1 and n == NT - 1:
-                    nc.vector.scalar_tensor_tensor(cos_up[:], half_cos[:], 2.0, half_cos[:], ALU.mult, ALU.mult)
-                else:
-                    nc.scalar.activation(cos_up[:], half_cos[:], ACT.Square, scale=math.sqrt(2.0))
+                nc.scalar.activation(cos_up[:], half_cos[:], ACT.Square, scale=math.sqrt(2.0))
                 y = work.tile([P, BANK], F32, name="y", bufs=12)
                 nc.vector.scalar_tensor_tensor(y[:], cos_up[:], -1.0, value[:], ALU.add, ALU.mult)
                 nc.sync.dma_start(out_0[n * P : (n + 1) * P, cols], y[:])
@@ -238,6 +247,8 @@ def tile_list_rod_checkpoint_kernel(
         pieces[0] = [(0, BANK // 2), (BANK // 2, BANK)]
         for piece in pieces[0]:
             quantise_page(*piece)
+        wd_q = keep.tile([P, N], U32, name="wd_q", tag="factor3", align_bytes=64)
+        wd_sc = keep.tile([P, N], U8, name="wd_sc", align_bytes=64)
         for n0, n1 in ((0, P), (P, N)):
             nc.vector.quantize_mx(
                 out=wd_q[:, n0:n1].bitcast(FP8X4),

@@ -41,19 +41,19 @@ def tile_list_rod_checkpoint_kernel(
         pick = lists.tile([P, S // 16], U16, name="pick")
         put = lists.tile([P, S // 16], U16, name="put")
 
+        tab_sc = keep.tile([P, T], U8, name="tab_sc", align_bytes=64)
+        nc.vector.memset(tab_sc[:].bitcast(I32), 0)
+
         one = keep.tile([P, 8], F32, name="one")
         warm = keep.tile([P, 8], F32, name="warm")
         nc.vector.memset(one[:], 1.0)
         nc.scalar.activation(warm[:], one[:], ACT.Abs_reciprocal_sqrt)
 
-        tab_sc = keep.tile([P, T], U8, name="tab_sc", align_bytes=64)
-        nc.vector.memset(tab_sc[:].bitcast(I32), 0)
         wc_sc = keep.tile([P, N], U8, name="wc_sc", align_bytes=64)
         nc.vector.memset(wc_sc[:].bitcast(I32), 0)
 
         tab = [keep.tile([P, T], U32, name=f"tab{a}", align_bytes=64) for a in range(PASSES)]
-        w1_first = keep.tile([P, PACK, H], F32, name="w1_first")
-        w1_last = [keep.tile([P, PACK, H // 2], F32, name=f"w1_last{u}") for u in range(2)]
+        w1_raw = [keep.tile([P, PACK, H], F32, name=f"w1_raw{a}") for a in range(PASSES)]
         w1_rows = w1.rearrange("(a p j) c -> a p j c", p=P, j=PACK)
 
         def tab_src(a):
@@ -66,31 +66,34 @@ def tile_list_rod_checkpoint_kernel(
                 tab_sc[32 * q : 32 * q + 4 * PASSES, :].bitcast(I32),
                 tab_scales[:, 4 * q : 4 * q + 4, :].bitcast(I32),
             )
-        gains = keep.tile([P, 8], F32, name="gains")
-        nc.sync.dma_start(gains[:, 0:PACK], gain.rearrange("(p t) -> p t", t=PACK))
-        nc.sync.dma_start(w1_first[:], w1_rows[0])
-        nc.sync.dma_start(tab[1][:].bitcast(I32), tab_src(1))
-        for u in range(2):
-            nc.sync.dma_start(w1_last[u][:], w1_rows[1][:, :, u * (H // 2) : (u + 1) * (H // 2)])
+        for a in range(PASSES):
+            nc.sync.dma_start(w1_raw[a][:], w1_rows[a])
 
         wgs_rows = wgs.rearrange("(q t) j -> q t j", t=PACK)
-        resp = [keep.tile([P, S], F32, name=f"resp{t}") for t in range(PACK)]
+        dealt = [keep.tile([P, S], F32, name=f"dealt{t}") for t in range(PACK)]
 
         def load_wgs(t, j0, j1):
             for q in (0, 2, 1, 3):
-                nc.sync.dma_start(resp[t][32 * q : 32 * q + 32, j0:j1], wgs_rows[:, t, j0:j1])
+                nc.sync.dma_start(dealt[t][32 * q : 32 * q + 32, j0:j1], wgs_rows[:, t, j0:j1])
 
+        nc.sync.dma_start(tab[1][:].bitcast(I32), tab_src(1))
+        FIRST = BANK // 2
+        gains = keep.tile([P, 8], F32, name="gains")
+        nc.sync.dma_start(gains[:, 0:PACK], gain.rearrange("(p t) -> p t", t=PACK))
         load_wgs(0, 0, BANK)
+        nc.sync.dma_start(put[:], offs2)
         page = [keep.tile([P, T2], F32, name=f"page{t}") for t in range(PACK)]
         page_src = page0.rearrange("(p t) m -> t p m", t=PACK)
         page_dst = out_1.rearrange("(p t) m -> t p m", t=PACK)
         nc.sync.dma_start(page[0][:], page_src[0])
-        nc.sync.dma_start(put[:], offs2)
         load_wgs(0, BANK, S)
         for t in range(1, PACK - 1):
             load_wgs(t, 0, S)
             nc.sync.dma_start(page[t][:], page_src[t])
+        wd_raw = keep.tile([P, PACK, N], F32, name="wd_raw")
+        nc.sync.dma_start(wd_raw[:], wd.rearrange("(p j) n -> p j n", j=PACK))
         load_wgs(PACK - 1, 0, S)
+        nc.sync.dma_start(page[PACK - 1][:], page_src[PACK - 1])
         wc = keep.tile([P, 2 * N], U8, name="wc", align_bytes=64)
         nc.sync.dma_start(wc[:].bitcast(I32), wc_words[0].bitcast(I32))
         for q in range(QUADS):
@@ -98,86 +101,105 @@ def tile_list_rod_checkpoint_kernel(
                 wc_sc[32 * q : 32 * q + 4, :].bitcast(I32),
                 wc_scales[0, 4 * q : 4 * q + 4, :].bitcast(I32),
             )
-        wd_raw = keep.tile([P, PACK, N], F32, name="wd_raw")
-        nc.sync.dma_start(wd_raw[:], wd.rearrange("(p j) n -> p j n", j=PACK))
-        nc.sync.dma_start(page[PACK - 1][:], page_src[PACK - 1])
+
+        def entries(lst, j0, j1):
+            return lst[:] if (j0, j1) == (0, S) else lst[:, j0 // 16 : j1 // 16]
 
         v = [keep.tile([P, S], U32, name=f"v{a}", align_bytes=64) for a in range(PASSES)]
         v_sc = keep.tile([P, S], U8, name="v_sc", align_bytes=64)
         nc.vector.tensor_copy(v[0][:], tab[0][:].indirect(pick[:]))
         nc.vector.tensor_copy(v_sc[:], tab_sc[:].indirect(pick[:]))
 
-        for half in range(HALVES):
-            nc.vector.tensor_copy(
-                v[1][:, half * BANK : (half + 1) * BANK],
-                tab[1][:].indirect(pick[:, half * (BANK // 16) : (half + 1) * (BANK // 16)]),
-            )
+        w1_q = {}
 
-        w1_q = keep.tile([P, PASSES * H], U32, name="w1_q", align_bytes=64)
-        w1_sc = keep.tile([P, PASSES * H], U8, name="w1_sc", align_bytes=64)
-        w1_bf = keep.tile([P, PACK, PASSES, P, PACK], BF16, name="w1_bf", align_bytes=64)
-
-        def round_w1(engine_copy, raw, a, m0, m1):
+        def round_w1(engine_copy, a, t0, t1):
+            bf = keep.tile([P, t1 - t0, P, PACK], BF16, name=f"w1_bf{a}_{t0}", align_bytes=64)
             engine_copy(
-                w1_bf[:, :, a, m0:m1, :].rearrange("p t m j -> p m j t"),
-                raw.rearrange("p j (m t) -> p m j t", t=PACK),
+                bf[:].rearrange("p t m j -> p m j t"),
+                w1_raw[a][:].rearrange("p j (m t) -> p m j t", t=PACK)[:, :, :, t0:t1],
             )
+            return bf
 
-        round_w1(nc.scalar.copy, w1_first[:], 0, 0, P)
-        round_w1(nc.scalar.copy, w1_last[0][:], 1, 0, P // 2)
-        round_w1(nc.vector.tensor_copy, w1_last[1][:], 1, P // 2, P)
-        w1_flat = w1_bf[:].rearrange("p t a m j -> p (t a m j)")
-        for t0, t1 in ((0, 1), (1, 2), (2, 4)):
-            c0, c1 = t0 * PASSES * P, t1 * PASSES * P
+        def quantise_w1(bf, a, t0, t1):
+            codes = keep.tile([P, (t1 - t0) * P], U32, name=f"w1_q{a}_{t0}", align_bytes=64)
+            bytes_ = keep.tile([P, (t1 - t0) * P], U8, name=f"w1_sc{a}_{t0}", align_bytes=64)
             nc.vector.quantize_mx(
-                out=w1_q[:, c0:c1].bitcast(FP8X4),
-                scales=w1_sc[:, c0:c1],
-                in_=w1_flat[:, c0 * PACK : c1 * PACK],
+                out=codes[:].bitcast(FP8X4), scales=bytes_[:], in_=bf[:].rearrange("p t m j -> p (t m j)")
             )
+            for t in range(t0, t1):
+                cols = slice((t - t0) * P, (t - t0 + 1) * P)
+                w1_q[a, t] = (codes[:, cols], bytes_[:, cols])
+
+        first = round_w1(nc.scalar.copy, 0, 0, PACK)
+        early = round_w1(nc.vector.tensor_copy, 1, 0, PACK // 2)
+        late = round_w1(nc.scalar.copy, 1, PACK // 2, PACK)
+        quantise_w1(first, 0, 0, PACK)
+        quantise_w1(early, 1, 0, PACK // 2)
+        for j0, j1 in ((0, FIRST), (FIRST, BANK), (BANK, S)):
+            nc.vector.tensor_copy(v[1][:, j0:j1], tab[1][:].indirect(entries(pick, j0, j1)))
+        quantise_w1(late, 1, PACK // 2, PACK)
 
         rounded = [keep.tile([P, PACK, 2 * BANK], BF16, name=f"rounded{g}", align_bytes=64) for g in range(HALVES)]
-
-        def round_page(t, m0, m1):
-            g, base = divmod(m0, 2 * BANK)
-            nc.scalar.copy(rounded[g][:, t, base : base + m1 - m0], page[t][:, m0:m1])
-
         wd_bf = keep.tile([P, N, PACK], BF16, name="wd_bf", align_bytes=64)
-
         factors = [keep.tile([P, S], F32, name=f"factor{t}", align_bytes=64) for t in range(PACK)]
-        for t in range(PACK):
-            h = resp[t][:]
-            factor = factors[t]
-            for half in range(HALVES):
-                cols = slice(half * BANK, (half + 1) * BANK)
-                nc.scalar.activation(factor[:, cols], h[:, cols], ACT.Copy, scale=gains[:, t : t + 1])
-                acc = psum.tile([P, BANK], F32, name="acc", bufs=2)
-                for a in range(PASSES):
-                    nc.tensor.matmul_mx(
-                        out=acc[:],
-                        lhsT=w1_q[:, (t * PASSES + a) * P : (t * PASSES + a + 1) * P].bitcast(FP8X4),
-                        lhsT_scale=w1_sc[:, (t * PASSES + a) * P : (t * PASSES + a + 1) * P],
-                        rhs=v[a][:, cols].bitcast(FP8X4),
-                        rhs_scale=v_sc[4 * a : P, cols],
-                        start=(a == 0),
-                        stop=(a == PASSES - 1),
-                    )
-                sq = factors[1][:, 0:BANK] if (t, half) == (0, 1) else h[:, cols]
-                if t + 1 < PACK:
-                    root = factors[t + 1][:, cols].rearrange("p (u m) -> p u m", u=PACK)
-                else:
-                    root = rounded[half][:].bitcast(F32)[:, :, 0 : BANK // PACK]
-                nc.scalar.activation(sq, acc[:], ACT.Square)
-                nc.scalar.activation(
-                    root, sq.rearrange("p (u m) -> p u m", u=PACK), ACT.Abs_reciprocal_sqrt, bias=1.0
+        resp = [keep.tile([P, S], F32, name=f"resp{t}", align_bytes=64) for t in range(PACK)]
+        roots = keep.tile([P, S], F32, name="roots", align_bytes=64)
+
+        halves = [(0, BANK), (BANK, S)]
+        quarters = [(j, j + FIRST) for j in range(0, S, FIRST)]
+
+        def weigh(t, j0, j1):
+            nc.scalar.activation(factors[t][:, j0:j1], dealt[t][:, j0:j1], ACT.Copy, scale=gains[:, t : t + 1])
+
+        def square(t, j0, j1, dst):
+            acc = psum.tile([P, j1 - j0], F32, name="acc", bufs=3)
+            for a in range(PASSES):
+                codes, bytes_ = w1_q[a, t]
+                nc.tensor.matmul_mx(
+                    out=acc[:],
+                    lhsT=codes.bitcast(FP8X4),
+                    lhsT_scale=bytes_,
+                    rhs=v[a][:, j0:j1].bitcast(FP8X4),
+                    rhs_scale=v_sc[4 * a : P, j0:j1],
+                    start=(a == 0),
+                    stop=(a == PASSES - 1),
                 )
-                nc.scalar.activation(h[:, cols].rearrange("p (u m) -> p u m", u=PACK), root, ACT.Square)
-                if t < 2:
-                    nc.vector.tensor_tensor(
-                        page[t][:].indirect(put[:, half * (BANK // 16) : (half + 1) * (BANK // 16)]),
-                        h[:, cols], factor[:, cols], ALU.mult,
-                    )
-            if t >= 2:
-                nc.vector.tensor_tensor(page[t][:].indirect(put[:]), h, factor[:], ALU.mult)
+            nc.scalar.activation(dst, acc[:], ACT.Square)
+
+        def in_four(ap):
+            return ap.rearrange("p (u m) -> p u m", u=PACK)
+
+        def root_of(t, j0, j1):
+            if t + 1 < PACK:
+                return in_four(roots[:, j0:j1])
+            return rounded[j0 // BANK][:].bitcast(F32)[:, :, 0 : BANK // PACK]
+
+        def root(t, j0, j1, src):
+            nc.scalar.activation(root_of(t, j0, j1), in_four(src), ACT.Abs_reciprocal_sqrt, bias=1.0)
+
+        def respond(t, j0, j1):
+            nc.scalar.activation(in_four(resp[t][:, j0:j1]), root_of(t, j0, j1), ACT.Square)
+
+        def scatter(t, j0, j1):
+            nc.vector.tensor_tensor(
+                page[t][:].indirect(entries(put, j0, j1)), resp[t][:, j0:j1], factors[t][:, j0:j1], ALU.mult
+            )
+
+        def pair(t, spans):
+            weigh(t, spans[0][0], spans[-1][1])
+            for j0, j1 in spans:
+                square(t, j0, j1, dealt[t][:, j0:j1])
+            for j0, j1 in spans:
+                root(t, j0, j1, dealt[t][:, j0:j1])
+            for j0, j1 in spans:
+                respond(t, j0, j1)
+            scatter(t, spans[0][0], spans[-1][1])
+
+        pair(0, quarters[:2])
+        pair(0, quarters[2:])
+        nc.sync.dma_start(page_dst[0], page[0][:])
+        for t in range(1, PACK):
+            pair(t, halves)
             nc.sync.dma_start(page_dst[t], page[t][:])
         nc.scalar.activation(warm[:, 0:1], resp[PACK - 1][:, S - 1 : S], ACT.Sin, scale=0.0)
 
@@ -185,83 +207,102 @@ def tile_list_rod_checkpoint_kernel(
             wd_bf[:].rearrange("p (c i) j -> p c j i", i=4),
             wd_raw[:].rearrange("p j (c i) -> p c j i", i=4),
         )
+
+        def round_page(t, m0, m1):
+            g, base = divmod(m0, 2 * BANK)
+            nc.scalar.copy(rounded[g][:, t, base : base + m1 - m0], page[t][:, m0:m1])
+
         for t in range(PACK - 1):
             for g in range(HALVES):
                 round_page(t, 2 * g * BANK, (2 * g + 2) * BANK)
 
+        pieces = [(0, FIRST), (FIRST, BANK)] + [(c * BANK, (c + 1) * BANK) for c in range(1, CHUNKS)]
+        for piece in pieces:
+            round_page(PACK - 1, *piece)
+
         words = keep.tile([P, T2], U32, name="words", align_bytes=64)
         scales = keep.tile([P, T2], U8, name="scales", align_bytes=64)
         words_dst = out_2[0].rearrange("p m t -> p (m t)").bitcast(I32)
-
-        def quantise_page(m0, m1):
-            cols = slice(m0, m1)
-            g, base = divmod(m0, 2 * BANK)
-            round_page(PACK - 1, m0, m1)
-            grouped = work.tile([P, m1 - m0, PACK], BF16, name="grouped", align_bytes=64)
-            nc.vector.tensor_copy(
-                grouped[:].rearrange("p (c i) t -> p c t i", i=4),
-                rounded[g][:, :, base : base + m1 - m0].rearrange("p t (c i) -> p c t i", i=4),
-            )
-            nc.vector.quantize_mx(
-                out=words[:, cols].bitcast(FP8X4),
-                scales=scales[:, cols],
-                in_=grouped[:].rearrange("p m t -> p (m t)"),
-            )
-            nc.sync.dma_start(words_dst[:, cols], words[:, cols].bitcast(I32))
-
-        def products(c, pieces):
-            cols = slice(c * BANK, (c + 1) * BANK)
-            for n in range(NT):
-                half_cos = work.tile([P, BANK], F32, name="half_cos")
-                for m0, m1 in pieces:
-                    phase = psum.tile([P, m1 - m0], F32, name="phase", tag="acc", bufs=2)
-                    nc.tensor.matmul_mx(
-                        out=phase[:],
-                        lhsT=wc[:, 2 * n * P : 2 * (n + 1) * P].bitcast(FP4X4),
-                        lhsT_scale=wc_sc[:, n * P : (n + 1) * P],
-                        rhs=words[:, m0:m1].bitcast(FP8X4),
-                        rhs_scale=scales[:, m0:m1],
-                        start=True,
-                        stop=True,
-                    )
-                    nc.scalar.activation(
-                        half_cos[:, m0 - c * BANK : m1 - c * BANK], phase[:], ACT.Sin, scale=0.5, bias=math.pi / 2
-                    )
-                value = psum.tile([P, BANK], F32, name="value", bufs=6)
-                nc.tensor.matmul_mx(
-                    out=value[:],
-                    lhsT=wd_q[:, n * P : (n + 1) * P].bitcast(FP8X4),
-                    lhsT_scale=wd_sc[:, n * P : (n + 1) * P],
-                    rhs=words[:, cols].bitcast(FP8X4),
-                    rhs_scale=scales[:, cols],
-                    start=True,
-                    stop=True,
-                )
-                cos_up = work.tile([P, BANK], F32, name="cos_up", bufs=6)
-                nc.scalar.activation(cos_up[:], half_cos[:], ACT.Square, scale=math.sqrt(2.0))
-                y = work.tile([P, BANK], F32, name="y", bufs=12)
-                nc.vector.scalar_tensor_tensor(y[:], cos_up[:], -1.0, value[:], ALU.add, ALU.mult)
-                nc.sync.dma_start(out_0[n * P : (n + 1) * P, cols], y[:])
-
-        pieces = [[(c * BANK, (c + 1) * BANK)] for c in range(CHUNKS)]
-        pieces[0] = [(0, BANK // 2), (BANK // 2, BANK)]
-        for piece in pieces[0]:
-            quantise_page(*piece)
         wd_q = keep.tile([P, N], U32, name="wd_q", tag="factor3", align_bytes=64)
         wd_sc = keep.tile([P, N], U8, name="wd_sc", align_bytes=64)
-        for n0, n1 in ((0, P), (P, N)):
+
+        def quantise_wd(n0, n1):
             nc.vector.quantize_mx(
                 out=wd_q[:, n0:n1].bitcast(FP8X4),
                 scales=wd_sc[:, n0:n1],
                 in_=wd_bf[:].rearrange("p n j -> p (n j)")[:, n0 * PACK : n1 * PACK],
             )
-        for c in range(CHUNKS):
-            if c + 1 < CHUNKS:
-                quantise_page(*pieces[c + 1][0])
-            else:
+
+        def regroup(m0, m1):
+            g, base = divmod(m0, 2 * BANK)
+            grouped = work.tile([P, m1 - m0, PACK], BF16, name="grouped", align_bytes=64)
+            nc.vector.tensor_copy(
+                grouped[:].rearrange("p (c i) t -> p c t i", i=4),
+                rounded[g][:, :, base : base + m1 - m0].rearrange("p t (c i) -> p c t i", i=4),
+            )
+            return grouped
+
+        def quantise_page(grouped, m0, m1):
+            nc.vector.quantize_mx(
+                out=words[:, m0:m1].bitcast(FP8X4),
+                scales=scales[:, m0:m1],
+                in_=grouped[:].rearrange("p m t -> p (m t)"),
+            )
+            nc.sync.dma_start(words_dst[:, m0:m1], words[:, m0:m1].bitcast(I32))
+
+        def half_cosine(n, m0, m1):
+            phase = psum.tile([P, m1 - m0], F32, name="phase", tag="acc", bufs=3)
+            nc.tensor.matmul_mx(
+                out=phase[:],
+                lhsT=wc[:, 2 * n * P : 2 * (n + 1) * P].bitcast(FP4X4),
+                lhsT_scale=wc_sc[:, n * P : (n + 1) * P],
+                rhs=words[:, m0:m1].bitcast(FP8X4),
+                rhs_scale=scales[:, m0:m1],
+                start=True,
+                stop=True,
+            )
+            half_cos = work.tile([P, m1 - m0], F32, name="half_cos", bufs=4)
+            nc.scalar.activation(half_cos[:], phase[:], ACT.Sin, scale=0.5, bias=math.pi / 2)
+            return half_cos
+
+        def finish(half_cos, n, m0, m1):
+            value = psum.tile([P, m1 - m0], F32, name="value", bufs=5)
+            nc.tensor.matmul_mx(
+                out=value[:],
+                lhsT=wd_q[:, n * P : (n + 1) * P].bitcast(FP8X4),
+                lhsT_scale=wd_sc[:, n * P : (n + 1) * P],
+                rhs=words[:, m0:m1].bitcast(FP8X4),
+                rhs_scale=scales[:, m0:m1],
+                start=True,
+                stop=True,
+            )
+            cos_up = work.tile([P, m1 - m0], F32, name="cos_up", bufs=6)
+            nc.scalar.activation(cos_up[:], half_cos[:], ACT.Square, scale=math.sqrt(2.0))
+            y = work.tile([P, m1 - m0], F32, name="y", bufs=12)
+            nc.vector.scalar_tensor_tensor(y[:], cos_up[:], -1.0, value[:], ALU.add, ALU.mult)
+            nc.sync.dma_start(out_0[n * P : (n + 1) * P, m0:m1], y[:])
+
+        quantise_wd(0, P)
+        grouped = regroup(*pieces[0])
+        quantise_wd(P, N)
+        quantise_page(grouped, *pieces[0])
+        quantise_page(regroup(*pieces[1]), *pieces[1])
+        behind = None
+        for i, whole in enumerate(pieces):
+            if i + 2 < len(pieces):
+                quantise_page(regroup(*pieces[i + 2]), *pieces[i + 2])
+            if i + 3 == len(pieces):
                 for q in range(QUADS):
                     nc.sync.dma_start(
                         out_3[0, 4 * q : 4 * q + 4, :].bitcast(I32),
                         scales[32 * q : 32 * q + 4, :].bitcast(I32),
                     )
-            products(c, pieces[c])
+            for n in range(NT):
+                m0, m1 = whole
+                last = i + 1 == len(pieces) and n + 1 == NT
+                for piece in ((m0, m1 - FIRST), (m1 - FIRST, m1)) if last else (whole,):
+                    now = (half_cosine(n, *piece), n, *piece)
+                    if behind is not None:
+                        finish(*behind)
+                    behind = now
+        finish(*behind)

@@ -2,6 +2,7 @@ import math
 from contextlib import ExitStack
 
 import concourse.mybir as mybir
+from concourse.masks import make_identity
 
 K, T, S, T2, H, N = 1024, 2048, 1024, 2048, 512, 384
 FLOPS = 2 * K * H * S + 2 * 2 * H * N * T2
@@ -22,9 +23,12 @@ PACK = 4
 QUADS = 4
 BANK = 512
 PASSES = K // (P * PACK)
-HALVES = S // BANK
+TILES = H // P
 CHUNKS = T2 // BANK
 NT = N // P
+QUARTER = S // 4
+HALF = S // 2
+PIECE = BANK // 2
 
 
 def tile_list_rod_checkpoint_kernel(
@@ -42,7 +46,7 @@ def tile_list_rod_checkpoint_kernel(
         put = lists.tile([P, S // 16], U16, name="put")
 
         tab_sc = keep.tile([P, T], U8, name="tab_sc", align_bytes=64)
-        nc.vector.memset(tab_sc[:].bitcast(I32), 0)
+        nc.gpsimd.memset(tab_sc[:].bitcast(I32), 0)
 
         one = keep.tile([P, 8], F32, name="one")
         warm = keep.tile([P, 8], F32, name="warm")
@@ -51,50 +55,52 @@ def tile_list_rod_checkpoint_kernel(
 
         wc_sc = keep.tile([P, N], U8, name="wc_sc", align_bytes=64)
         nc.vector.memset(wc_sc[:].bitcast(I32), 0)
+        ident = keep.tile([P, P], F32, name="ident")
+        make_identity(nc, ident[:])
 
         tab = [keep.tile([P, T], U32, name=f"tab{a}", align_bytes=64) for a in range(PASSES)]
-        w1_raw = [keep.tile([P, PACK, H], F32, name=f"w1_raw{a}") for a in range(PASSES)]
+        w1_raw = [keep.tile([P, PASSES * PACK * P], F32, name=f"w1_raw{u}") for u in range(TILES)]
         w1_rows = w1.rearrange("(a p j) c -> a p j c", p=P, j=PACK)
+        page = [keep.tile([P, T2], F32, name=f"page{u}") for u in range(TILES)]
+        weights = keep.tile([P, S], F32, name="weights", align_bytes=64)
+        gains = keep.tile([P, 8], F32, name="gains")
+        wd_raw = keep.tile([P, PACK * N], F32, name="wd_raw")
+        wc = keep.tile([P, 2 * N], U8, name="wc", align_bytes=64)
 
-        def tab_src(a):
-            return tab_words[a].rearrange("p t i -> p (t i)").bitcast(I32)
+        def load_tab(a):
+            nc.sync.dma_start(tab[a][:].bitcast(I32), tab_words[a].rearrange("p t i -> p (t i)").bitcast(I32))
+
+        def load_w1(u):
+            for a in range(PASSES):
+                nc.sync.dma_start(
+                    w1_raw[u][:, a * PACK * P : (a + 1) * PACK * P].rearrange("p (j c) -> p j c", j=PACK),
+                    w1_rows[a][:, :, u * P : (u + 1) * P],
+                )
+
+        def load_page(u):
+            nc.sync.dma_start(page[u][:], page0[u * P : (u + 1) * P, :])
 
         nc.sync.dma_start(pick[:], offs)
-        nc.sync.dma_start(tab[0][:].bitcast(I32), tab_src(0))
         for q in range(QUADS):
             nc.sync.dma_start(
                 tab_sc[32 * q : 32 * q + 4 * PASSES, :].bitcast(I32),
                 tab_scales[:, 4 * q : 4 * q + 4, :].bitcast(I32),
             )
-        for a in range(PASSES):
-            nc.sync.dma_start(w1_raw[a][:], w1_rows[a])
-
-        wgs_rows = wgs.rearrange("(q t) j -> q t j", t=PACK)
-        dealt = [keep.tile([P, S], F32, name=f"dealt{t}") for t in range(PACK)]
-
-        def load_wgs(t, j0, j1):
-            for q in (0, 2, 1, 3):
-                nc.sync.dma_start(dealt[t][32 * q : 32 * q + 32, j0:j1], wgs_rows[:, t, j0:j1])
-
-        nc.sync.dma_start(tab[1][:].bitcast(I32), tab_src(1))
-        FIRST = BANK // 2
-        gains = keep.tile([P, 8], F32, name="gains")
-        nc.sync.dma_start(gains[:, 0:PACK], gain.rearrange("(p t) -> p t", t=PACK))
-        load_wgs(0, 0, BANK)
+        with nc.allow_non_contiguous_dma(reason="one gain for each partition and row tile"):
+            nc.sync.dma_start(gains[:, 0:TILES], gain.rearrange("(u p) -> p u", p=P))
+        nc.sync.dma_start(weights[:], wgs)
+        load_tab(0)
+        load_w1(0)
+        load_tab(1)
         nc.sync.dma_start(put[:], offs2)
-        page = [keep.tile([P, T2], F32, name=f"page{t}") for t in range(PACK)]
-        page_src = page0.rearrange("(p t) m -> t p m", t=PACK)
-        page_dst = out_1.rearrange("(p t) m -> t p m", t=PACK)
-        nc.sync.dma_start(page[0][:], page_src[0])
-        load_wgs(0, BANK, S)
-        for t in range(1, PACK - 1):
-            load_wgs(t, 0, S)
-            nc.sync.dma_start(page[t][:], page_src[t])
-        wd_raw = keep.tile([P, PACK, N], F32, name="wd_raw")
-        nc.sync.dma_start(wd_raw[:], wd.rearrange("(p j) n -> p j n", j=PACK))
-        load_wgs(PACK - 1, 0, S)
-        nc.sync.dma_start(page[PACK - 1][:], page_src[PACK - 1])
-        wc = keep.tile([P, 2 * N], U8, name="wc", align_bytes=64)
+        load_page(0)
+        load_w1(1)
+        load_w1(2)
+        load_w1(3)
+        load_page(1)
+        nc.sync.dma_start(wd_raw[:].rearrange("p (j n) -> p j n", j=PACK), wd.rearrange("(p j) n -> p j n", j=PACK))
+        load_page(2)
+        load_page(3)
         nc.sync.dma_start(wc[:].bitcast(I32), wc_words[0].bitcast(I32))
         for q in range(QUADS):
             nc.sync.dma_start(
@@ -105,153 +111,181 @@ def tile_list_rod_checkpoint_kernel(
         def entries(lst, j0, j1):
             return lst[:] if (j0, j1) == (0, S) else lst[:, j0 // 16 : j1 // 16]
 
-        v = [keep.tile([P, S], U32, name=f"v{a}", align_bytes=64) for a in range(PASSES)]
-        v_sc = keep.tile([P, S], U8, name="v_sc", align_bytes=64)
-        nc.vector.tensor_copy(v[0][:], tab[0][:].indirect(pick[:]))
-        nc.vector.tensor_copy(v_sc[:], tab_sc[:].indirect(pick[:]))
-
-        w1_q = {}
-
-        def round_w1(engine_copy, a, t0, t1):
-            bf = keep.tile([P, t1 - t0, P, PACK], BF16, name=f"w1_bf{a}_{t0}", align_bytes=64)
-            engine_copy(
-                bf[:].rearrange("p t m j -> p m j t"),
-                w1_raw[a][:].rearrange("p j (m t) -> p m j t", t=PACK)[:, :, :, t0:t1],
+        def interleave(raw, width):
+            bf = work.tile([P, raw.shape[1]], BF16, name="bf", bufs=2, align_bytes=64)
+            nc.scalar.copy(
+                bf[:].rearrange("p (a c i j) -> p a c j i", i=4, j=PACK, c=width // 4),
+                raw.rearrange("p (a j c i) -> p a c j i", i=4, j=PACK, c=width // 4),
             )
             return bf
 
-        def quantise_w1(bf, a, t0, t1):
-            codes = keep.tile([P, (t1 - t0) * P], U32, name=f"w1_q{a}_{t0}", align_bytes=64)
-            bytes_ = keep.tile([P, (t1 - t0) * P], U8, name=f"w1_sc{a}_{t0}", align_bytes=64)
-            nc.vector.quantize_mx(
-                out=codes[:].bitcast(FP8X4), scales=bytes_[:], in_=bf[:].rearrange("p t m j -> p (t m j)")
-            )
-            for t in range(t0, t1):
-                cols = slice((t - t0) * P, (t - t0 + 1) * P)
-                w1_q[a, t] = (codes[:, cols], bytes_[:, cols])
+        def quantise(bf, name, c0, c1):
+            codes = keep.tile([P, c1 - c0], U32, name=f"{name}_q", align_bytes=64)
+            bytes_ = keep.tile([P, c1 - c0], U8, name=f"{name}_sc", align_bytes=64)
+            nc.vector.quantize_mx(out=codes[:].bitcast(FP8X4), scales=bytes_[:], in_=bf[:, c0 * PACK : c1 * PACK])
+            return codes, bytes_
 
-        first = round_w1(nc.scalar.copy, 0, 0, PACK)
-        early = round_w1(nc.vector.tensor_copy, 1, 0, PACK // 2)
-        late = round_w1(nc.scalar.copy, 1, PACK // 2, PACK)
-        quantise_w1(first, 0, 0, PACK)
-        quantise_w1(early, 1, 0, PACK // 2)
-        for j0, j1 in ((0, FIRST), (FIRST, BANK), (BANK, S)):
+        v = [keep.tile([P, S], U32, name=f"v{a}", align_bytes=64) for a in range(PASSES)]
+        v_sc = keep.tile([P, S], U8, name="v_sc", align_bytes=64)
+        nc.vector.tensor_copy(v_sc[:], tab_sc[:].indirect(pick[:]))
+        nc.vector.tensor_copy(v[0][:], tab[0][:].indirect(pick[:]))
+        factors = [keep.tile([P, S], F32, name=f"factor{u}", align_bytes=64) for u in range(TILES - 1)]
+        factors.append(w1_raw[0])
+
+        def weigh(u):
+            nc.scalar.activation(factors[u][:], weights[:], ACT.Copy, scale=gains[:, u : u + 1])
+
+        for u in range(TILES - 1):
+            weigh(u)
+        w1_q = [quantise(interleave(w1_raw[0][:], P), "w1_0", 0, PASSES * P)]
+        weigh(TILES - 1)
+        for j0, j1 in ((0, QUARTER), (QUARTER, HALF), (HALF, S)):
             nc.vector.tensor_copy(v[1][:, j0:j1], tab[1][:].indirect(entries(pick, j0, j1)))
-        quantise_w1(late, 1, PACK // 2, PACK)
 
-        rounded = [keep.tile([P, PACK, 2 * BANK], BF16, name=f"rounded{g}", align_bytes=64) for g in range(HALVES)]
-        wd_bf = keep.tile([P, N, PACK], BF16, name="wd_bf", align_bytes=64)
-        factors = [keep.tile([P, S], F32, name=f"factor{t}", align_bytes=64) for t in range(PACK)]
-        resp = [keep.tile([P, S], F32, name=f"resp{t}", align_bytes=64) for t in range(PACK)]
-        roots = keep.tile([P, S], F32, name="roots", align_bytes=64)
+        turned = keep.tile([P, T2 * PACK], BF16, name="turned", align_bytes=64)
+        turned_words = turned[:].bitcast(F32)
+        squares = keep.tile([P, S], F32, name="squares", align_bytes=64)
+        rows = turned_words.rearrange("p (a x) -> p a x", x=P)
+        roots_at = [3, 3, 0, 2]
 
-        halves = [(0, BANK), (BANK, S)]
-        quarters = [(j, j + FIRST) for j in range(0, S, FIRST)]
+        def in_runs(ap):
+            return ap.rearrange("p (a b) -> p a b", a=32)
 
-        def weigh(t, j0, j1):
-            nc.scalar.activation(factors[t][:, j0:j1], dealt[t][:, j0:j1], ACT.Copy, scale=gains[:, t : t + 1])
+        def roots_of(u, j0, j1):
+            at = 32 * roots_at[u]
+            return rows[:, :, at + j0 // 32 : at + j1 // 32]
 
-        def square(t, j0, j1, dst):
-            acc = psum.tile([P, j1 - j0], F32, name="acc", bufs=3)
+        def square(u, j0, j1, dst):
+            acc = psum.tile([P, j1 - j0], F32, name="acc", bufs=2)
+            codes, bytes_ = w1_q[u]
             for a in range(PASSES):
-                codes, bytes_ = w1_q[a, t]
                 nc.tensor.matmul_mx(
                     out=acc[:],
-                    lhsT=codes.bitcast(FP8X4),
-                    lhsT_scale=bytes_,
+                    lhsT=codes[:, a * P : (a + 1) * P].bitcast(FP8X4),
+                    lhsT_scale=bytes_[:, a * P : (a + 1) * P],
                     rhs=v[a][:, j0:j1].bitcast(FP8X4),
                     rhs_scale=v_sc[4 * a : P, j0:j1],
                     start=(a == 0),
                     stop=(a == PASSES - 1),
                 )
-            nc.scalar.activation(dst, acc[:], ACT.Square)
+            nc.scalar.activation(dst, in_runs(acc[:]), ACT.Square)
 
-        def in_four(ap):
-            return ap.rearrange("p (u m) -> p u m", u=PACK)
+        def root(u, j0, j1, src):
+            nc.scalar.activation(roots_of(u, j0, j1), src, ACT.Abs_reciprocal_sqrt, bias=1.0)
 
-        def root_of(t, j0, j1):
-            if t + 1 < PACK:
-                return in_four(roots[:, j0:j1])
-            return rounded[j0 // BANK][:].bitcast(F32)[:, :, 0 : BANK // PACK]
+        def respond(u, j0, j1, dst):
+            nc.scalar.activation(in_runs(dst), roots_of(u, j0, j1), ACT.Square)
 
-        def root(t, j0, j1, src):
-            nc.scalar.activation(root_of(t, j0, j1), in_four(src), ACT.Abs_reciprocal_sqrt, bias=1.0)
+        def scatter(u, j0, j1, resp):
+            nc.vector.tensor_tensor(page[u][:].indirect(entries(put, j0, j1)), resp, factors[u][:, j0:j1], ALU.mult)
 
-        def respond(t, j0, j1):
-            nc.scalar.activation(in_four(resp[t][:, j0:j1]), root_of(t, j0, j1), ACT.Square)
+        def turn_columns(u, m0, m1, bank, engine_copy):
+            for m in range(m0, m1, P):
+                nc.tensor.transpose(bank[:, m - m0 : m - m0 + P], page[u][:, m : m + P], ident[:])
+            dst = turned[:, m0 * PACK : m1 * PACK].rearrange("p (b h g q e) -> p b h g q e", h=2, g=TILES, q=32, e=2)
+            engine_copy(dst[:, :, :, u, :, :], bank[:].rearrange("p (b q h e) -> p b h q e", q=32, h=2, e=2))
 
-        def scatter(t, j0, j1):
-            nc.vector.tensor_tensor(
-                page[t][:].indirect(entries(put, j0, j1)), resp[t][:, j0:j1], factors[t][:, j0:j1], ALU.mult
-            )
+        def turn_page(u, c, engine_copy):
+            bank = psum.tile([P, BANK], F32, name="turn", bufs=3)
+            turn_columns(u, c * BANK, (c + 1) * BANK, bank, engine_copy)
 
-        def pair(t, spans):
-            weigh(t, spans[0][0], spans[-1][1])
-            for j0, j1 in spans:
-                square(t, j0, j1, dealt[t][:, j0:j1])
-            for j0, j1 in spans:
-                root(t, j0, j1, dealt[t][:, j0:j1])
-            for j0, j1 in spans:
-                respond(t, j0, j1)
-            scatter(t, spans[0][0], spans[-1][1])
+        def store_page(u):
+            nc.sync.dma_start(out_1[u * P : (u + 1) * P, :], page[u][:])
 
-        pair(0, quarters[:2])
-        pair(0, quarters[2:])
-        nc.sync.dma_start(page_dst[0], page[0][:])
-        for t in range(1, PACK):
-            pair(t, halves)
-            nc.sync.dma_start(page_dst[t], page[t][:])
-        nc.scalar.activation(warm[:, 0:1], resp[PACK - 1][:, S - 1 : S], ACT.Sin, scale=0.0)
+        def squares_of(j0, j1):
+            return in_runs(squares[:, j0:j1])
 
-        nc.scalar.copy(
-            wd_bf[:].rearrange("p (c i) j -> p c j i", i=4),
-            wd_raw[:].rearrange("p j (c i) -> p c j i", i=4),
+        def round_w1(u):
+            w1_q.append(quantise(interleave(w1_raw[u][:], P), f"w1_{u}", 0, PASSES * P))
+
+        resp = keep.tile([P, S], F32, name="resp", align_bytes=64)
+
+        quarters = [(0, QUARTER), (QUARTER, HALF)]
+        for span in quarters:
+            square(0, *span, squares_of(*span))
+        for span in quarters:
+            root(0, *span, squares_of(*span))
+        for j0, j1 in quarters:
+            respond(0, j0, j1, resp[:, j0:j1])
+        scatter(0, 0, HALF, resp[:, 0:HALF])
+        square(0, HALF, S, roots_of(0, 0, HALF))
+        round_w1(1)
+        root(0, HALF, S, roots_of(0, 0, HALF))
+        respond(0, HALF, S, w1_raw[1][:, 0:HALF])
+        scatter(0, HALF, S, w1_raw[1][:, 0:HALF])
+        store_page(0)
+
+        round_w1(2)
+        square(1, 0, QUARTER, squares_of(0, QUARTER))
+        root(1, 0, QUARTER, squares_of(0, QUARTER))
+        respond(1, 0, QUARTER, w1_raw[2][:, 0:QUARTER])
+        scatter(1, 0, QUARTER, w1_raw[2][:, 0:QUARTER])
+        square(1, QUARTER, HALF, squares_of(QUARTER, HALF))
+        square(1, HALF, S, squares_of(HALF, S))
+        root(1, QUARTER, S, squares_of(QUARTER, S))
+        respond(1, QUARTER, S, resp[:, QUARTER:S])
+        scatter(1, QUARTER, S, resp[:, QUARTER:S])
+        store_page(1)
+
+        round_w1(3)
+        square(2, 0, HALF, squares_of(0, HALF))
+        square(2, HALF, S, squares_of(HALF, S))
+        nc.scalar.activation(
+            roots_of(2, 0, S).rearrange("p a (h x) -> p a h x", h=2),
+            squares[:].rearrange("p (h a x) -> p a h x", h=2, a=32),
+            ACT.Abs_reciprocal_sqrt,
+            bias=1.0,
         )
+        respond(2, 0, HALF, w1_raw[3][:, 0:HALF])
+        scatter(2, 0, HALF, w1_raw[3][:, 0:HALF])
+        wd_bf = work.tile([P, PACK * N], BF16, name="bf", bufs=2, align_bytes=64)
+        nc.scalar.activation(
+            wd_bf[:].rearrange("p (c i j) -> p c j i", i=4, j=PACK),
+            wd_raw[:].rearrange("p (j c i) -> p c j i", i=4, j=PACK),
+            ACT.Copy,
+            scale=2.0,
+        )
+        wd_q = [quantise(wd_bf, "wd0", 0, P), quantise(wd_bf, "wd1", P, N)]
+        respond(2, HALF, S, wd_raw[:, 0:HALF])
+        scatter(2, HALF, S, wd_raw[:, 0:HALF])
+        store_page(2)
+        for c in range(CHUNKS):
+            turn_page(0, c, nc.scalar.copy)
 
-        def round_page(t, m0, m1):
-            g, base = divmod(m0, 2 * BANK)
-            nc.scalar.copy(rounded[g][:, t, base : base + m1 - m0], page[t][:, m0:m1])
-
-        for t in range(PACK - 1):
-            for g in range(HALVES):
-                round_page(t, 2 * g * BANK, (2 * g + 2) * BANK)
-
-        pieces = [(0, FIRST), (FIRST, BANK)] + [(c * BANK, (c + 1) * BANK) for c in range(1, CHUNKS)]
-        for piece in pieces:
-            round_page(PACK - 1, *piece)
+        square(3, 0, HALF, squares_of(0, HALF))
+        square(3, HALF, S, squares_of(HALF, S))
+        root(3, 0, S, squares_of(0, S))
+        respond(3, 0, S, w1_raw[2][:])
+        scatter(3, 0, S, w1_raw[2][:])
+        store_page(3)
+        for u, c in ((2, 0), (2, 1), (2, 2), (1, 0), (1, 1), (1, 2), (1, 3), (2, 3)):
+            turn_page(u, c, nc.scalar.copy)
+        nc.scalar.activation(warm[:, 0:1], w1_raw[2][:, S - 1 : S], ACT.Sin, scale=0.0)
 
         words = keep.tile([P, T2], U32, name="words", align_bytes=64)
         scales = keep.tile([P, T2], U8, name="scales", align_bytes=64)
         words_dst = out_2[0].rearrange("p m t -> p (m t)").bitcast(I32)
-        wd_q = keep.tile([P, N], U32, name="wd_q", tag="factor3", align_bytes=64)
-        wd_sc = keep.tile([P, N], U8, name="wd_sc", align_bytes=64)
 
-        def quantise_wd(n0, n1):
-            nc.vector.quantize_mx(
-                out=wd_q[:, n0:n1].bitcast(FP8X4),
-                scales=wd_sc[:, n0:n1],
-                in_=wd_bf[:].rearrange("p n j -> p (n j)")[:, n0 * PACK : n1 * PACK],
-            )
-
-        def regroup(m0, m1):
-            g, base = divmod(m0, 2 * BANK)
-            grouped = work.tile([P, m1 - m0, PACK], BF16, name="grouped", align_bytes=64)
-            nc.vector.tensor_copy(
-                grouped[:].rearrange("p (c i) t -> p c t i", i=4),
-                rounded[g][:, :, base : base + m1 - m0].rearrange("p t (c i) -> p c t i", i=4),
+        def turn_back(i, engine_copy):
+            bank = psum.tile([P, BANK], F32, name="turn", bufs=3)
+            for k in range(BANK // P):
+                x0 = i * BANK + k * P
+                nc.tensor.transpose(bank[:, k * P : (k + 1) * P], turned_words[:, x0 : x0 + P], ident[:])
+            grouped = work.tile([P, PIECE * PACK], BF16, name="grouped", bufs=4, align_bytes=64)
+            engine_copy(
+                grouped[:].bitcast(F32).rearrange("p (b c h) -> p b c h", b=2, h=2),
+                bank[:].rearrange("p (b h c) -> p b c h", b=2, h=2),
             )
             return grouped
 
-        def quantise_page(grouped, m0, m1):
-            nc.vector.quantize_mx(
-                out=words[:, m0:m1].bitcast(FP8X4),
-                scales=scales[:, m0:m1],
-                in_=grouped[:].rearrange("p m t -> p (m t)"),
-            )
-            nc.sync.dma_start(words_dst[:, m0:m1], words[:, m0:m1].bitcast(I32))
+        def quantise_page(grouped, i):
+            m0, m1 = i * PIECE, (i + 1) * PIECE
+            nc.vector.quantize_mx(out=words[:, m0:m1].bitcast(FP8X4), scales=scales[:, m0:m1], in_=grouped[:])
+            if i % 2 == 1:
+                nc.sync.dma_start(words_dst[:, m0 - PIECE : m1], words[:, m0 - PIECE : m1].bitcast(I32))
 
         def half_cosine(n, m0, m1):
-            phase = psum.tile([P, m1 - m0], F32, name="phase", tag="acc", bufs=3)
+            phase = psum.tile([P, m1 - m0], F32, name="phase", tag="acc", bufs=2)
             nc.tensor.matmul_mx(
                 out=phase[:],
                 lhsT=wc[:, 2 * n * P : 2 * (n + 1) * P].bitcast(FP4X4),
@@ -265,33 +299,54 @@ def tile_list_rod_checkpoint_kernel(
             nc.scalar.activation(half_cos[:], phase[:], ACT.Sin, scale=0.5, bias=math.pi / 2)
             return half_cos
 
-        def finish(half_cos, n, m0, m1):
-            value = psum.tile([P, m1 - m0], F32, name="value", bufs=5)
+        def finish(half_cos, n, m0, m1, on_vector):
+            value = psum.tile([P, m1 - m0], F32, name="value", bufs=3)
+            codes, bytes_ = wd_q[min(n, 1)]
+            cols = slice(max(n - 1, 0) * P, max(n, 1) * P)
             nc.tensor.matmul_mx(
                 out=value[:],
-                lhsT=wd_q[:, n * P : (n + 1) * P].bitcast(FP8X4),
-                lhsT_scale=wd_sc[:, n * P : (n + 1) * P],
+                lhsT=codes[:, cols].bitcast(FP8X4),
+                lhsT_scale=bytes_[:, cols],
                 rhs=words[:, m0:m1].bitcast(FP8X4),
                 rhs_scale=scales[:, m0:m1],
                 start=True,
                 stop=True,
             )
-            cos_up = work.tile([P, m1 - m0], F32, name="cos_up", bufs=6)
-            nc.scalar.activation(cos_up[:], half_cos[:], ACT.Square, scale=math.sqrt(2.0))
-            y = work.tile([P, m1 - m0], F32, name="y", bufs=12)
-            nc.vector.scalar_tensor_tensor(y[:], cos_up[:], -1.0, value[:], ALU.add, ALU.mult)
+            cos_up = work.tile([P, m1 - m0], F32, name="cos_up", bufs=4)
+            if on_vector:
+                nc.vector.tensor_tensor(cos_up[:], half_cos[:], half_cos[:], ALU.mult)
+            else:
+                nc.scalar.activation(cos_up[:], half_cos[:], ACT.Square)
+            y = work.tile([P, m1 - m0], F32, name="y", bufs=8)
+            nc.vector.scalar_tensor_tensor(y[:], cos_up[:], -0.5, value[:], ALU.add, ALU.mult)
             nc.sync.dma_start(out_0[n * P : (n + 1) * P, m0:m1], y[:])
 
-        quantise_wd(0, P)
-        grouped = regroup(*pieces[0])
-        quantise_wd(P, N)
-        quantise_page(grouped, *pieces[0])
-        quantise_page(regroup(*pieces[1]), *pieces[1])
+        last = TILES - 1
+        for i, engine_copy in enumerate((nc.vector.tensor_copy, nc.vector.tensor_copy)):
+            bank = psum.tile([P, PIECE], F32, name="turn", bufs=3)
+            turn_columns(last, i * PIECE, (i + 1) * PIECE, bank, engine_copy)
+        ready = [turn_back(0, nc.vector.tensor_copy), turn_back(1, nc.vector.tensor_copy)]
+        quantise_page(ready[0], 0)
+        quantise_page(ready[1], 1)
+        for c in range(1, CHUNKS):
+            bank = psum.tile([P, BANK], F32, name="value", bufs=3)
+            turn_columns(last, c * BANK, (c + 1) * BANK, bank, nc.scalar.copy)
+        ready = [turn_back(2, nc.scalar.copy), turn_back(3, nc.vector.tensor_copy)]
+        quantise_page(ready[0], 2)
+        quantise_page(ready[1], 3)
+
+        spans = [(0, PIECE), (PIECE, BANK)] + [(c * BANK, (c + 1) * BANK) for c in range(1, CHUNKS)]
         behind = None
-        for i, whole in enumerate(pieces):
-            if i + 2 < len(pieces):
-                quantise_page(regroup(*pieces[i + 2]), *pieces[i + 2])
-            if i + 3 == len(pieces):
+        count = 0
+        for i, whole in enumerate(spans):
+            if 1 <= i <= 2:
+                pair = [
+                    turn_back(2 * i + 2, nc.scalar.copy if i == 1 else nc.vector.tensor_copy),
+                    turn_back(2 * i + 3, nc.vector.tensor_copy),
+                ]
+                quantise_page(pair[0], 2 * i + 2)
+                quantise_page(pair[1], 2 * i + 3)
+            if i == 2:
                 for q in range(QUADS):
                     nc.sync.dma_start(
                         out_3[0, 4 * q : 4 * q + 4, :].bitcast(I32),
@@ -299,9 +354,10 @@ def tile_list_rod_checkpoint_kernel(
                     )
             for n in range(NT):
                 m0, m1 = whole
-                last = i + 1 == len(pieces) and n + 1 == NT
-                for piece in ((m0, m1 - FIRST), (m1 - FIRST, m1)) if last else (whole,):
-                    now = (half_cosine(n, *piece), n, *piece)
+                final = i + 1 == len(spans) and n + 1 == NT
+                for piece in ((m0, m1 - PIECE), (m1 - PIECE, m1)) if final else (whole,):
+                    now = (half_cosine(n, *piece), n, *piece, count % 4 == 3 and not final)
+                    count = count + 1
                     if behind is not None:
                         finish(*behind)
                     behind = now

@@ -59,7 +59,7 @@ def tile_list_rod_checkpoint_kernel(
         make_identity(nc, ident[:])
 
         tab = [keep.tile([P, T], U32, name=f"tab{a}", align_bytes=64) for a in range(PASSES)]
-        w1_raw = [keep.tile([P, PASSES * PACK * P], F32, name=f"w1_raw{u}") for u in range(TILES)]
+        w1_raw = [keep.tile([P, PASSES * PACK * P], F32, name=f"w1_raw{u}", align_bytes=64) for u in range(TILES)]
         w1_rows = w1.rearrange("(a p j) c -> a p j c", p=P, j=PACK)
         page = [keep.tile([P, T2], F32, name=f"page{u}") for u in range(TILES)]
         weights = keep.tile([P, S], F32, name="weights", align_bytes=64)
@@ -119,10 +119,10 @@ def tile_list_rod_checkpoint_kernel(
             )
             return bf
 
-        def quantise(bf, name, c0, c1):
-            codes = keep.tile([P, c1 - c0], U32, name=f"{name}_q", align_bytes=64)
-            bytes_ = keep.tile([P, c1 - c0], U8, name=f"{name}_sc", align_bytes=64)
-            nc.vector.quantize_mx(out=codes[:].bitcast(FP8X4), scales=bytes_[:], in_=bf[:, c0 * PACK : c1 * PACK])
+        def quantise(bf, name, tag):
+            codes = keep.tile([P, PASSES * P], U32, name=f"{name}_q", tag=tag, align_bytes=64)
+            bytes_ = keep.tile([P, PASSES * P], U8, name=f"{name}_sc", align_bytes=64)
+            nc.vector.quantize_mx(out=codes[:].bitcast(FP8X4), scales=bytes_[:], in_=bf[:])
             return codes, bytes_
 
         v = [keep.tile([P, S], U32, name=f"v{a}", align_bytes=64) for a in range(PASSES)]
@@ -137,7 +137,7 @@ def tile_list_rod_checkpoint_kernel(
 
         for u in range(TILES - 1):
             weigh(u)
-        w1_q = [quantise(interleave(w1_raw[0][:], P), "w1_0", 0, PASSES * P)]
+        w1_q = [quantise(interleave(w1_raw[0][:], P), "w1_0", "w1_0_q")]
         weigh(TILES - 1)
         for j0, j1 in ((0, QUARTER), (QUARTER, HALF), (HALF, S)):
             nc.vector.tensor_copy(v[1][:, j0:j1], tab[1][:].indirect(entries(pick, j0, j1)))
@@ -155,8 +155,8 @@ def tile_list_rod_checkpoint_kernel(
             at = 32 * roots_at[u]
             return rows[:, :, at + j0 // 32 : at + j1 // 32]
 
-        def square(u, j0, j1, dst):
-            acc = psum.tile([P, j1 - j0], F32, name="acc", bufs=2)
+        def square(u, j0, j1, dst, tag="acc"):
+            acc = psum.tile([P, j1 - j0], F32, name=tag, bufs=2 if tag == "acc" else 3)
             codes, bytes_ = w1_q[u]
             for a in range(PASSES):
                 nc.tensor.matmul_mx(
@@ -168,7 +168,7 @@ def tile_list_rod_checkpoint_kernel(
                     start=(a == 0),
                     stop=(a == PASSES - 1),
                 )
-            nc.scalar.activation(dst, in_runs(acc[:]), ACT.Square)
+            nc.scalar.activation(dst, acc[:] if dst.ndim == 2 else in_runs(acc[:]), ACT.Square)
 
         def root(u, j0, j1, src):
             nc.scalar.activation(roots_of(u, j0, j1), src, ACT.Abs_reciprocal_sqrt, bias=1.0)
@@ -196,7 +196,7 @@ def tile_list_rod_checkpoint_kernel(
             return in_runs(squares[:, j0:j1])
 
         def round_w1(u):
-            w1_q.append(quantise(interleave(w1_raw[u][:], P), f"w1_{u}", 0, PASSES * P))
+            return interleave(w1_raw[u][:], P)
 
         resp = keep.tile([P, S], F32, name="resp", align_bytes=64)
 
@@ -209,65 +209,57 @@ def tile_list_rod_checkpoint_kernel(
             respond(0, j0, j1, resp[:, j0:j1])
         scatter(0, 0, HALF, resp[:, 0:HALF])
         square(0, HALF, S, roots_of(0, 0, HALF))
-        round_w1(1)
+        w1_q.append(quantise(round_w1(1), "w1_1", "w1_1_q"))
         root(0, HALF, S, roots_of(0, 0, HALF))
         respond(0, HALF, S, w1_raw[1][:, 0:HALF])
         scatter(0, HALF, S, w1_raw[1][:, 0:HALF])
         store_page(0)
 
-        round_w1(2)
+        w1_q.append(quantise(round_w1(2), "w1_2", "w1_2_q"))
+        bf3 = round_w1(3)
         square(1, 0, QUARTER, squares_of(0, QUARTER))
         root(1, 0, QUARTER, squares_of(0, QUARTER))
         respond(1, 0, QUARTER, w1_raw[2][:, 0:QUARTER])
         scatter(1, 0, QUARTER, w1_raw[2][:, 0:QUARTER])
+        w1_q.append(quantise(bf3, "w1_3", "w1_raw2"))
         square(1, QUARTER, HALF, squares_of(QUARTER, HALF))
-        square(1, HALF, S, squares_of(HALF, S))
+        square(1, HALF, S, squares_of(HALF, S), "value")
         root(1, QUARTER, S, squares_of(QUARTER, S))
         respond(1, QUARTER, S, resp[:, QUARTER:S])
         scatter(1, QUARTER, S, resp[:, QUARTER:S])
         store_page(1)
 
-        round_w1(3)
-        square(2, 0, HALF, squares_of(0, HALF))
-        square(2, HALF, S, squares_of(HALF, S))
-        nc.scalar.activation(
-            roots_of(2, 0, S).rearrange("p a (h x) -> p a h x", h=2),
-            squares[:].rearrange("p (h a x) -> p a h x", h=2, a=32),
-            ACT.Abs_reciprocal_sqrt,
-            bias=1.0,
-        )
-        respond(2, 0, HALF, w1_raw[3][:, 0:HALF])
-        scatter(2, 0, HALF, w1_raw[3][:, 0:HALF])
-        wd_bf = work.tile([P, PACK * N], BF16, name="bf", bufs=2, align_bytes=64)
+        def whole(u, sq, dst, tag):
+            square(u, 0, HALF, sq[:, 0:HALF], tag)
+            square(u, HALF, S, sq[:, HALF:S], tag)
+            root(u, 0, S, in_runs(sq))
+            respond(u, 0, S, dst)
+            scatter(u, 0, S, dst)
+            store_page(u)
+
+        whole(2, w1_raw[3][:], squares[:], "turn")
+        for c in range(CHUNKS):
+            turn_page(0, c, nc.scalar.copy)
+        whole(3, w1_raw[3][:], w1_raw[1][:], "acc")
+        for c in range(CHUNKS):
+            turn_page(1, c, nc.scalar.copy)
+        wd_bf = keep.tile([P, PACK * N], BF16, name="wd_bf", tag="w1_raw3", align_bytes=64)
         nc.scalar.activation(
             wd_bf[:].rearrange("p (c i j) -> p c j i", i=4, j=PACK),
             wd_raw[:].rearrange("p (j c i) -> p c j i", i=4, j=PACK),
             ACT.Copy,
             scale=2.0,
         )
-        wd_q = [quantise(wd_bf, "wd0", 0, P), quantise(wd_bf, "wd1", P, N)]
-        respond(2, HALF, S, wd_raw[:, 0:HALF])
-        scatter(2, HALF, S, wd_raw[:, 0:HALF])
-        store_page(2)
         for c in range(CHUNKS):
-            turn_page(0, c, nc.scalar.copy)
-
-        square(3, 0, HALF, squares_of(0, HALF))
-        square(3, HALF, S, squares_of(HALF, S))
-        root(3, 0, S, squares_of(0, S))
-        respond(3, 0, S, w1_raw[2][:])
-        scatter(3, 0, S, w1_raw[2][:])
-        store_page(3)
-        for u, c in ((2, 0), (2, 1), (2, 2), (1, 0), (1, 1), (1, 2), (1, 3), (2, 3)):
-            turn_page(u, c, nc.scalar.copy)
-        nc.scalar.activation(warm[:, 0:1], w1_raw[2][:, S - 1 : S], ACT.Sin, scale=0.0)
+            turn_page(2, c, nc.scalar.copy)
+        nc.scalar.activation(warm[:, 0:1], w1_raw[1][:, S - 1 : S], ACT.Sin, scale=0.0)
 
         words = keep.tile([P, T2], U32, name="words", align_bytes=64)
         scales = keep.tile([P, T2], U8, name="scales", align_bytes=64)
         words_dst = out_2[0].rearrange("p m t -> p (m t)").bitcast(I32)
 
         def turn_back(i, engine_copy):
-            bank = psum.tile([P, BANK], F32, name="turn", bufs=3)
+            bank = psum.tile([P, BANK], F32, name="value" if i < 3 else "turn", bufs=3)
             for k in range(BANK // P):
                 x0 = i * BANK + k * P
                 nc.tensor.transpose(bank[:, k * P : (k + 1) * P], turned_words[:, x0 : x0 + P], ident[:])
@@ -301,8 +293,8 @@ def tile_list_rod_checkpoint_kernel(
 
         def finish(half_cos, n, m0, m1, on_vector):
             value = psum.tile([P, m1 - m0], F32, name="value", bufs=3)
-            codes, bytes_ = wd_q[min(n, 1)]
-            cols = slice(max(n - 1, 0) * P, max(n, 1) * P)
+            codes, bytes_ = wd_q, wd_sc
+            cols = slice(n * P, (n + 1) * P)
             nc.tensor.matmul_mx(
                 out=value[:],
                 lhsT=codes[:, cols].bitcast(FP8X4),
@@ -321,16 +313,21 @@ def tile_list_rod_checkpoint_kernel(
             nc.vector.scalar_tensor_tensor(y[:], cos_up[:], -0.5, value[:], ALU.add, ALU.mult)
             nc.sync.dma_start(out_0[n * P : (n + 1) * P, m0:m1], y[:])
 
+        wd_q = keep.tile([P, N], U32, name="wd_q", tag="w1_raw1", align_bytes=64)
+        wd_sc = keep.tile([P, N], U8, name="wd_sc", align_bytes=64)
+        for n0, n1 in ((0, P), (P, N)):
+            nc.vector.quantize_mx(
+                out=wd_q[:, n0:n1].bitcast(FP8X4), scales=wd_sc[:, n0:n1], in_=wd_bf[:, n0 * PACK : n1 * PACK]
+            )
         last = TILES - 1
-        for i, engine_copy in enumerate((nc.vector.tensor_copy, nc.vector.tensor_copy)):
+        for i, engine_copy in enumerate((nc.vector.tensor_copy, nc.scalar.copy)):
             bank = psum.tile([P, PIECE], F32, name="turn", bufs=3)
             turn_columns(last, i * PIECE, (i + 1) * PIECE, bank, engine_copy)
         ready = [turn_back(0, nc.vector.tensor_copy), turn_back(1, nc.vector.tensor_copy)]
         quantise_page(ready[0], 0)
         quantise_page(ready[1], 1)
         for c in range(1, CHUNKS):
-            bank = psum.tile([P, BANK], F32, name="value", bufs=3)
-            turn_columns(last, c * BANK, (c + 1) * BANK, bank, nc.scalar.copy)
+            turn_page(last, c, nc.scalar.copy)
         ready = [turn_back(2, nc.scalar.copy), turn_back(3, nc.vector.tensor_copy)]
         quantise_page(ready[0], 2)
         quantise_page(ready[1], 3)
@@ -356,7 +353,7 @@ def tile_list_rod_checkpoint_kernel(
                 m0, m1 = whole
                 final = i + 1 == len(spans) and n + 1 == NT
                 for piece in ((m0, m1 - PIECE), (m1 - PIECE, m1)) if final else (whole,):
-                    now = (half_cosine(n, *piece), n, *piece, count % 4 == 3 and not final)
+                    now = (half_cosine(n, *piece), n, *piece, count in (7, 10, 12))
                     count = count + 1
                     if behind is not None:
                         finish(*behind)

@@ -2,7 +2,6 @@ import math
 from contextlib import ExitStack
 
 import concourse.mybir as mybir
-from concourse.masks import make_identity
 
 K, T, S, T2, H, N = 1024, 2048, 1024, 2048, 512, 384
 FLOPS = 2 * K * H * S + 2 * 2 * H * N * T2
@@ -21,6 +20,7 @@ ALU = mybir.AluOpType
 P = 128
 PACK = 4
 QUADS = 4
+QUAD = 32
 BANK = 512
 PASSES = K // (P * PACK)
 TILES = H // P
@@ -29,6 +29,7 @@ NT = N // P
 QUARTER = S // 4
 HALF = S // 2
 PIECE = BANK // 2
+W1_HALF = H // 2
 
 
 def tile_list_rod_checkpoint_kernel(
@@ -55,51 +56,89 @@ def tile_list_rod_checkpoint_kernel(
 
         wc_sc = keep.tile([P, N], U8, name="wc_sc", align_bytes=64)
         nc.vector.memset(wc_sc[:].bitcast(I32), 0)
-        ident = keep.tile([P, P], F32, name="ident")
-        make_identity(nc, ident[:])
 
         tab = [keep.tile([P, T], U32, name=f"tab{a}", align_bytes=64) for a in range(PASSES)]
-        w1_raw = [keep.tile([P, PASSES * PACK * P], F32, name=f"w1_raw{u}", align_bytes=64) for u in range(TILES)]
+        w1_raw = [
+            [keep.tile([P, PACK * W1_HALF], F32, name=f"w1_raw{g}{a}", align_bytes=64) for a in range(PASSES)]
+            for g in range(2)
+        ]
         w1_rows = w1.rearrange("(a p j) c -> a p j c", p=P, j=PACK)
         page = [keep.tile([P, T2], F32, name=f"page{u}") for u in range(TILES)]
         weights = keep.tile([P, S], F32, name="weights", align_bytes=64)
-        gains = keep.tile([P, 8], F32, name="gains")
-        wd_raw = keep.tile([P, PACK * N], F32, name="wd_raw")
+        late_factors = [keep.tile([P, S], F32, name=f"late_factor{e}", align_bytes=64) for e in range(2)]
+        rounded = [keep.tile([P, T2], BF16, name=f"rounded{g}", align_bytes=64) for g in range(2)]
+        third_weights = keep.tile([P, S], F32, name="third_weights", align_bytes=64)
+        late_weights = [third_weights[:], rounded[1][:].bitcast(F32)]
+        gains = [keep.tile([P, 8], F32, name=f"gains{g}") for g in range(2)]
+        late_gains = keep.tile([P, 8], F32, name="late_gains")
         wc = keep.tile([P, 2 * N], U8, name="wc", align_bytes=64)
+        slots = keep.tile([P, 3 * T2 + 2 * PACK * N], BF16, name="slots", align_bytes=64)
+        wd_raw = slots[:, 3 * T2 :].bitcast(F32)
+
+        def paired_rows(x):
+            return x.rearrange("(g c q f) m -> g c q f m", g=2, c=2, f=PACK)
+
+        def slot_rows(x):
+            return x.rearrange("(p t) m -> p t m", t=PACK)
 
         def load_tab(a):
             nc.sync.dma_start(tab[a][:].bitcast(I32), tab_words[a].rearrange("p t i -> p (t i)").bitcast(I32))
 
-        def load_w1(u):
+        def load_w1(g):
             for a in range(PASSES):
                 nc.sync.dma_start(
-                    w1_raw[u][:, a * PACK * P : (a + 1) * PACK * P].rearrange("p (j c) -> p j c", j=PACK),
-                    w1_rows[a][:, :, u * P : (u + 1) * P],
+                    w1_raw[g][a][:].rearrange("p (j c) -> p j c", j=PACK),
+                    w1_rows[a][:, :, g * W1_HALF : (g + 1) * W1_HALF],
                 )
 
         def load_page(u):
-            nc.sync.dma_start(page[u][:], page0[u * P : (u + 1) * P, :])
+            if u < 2:
+                for c in range(2):
+                    nc.sync.dma_start(page[u][c:P:2, :], paired_rows(page0)[u][c][:, 0:2, :])
+            else:
+                nc.sync.dma_start(page[u][:], slot_rows(page0)[:, u, :])
+
+        def store_page(u):
+            if u < 2:
+                for c in range(2):
+                    nc.sync.dma_start(paired_rows(out_1)[u][c][:, 0:2, :], page[u][c:P:2, :])
+            else:
+                nc.sync.dma_start(slot_rows(out_1)[:, u, :], page[u][:])
+
+        def load_gain(g):
+            rows = gain.rearrange("(g c q f o) -> g c q f o", g=2, c=2, f=PACK, o=1)
+            with nc.allow_non_contiguous_dma(reason="one gain for each partition"):
+                for c in range(2):
+                    nc.sync.dma_start(gains[g][c:P:2, 0:1], rows[g][c][:, 0:2, :])
+
+        wgs_rows = wgs.rearrange("(q f) s -> q f s", f=PACK)
+
+        def load_late_weights(u):
+            for c in range(QUADS):
+                nc.sync.dma_start(late_weights[u - 2][QUAD * c : QUAD * (c + 1), :], wgs_rows[:, u, :])
 
         nc.sync.dma_start(pick[:], offs)
+        load_tab(0)
         for q in range(QUADS):
             nc.sync.dma_start(
                 tab_sc[32 * q : 32 * q + 4 * PASSES, :].bitcast(I32),
                 tab_scales[:, 4 * q : 4 * q + 4, :].bitcast(I32),
             )
-        with nc.allow_non_contiguous_dma(reason="one gain for each partition and row tile"):
-            nc.sync.dma_start(gains[:, 0:TILES], gain.rearrange("(u p) -> p u", p=P))
-        nc.sync.dma_start(weights[:], wgs)
-        load_tab(0)
         load_w1(0)
         load_tab(1)
+        load_gain(0)
         nc.sync.dma_start(put[:], offs2)
+        for c in range(2):
+            nc.sync.dma_start(weights[c:P:2, :], wgs_rows[:, 0:2, :])
+        load_gain(1)
         load_page(0)
         load_w1(1)
-        load_w1(2)
-        load_w1(3)
+        nc.sync.dma_start(late_gains[:, 0:2], gain.rearrange("(p t) -> p t", t=PACK)[:, 2:4])
+        load_late_weights(2)
         load_page(1)
-        nc.sync.dma_start(wd_raw[:].rearrange("p (j n) -> p j n", j=PACK), wd.rearrange("(p j) n -> p j n", j=PACK))
+        load_late_weights(3)
         load_page(2)
+        nc.sync.dma_start(wd_raw.rearrange("p (j n) -> p j n", j=PACK), wd.rearrange("(p j) n -> p j n", j=PACK))
         load_page(3)
         nc.sync.dma_start(wc[:].bitcast(I32), wc_words[0].bitcast(I32))
         for q in range(QUADS):
@@ -111,52 +150,57 @@ def tile_list_rod_checkpoint_kernel(
         def entries(lst, j0, j1):
             return lst[:] if (j0, j1) == (0, S) else lst[:, j0 // 16 : j1 // 16]
 
-        def interleave(raw, width):
-            bf = work.tile([P, raw.shape[1]], BF16, name="bf", bufs=2, align_bytes=64)
-            nc.scalar.copy(
-                bf[:].rearrange("p (a c i j) -> p a c j i", i=4, j=PACK, c=width // 4),
-                raw.rearrange("p (a j c i) -> p a c j i", i=4, j=PACK, c=width // 4),
-            )
-            return bf
+        paired_bf = [keep.tile([P, PASSES * P * PACK], BF16, name=f"paired_bf{g}", align_bytes=64) for g in range(2)]
+        late_bf = keep.tile([P, 2 * PASSES * P * PACK], BF16, name="late_bf", align_bytes=64)
 
-        def quantise(bf, name, tag):
-            codes = keep.tile([P, PASSES * P], U32, name=f"{name}_q", tag=tag, align_bytes=64)
-            bytes_ = keep.tile([P, PASSES * P], U8, name=f"{name}_sc", align_bytes=64)
+        def round_paired(g, a):
+            nc.scalar.copy(
+                paired_bf[g][:, a * P * PACK : (a + 1) * P * PACK].rearrange(
+                    "p (q e c j) -> p q c j e", e=2, c=2, j=PACK
+                ),
+                w1_raw[g][a][:].rearrange("p (j c q f) -> p q c j f", j=PACK, c=2, f=PACK)[:, :, :, :, 0:2],
+            )
+
+        def round_late(g, a):
+            nc.scalar.copy(
+                late_bf[:].rearrange("p (e a g r j) -> p a g r j e", e=2, a=PASSES, g=2, j=PACK)[:, a, g],
+                w1_raw[g][a][:].rearrange("p (j r f) -> p r j f", j=PACK, f=PACK)[:, :, :, 2:4],
+            )
+
+        def quantise(bf, name, tag=None):
+            width = bf.shape[1] // PACK
+            codes = keep.tile([P, width], U32, name=f"{name}_q", tag=tag or f"{name}_q", align_bytes=64)
+            bytes_ = keep.tile([P, width], U8, name=f"{name}_sc", align_bytes=64)
             nc.vector.quantize_mx(out=codes[:].bitcast(FP8X4), scales=bytes_[:], in_=bf[:])
             return codes, bytes_
 
         v = [keep.tile([P, S], U32, name=f"v{a}", align_bytes=64) for a in range(PASSES)]
         v_sc = keep.tile([P, S], U8, name="v_sc", align_bytes=64)
-        nc.vector.tensor_copy(v_sc[:], tab_sc[:].indirect(pick[:]))
         nc.vector.tensor_copy(v[0][:], tab[0][:].indirect(pick[:]))
-        factors = [keep.tile([P, S], F32, name=f"factor{u}", align_bytes=64) for u in range(TILES - 1)]
-        factors.append(w1_raw[0])
-
-        def weigh(u):
-            nc.scalar.activation(factors[u][:], weights[:], ACT.Copy, scale=gains[:, u : u + 1])
-
-        for u in range(TILES - 1):
-            weigh(u)
-        w1_q = [quantise(interleave(w1_raw[0][:], P), "w1_0", "w1_0_q")]
-        weigh(TILES - 1)
+        nc.vector.tensor_copy(v_sc[:], tab_sc[:].indirect(pick[:]))
+        for a in range(PASSES):
+            round_paired(0, a)
+        codes, bytes_ = quantise(paired_bf[0], "w1_0")
+        w1_q = [(codes[:], bytes_[:])]
         for j0, j1 in ((0, QUARTER), (QUARTER, HALF), (HALF, S)):
             nc.vector.tensor_copy(v[1][:, j0:j1], tab[1][:].indirect(entries(pick, j0, j1)))
+        early_factors = keep.tile([P, 2 * S], F32, name="early_factors", align_bytes=64)
+        for u in range(2):
+            nc.vector.tensor_scalar(
+                early_factors[:, u * S : (u + 1) * S], weights[:], gains[u][:, 0:1], None, ALU.mult
+            )
+        factors = [early_factors[:, 0:S], early_factors[:, S:], late_factors[0][:], late_factors[1][:]]
 
-        turned = keep.tile([P, T2 * PACK], BF16, name="turned", align_bytes=64)
-        turned_words = turned[:].bitcast(F32)
+
         squares = keep.tile([P, S], F32, name="squares", align_bytes=64)
-        rows = turned_words.rearrange("p (a x) -> p a x", x=P)
-        roots_at = [3, 3, 0, 2]
+        roots = keep.tile([P, S], F32, name="roots", align_bytes=64)
+        resp = [keep.tile([P, S], F32, name=f"resp{u}", align_bytes=64) for u in range(TILES)]
 
-        def in_runs(ap):
-            return ap.rearrange("p (a b) -> p a b", a=32)
+        def slot(t, m0=0, m1=T2):
+            return slots[:, t * T2 + m0 : t * T2 + m1]
 
-        def roots_of(u, j0, j1):
-            at = 32 * roots_at[u]
-            return rows[:, :, at + j0 // 32 : at + j1 // 32]
-
-        def square(u, j0, j1, dst, tag="acc"):
-            acc = psum.tile([P, j1 - j0], F32, name=tag, bufs=2 if tag == "acc" else 3)
+        def square(u, j0, j1):
+            acc = psum.tile([P, j1 - j0], F32, name="phase", bufs=4)
             codes, bytes_ = w1_q[u]
             for a in range(PASSES):
                 nc.tensor.matmul_mx(
@@ -168,116 +212,99 @@ def tile_list_rod_checkpoint_kernel(
                     start=(a == 0),
                     stop=(a == PASSES - 1),
                 )
-            nc.scalar.activation(dst, acc[:] if dst.ndim == 2 else in_runs(acc[:]), ACT.Square)
+            nc.scalar.activation(squares[:, j0:j1], acc[:], ACT.Square)
 
-        def root(u, j0, j1, src):
-            nc.scalar.activation(roots_of(u, j0, j1), src, ACT.Abs_reciprocal_sqrt, bias=1.0)
+        def respond(u, spans, root_at, resp_at):
+            for span in spans:
+                square(u, *span)
+            for (j0, j1), dst in zip(spans, root_at):
+                nc.scalar.activation(dst, squares[:, j0:j1], ACT.Abs_reciprocal_sqrt, bias=1.0)
+            for src, dst in zip(root_at, resp_at):
+                nc.scalar.activation(dst, src, ACT.Square)
 
-        def respond(u, j0, j1, dst):
-            nc.scalar.activation(in_runs(dst), roots_of(u, j0, j1), ACT.Square)
+        def scatter(u, j0, j1, src):
+            nc.vector.tensor_tensor(page[u][:].indirect(entries(put, j0, j1)), src, factors[u][:, j0:j1], ALU.mult)
 
-        def scatter(u, j0, j1, resp):
-            nc.vector.tensor_tensor(page[u][:].indirect(entries(put, j0, j1)), resp, factors[u][:, j0:j1], ALU.mult)
-
-        def turn_columns(u, m0, m1, bank, engine_copy):
-            for m in range(m0, m1, P):
-                nc.tensor.transpose(bank[:, m - m0 : m - m0 + P], page[u][:, m : m + P], ident[:])
-            dst = turned[:, m0 * PACK : m1 * PACK].rearrange("p (b h g q e) -> p b h g q e", h=2, g=TILES, q=32, e=2)
-            engine_copy(dst[:, :, :, u, :, :], bank[:].rearrange("p (b q h e) -> p b h q e", q=32, h=2, e=2))
-
-        def turn_page(u, c, engine_copy):
-            bank = psum.tile([P, BANK], F32, name="turn", bufs=3)
-            turn_columns(u, c * BANK, (c + 1) * BANK, bank, engine_copy)
-
-        def store_page(u):
-            nc.sync.dma_start(out_1[u * P : (u + 1) * P, :], page[u][:])
-
-        def squares_of(j0, j1):
-            return in_runs(squares[:, j0:j1])
-
-        def round_w1(u):
-            return interleave(w1_raw[u][:], P)
-
-        resp = keep.tile([P, S], F32, name="resp", align_bytes=64)
+        def round_and_move(g):
+            nc.scalar.copy(rounded[g][:], page[g][:])
+            for c in range(2):
+                for e in range(2):
+                    p0 = 2 * QUAD * g + QUAD * c
+                    nc.sync.dma_start(slot(e)[p0 : p0 + QUAD, :], rounded[g][2 * e + c : P : 4, :])
 
         quarters = [(0, QUARTER), (QUARTER, HALF)]
-        for span in quarters:
-            square(0, *span, squares_of(*span))
-        for span in quarters:
-            root(0, *span, squares_of(*span))
-        for j0, j1 in quarters:
-            respond(0, j0, j1, resp[:, j0:j1])
-        scatter(0, 0, HALF, resp[:, 0:HALF])
-        square(0, HALF, S, roots_of(0, 0, HALF))
-        w1_q.append(quantise(round_w1(1), "w1_1", "w1_1_q"))
-        root(0, HALF, S, roots_of(0, 0, HALF))
-        respond(0, HALF, S, w1_raw[1][:, 0:HALF])
-        scatter(0, HALF, S, w1_raw[1][:, 0:HALF])
+        halves = [(0, HALF), (HALF, S)]
+
+        respond(0, quarters, [roots[:, a:b] for a, b in quarters], [resp[0][:, a:b] for a, b in quarters])
+        scatter(0, 0, HALF, resp[0][:, 0:HALF])
+        for a in range(PASSES):
+            round_late(0, a)
+        for a in range(PASSES):
+            round_paired(1, a)
+            round_late(1, a)
+        codes, bytes_ = quantise(paired_bf[1], "w1_1")
+        w1_q.append((codes[:], bytes_[:]))
+        codes, bytes_ = quantise(late_bf, "w1_late")
+        for e in range(2):
+            cols = slice(e * PASSES * P, (e + 1) * PASSES * P)
+            w1_q.append((codes[:, cols], bytes_[:, cols]))
+        spent = w1_raw[1][1][:, 0:HALF]
+        respond(0, [(HALF, S)], [roots[:, HALF:S]], [spent])
+        scatter(0, HALF, S, spent)
         store_page(0)
 
-        w1_q.append(quantise(round_w1(2), "w1_2", "w1_2_q"))
-        bf3 = round_w1(3)
-        square(1, 0, QUARTER, squares_of(0, QUARTER))
-        root(1, 0, QUARTER, squares_of(0, QUARTER))
-        respond(1, 0, QUARTER, w1_raw[2][:, 0:QUARTER])
-        scatter(1, 0, QUARTER, w1_raw[2][:, 0:QUARTER])
-        w1_q.append(quantise(bf3, "w1_3", "w1_raw2"))
-        square(1, QUARTER, HALF, squares_of(QUARTER, HALF))
-        square(1, HALF, S, squares_of(HALF, S), "value")
-        root(1, QUARTER, S, squares_of(QUARTER, S))
-        respond(1, QUARTER, S, resp[:, QUARTER:S])
-        scatter(1, QUARTER, S, resp[:, QUARTER:S])
+        held = [rounded[0][:].bitcast(F32), rounded[1][:].bitcast(F32), slot(2).bitcast(F32)]
+        first = factors[2][:, 0:QUARTER]
+        respond(1, [(0, QUARTER)], [held[0][:, 0:QUARTER]], [first])
+        scatter(1, 0, QUARTER, first)
+        nc.vector.tensor_scalar(factors[2], late_weights[0], late_gains[:, 0:1], None, ALU.mult)
+        square(1, QUARTER, HALF)
+        square(1, HALF, S)
+        nc.scalar.activation(held[0][:, QUARTER:S], squares[:, QUARTER:S], ACT.Abs_reciprocal_sqrt, bias=1.0)
+        nc.scalar.activation(resp[1][:, QUARTER:S], held[0][:, QUARTER:S], ACT.Square)
+        scatter(1, QUARTER, S, resp[1][:, QUARTER:S])
+        round_and_move(0)
         store_page(1)
 
-        def whole(u, sq, dst, tag):
-            square(u, 0, HALF, sq[:, 0:HALF], tag)
-            square(u, HALF, S, sq[:, HALF:S], tag)
-            root(u, 0, S, in_runs(sq))
-            respond(u, 0, S, dst)
-            scatter(u, 0, S, dst)
-            store_page(u)
+        respond(2, halves, [factors[3][:, a:b] for a, b in halves], [resp[2][:, a:b] for a, b in halves])
+        nc.scalar.activation(factors[3], late_weights[1], ACT.Copy, scale=late_gains[:, 1:2])
+        scatter(2, 0, S, resp[2][:])
+        round_and_move(1)
+        store_page(2)
 
-        whole(2, w1_raw[3][:], squares[:], "turn")
-        for c in range(CHUNKS):
-            turn_page(0, c, nc.scalar.copy)
-        whole(3, w1_raw[3][:], w1_raw[1][:], "acc")
-        for c in range(CHUNKS):
-            turn_page(1, c, nc.scalar.copy)
-        wd_bf = keep.tile([P, PACK * N], BF16, name="wd_bf", tag="w1_raw3", align_bytes=64)
+        wd_bf = keep.tile([P, PACK * N], BF16, name="wd_bf", align_bytes=64)
+        respond(3, halves, [wd_bf[:].bitcast(F32)[:, 0:HALF], held[2][:, 0:HALF]], [resp[3][:, a:b] for a, b in halves])
+        scatter(3, 0, S, resp[3][:])
+        nc.scalar.activation(warm[:, 0:1], resp[3][:, S - 1 : S], ACT.Sin, scale=0.0)
+        nc.scalar.copy(slot(2), page[2][:])
         nc.scalar.activation(
             wd_bf[:].rearrange("p (c i j) -> p c j i", i=4, j=PACK),
-            wd_raw[:].rearrange("p (j c i) -> p c j i", i=4, j=PACK),
+            wd_raw.rearrange("p (j c i) -> p c j i", i=4, j=PACK),
             ACT.Copy,
             scale=2.0,
         )
-        for c in range(CHUNKS):
-            turn_page(2, c, nc.scalar.copy)
-        nc.scalar.activation(warm[:, 0:1], w1_raw[1][:, S - 1 : S], ACT.Sin, scale=0.0)
+        store_page(3)
 
         words = keep.tile([P, T2], U32, name="words", align_bytes=64)
         scales = keep.tile([P, T2], U8, name="scales", align_bytes=64)
         words_dst = out_2[0].rearrange("p m t -> p (m t)").bitcast(I32)
+        slot_view = slots[:, 0 : PACK * T2].rearrange("p (t m) -> p t m", t=PACK)
 
-        def turn_back(i, engine_copy):
-            bank = psum.tile([P, BANK], F32, name="value" if i < 3 else "turn", bufs=3)
-            for k in range(BANK // P):
-                x0 = i * BANK + k * P
-                nc.tensor.transpose(bank[:, k * P : (k + 1) * P], turned_words[:, x0 : x0 + P], ident[:])
-            grouped = work.tile([P, PIECE * PACK], BF16, name="grouped", bufs=4, align_bytes=64)
-            engine_copy(
-                grouped[:].bitcast(F32).rearrange("p (b c h) -> p b c h", b=2, h=2),
-                bank[:].rearrange("p (b h c) -> p b c h", b=2, h=2),
+        def regroup(m0, m1):
+            grouped = work.tile([P, (m1 - m0) * PACK], BF16, name="grouped", bufs=3, align_bytes=64)
+            nc.vector.tensor_copy(
+                grouped[:].rearrange("p (c i t) -> p c t i", i=4, t=PACK),
+                slot_view[:, :, m0:m1].rearrange("p t (c i) -> p c t i", i=4),
             )
             return grouped
 
-        def quantise_page(grouped, i):
-            m0, m1 = i * PIECE, (i + 1) * PIECE
+        def quantise_page(grouped, m0, m1):
             nc.vector.quantize_mx(out=words[:, m0:m1].bitcast(FP8X4), scales=scales[:, m0:m1], in_=grouped[:])
-            if i % 2 == 1:
-                nc.sync.dma_start(words_dst[:, m0 - PIECE : m1], words[:, m0 - PIECE : m1].bitcast(I32))
+            if m1 % BANK == 0:
+                nc.sync.dma_start(words_dst[:, m1 - BANK : m1], words[:, m1 - BANK : m1].bitcast(I32))
 
         def half_cosine(n, m0, m1):
-            phase = psum.tile([P, m1 - m0], F32, name="phase", tag="acc", bufs=2)
+            phase = psum.tile([P, m1 - m0], F32, name="phase", bufs=4)
             nc.tensor.matmul_mx(
                 out=phase[:],
                 lhsT=wc[:, 2 * n * P : 2 * (n + 1) * P].bitcast(FP4X4),
@@ -292,13 +319,12 @@ def tile_list_rod_checkpoint_kernel(
             return half_cos
 
         def finish(half_cos, n, m0, m1, on_vector):
-            value = psum.tile([P, m1 - m0], F32, name="value", bufs=3)
-            codes, bytes_ = wd_q, wd_sc
+            value = psum.tile([P, m1 - m0], F32, name="value", bufs=4)
             cols = slice(n * P, (n + 1) * P)
             nc.tensor.matmul_mx(
                 out=value[:],
-                lhsT=codes[:, cols].bitcast(FP8X4),
-                lhsT_scale=bytes_[:, cols],
+                lhsT=wd_q[:, cols].bitcast(FP8X4),
+                lhsT_scale=wd_sc[:, cols],
                 rhs=words[:, m0:m1].bitcast(FP8X4),
                 rhs_scale=scales[:, m0:m1],
                 start=True,
@@ -313,36 +339,23 @@ def tile_list_rod_checkpoint_kernel(
             nc.vector.scalar_tensor_tensor(y[:], cos_up[:], -0.5, value[:], ALU.add, ALU.mult)
             nc.sync.dma_start(out_0[n * P : (n + 1) * P, m0:m1], y[:])
 
-        wd_q = keep.tile([P, N], U32, name="wd_q", tag="w1_raw1", align_bytes=64)
+        wd_q = keep.tile([P, N], U32, name="wd_q", tag="resp3", align_bytes=64)
         wd_sc = keep.tile([P, N], U8, name="wd_sc", align_bytes=64)
         for n0, n1 in ((0, P), (P, N)):
             nc.vector.quantize_mx(
                 out=wd_q[:, n0:n1].bitcast(FP8X4), scales=wd_sc[:, n0:n1], in_=wd_bf[:, n0 * PACK : n1 * PACK]
             )
-        last = TILES - 1
-        for i, engine_copy in enumerate((nc.vector.tensor_copy, nc.scalar.copy)):
-            bank = psum.tile([P, PIECE], F32, name="turn", bufs=3)
-            turn_columns(last, i * PIECE, (i + 1) * PIECE, bank, engine_copy)
-        ready = [turn_back(0, nc.vector.tensor_copy), turn_back(1, nc.vector.tensor_copy)]
-        quantise_page(ready[0], 0)
-        quantise_page(ready[1], 1)
-        for c in range(1, CHUNKS):
-            turn_page(last, c, nc.scalar.copy)
-        ready = [turn_back(2, nc.scalar.copy), turn_back(3, nc.vector.tensor_copy)]
-        quantise_page(ready[0], 2)
-        quantise_page(ready[1], 3)
-
         spans = [(0, PIECE), (PIECE, BANK)] + [(c * BANK, (c + 1) * BANK) for c in range(1, CHUNKS)]
+        for m0, m1 in spans:
+            nc.scalar.copy(slot(3, m0, m1), page[3][:, m0:m1])
+        for span in spans[0:3]:
+            quantise_page(regroup(*span), *span)
+
         behind = None
         count = 0
         for i, whole in enumerate(spans):
             if 1 <= i <= 2:
-                pair = [
-                    turn_back(2 * i + 2, nc.scalar.copy if i == 1 else nc.vector.tensor_copy),
-                    turn_back(2 * i + 3, nc.vector.tensor_copy),
-                ]
-                quantise_page(pair[0], 2 * i + 2)
-                quantise_page(pair[1], 2 * i + 3)
+                quantise_page(regroup(*spans[i + 2]), *spans[i + 2])
             if i == 2:
                 for q in range(QUADS):
                     nc.sync.dma_start(
@@ -353,7 +366,7 @@ def tile_list_rod_checkpoint_kernel(
                 m0, m1 = whole
                 final = i + 1 == len(spans) and n + 1 == NT
                 for piece in ((m0, m1 - PIECE), (m1 - PIECE, m1)) if final else (whole,):
-                    now = (half_cosine(n, *piece), n, *piece, count in (7, 10, 12))
+                    now = (half_cosine(n, *piece), n, *piece, count in (11, 13))
                     count = count + 1
                     if behind is not None:
                         finish(*behind)

@@ -81,8 +81,10 @@ def tile_list_rod_checkpoint_kernel(
         def slot_rows(x):
             return x.rearrange("(p t) m -> p t m", t=PACK)
 
-        def load_tab(a):
-            nc.sync.dma_start(tab[a][:].bitcast(I32), tab_words[a].rearrange("p t i -> p (t i)").bitcast(I32))
+        def load_tab(a, cuts=(0, T)):
+            words_in = tab_words[a].rearrange("p t i -> p (t i)").bitcast(I32)
+            for t0, t1 in zip(cuts, cuts[1:]):
+                nc.sync.dma_start(tab[a][:, t0:t1].bitcast(I32), words_in[:, t0:t1])
 
         def load_w1(g):
             for a in range(PASSES):
@@ -118,7 +120,7 @@ def tile_list_rod_checkpoint_kernel(
                 nc.sync.dma_start(late_weights[u - 2][QUAD * c : QUAD * (c + 1), :], wgs_rows[:, u, :])
 
         nc.sync.dma_start(pick[:], offs)
-        load_tab(0)
+        load_tab(0, (0, 768, 1408, T))
         for q in range(QUADS):
             nc.sync.dma_start(
                 tab_sc[32 * q : 32 * q + 4 * PASSES, :].bitcast(I32),

@@ -30,6 +30,7 @@ QUARTER = S // 4
 HALF = S // 2
 PIECE = BANK // 2
 W1_HALF = H // 2
+ON_GPSIMD = (8, 10, 12)
 
 
 def tile_list_rod_checkpoint_kernel(
@@ -277,7 +278,7 @@ def tile_list_rod_checkpoint_kernel(
         wd_bf = keep.tile([P, PACK * N], BF16, name="wd_bf", align_bytes=64)
         respond(3, halves, [wd_bf[:].bitcast(F32)[:, 0:HALF], held[2][:, 0:HALF]], [resp[3][:, a:b] for a, b in halves])
         scatter(3, 0, S, resp[3][:])
-        nc.scalar.activation(warm[:, 0:1], resp[3][:, S - 1 : S], ACT.Sin, scale=0.0)
+        nc.scalar.activation(warm[:, 0:1], rounded[1][:, T2 - 1 : T2], ACT.Sin, scale=0.0, bias=resp[3][:, S - 1 : S])
         nc.scalar.copy(slot(2), page[2][:])
         nc.scalar.activation(
             wd_bf[:].rearrange("p (c i j) -> p c j i", i=4, j=PACK),
@@ -320,7 +321,7 @@ def tile_list_rod_checkpoint_kernel(
             nc.scalar.activation(half_cos[:], phase[:], ACT.Sin, scale=0.5, bias=math.pi / 2)
             return half_cos
 
-        def finish(half_cos, n, m0, m1, on_vector):
+        def finish(half_cos, n, m0, m1, spent):
             value = psum.tile([P, m1 - m0], F32, name="value", bufs=4)
             cols = slice(n * P, (n + 1) * P)
             nc.tensor.matmul_mx(
@@ -332,13 +333,15 @@ def tile_list_rod_checkpoint_kernel(
                 start=True,
                 stop=True,
             )
-            cos_up = work.tile([P, m1 - m0], F32, name="cos_up", bufs=4)
-            if on_vector:
-                nc.vector.tensor_tensor(cos_up[:], half_cos[:], half_cos[:], ALU.mult)
+            if spent is None:
+                cos_tile = work.tile([P, m1 - m0], F32, name="cos_up", bufs=4)
+                cos_up = cos_tile[:]
+                nc.scalar.activation(cos_up, half_cos[:], ACT.Square)
             else:
-                nc.scalar.activation(cos_up[:], half_cos[:], ACT.Square)
+                cos_up = spent
+                nc.gpsimd.tensor_tensor(cos_up, half_cos[:], half_cos[:], ALU.mult)
             y = work.tile([P, m1 - m0], F32, name="y", bufs=8)
-            nc.vector.scalar_tensor_tensor(y[:], cos_up[:], -0.5, value[:], ALU.add, ALU.mult)
+            nc.vector.scalar_tensor_tensor(y[:], cos_up, -0.5, value[:], ALU.add, ALU.mult)
             nc.sync.dma_start(out_0[n * P : (n + 1) * P, m0:m1], y[:])
 
         wd_q = keep.tile([P, N], U32, name="wd_q", tag="resp3", align_bytes=64)
@@ -357,7 +360,8 @@ def tile_list_rod_checkpoint_kernel(
         count = 0
         for i, whole in enumerate(spans):
             if 1 <= i <= 2:
-                quantise_page(regroup(*spans[i + 2]), *spans[i + 2])
+                last_grouped = regroup(*spans[i + 2])
+                quantise_page(last_grouped, *spans[i + 2])
             if i == 2:
                 for q in range(QUADS):
                     nc.sync.dma_start(
@@ -368,7 +372,11 @@ def tile_list_rod_checkpoint_kernel(
                 m0, m1 = whole
                 final = i + 1 == len(spans) and n + 1 == NT
                 for piece in ((m0, m1 - PIECE), (m1 - PIECE, m1)) if final else (whole,):
-                    now = (half_cosine(n, *piece), n, *piece, count in (11, 13))
+                    spent = None
+                    if count in ON_GPSIMD:
+                        at = ON_GPSIMD.index(count) % 2 * BANK
+                        spent = last_grouped[:].bitcast(F32)[:, at : at + BANK]
+                    now = (half_cosine(n, *piece), n, *piece, spent)
                     count = count + 1
                     if behind is not None:
                         finish(*behind)

@@ -189,8 +189,8 @@ def tile_list_rod_checkpoint_kernel(
             nc.vector.tensor_copy(v[1][:, j0:j1], tab[1][:].indirect(entries(pick, j0, j1)))
         early_factors = keep.tile([P, 2 * S], F32, name="early_factors", align_bytes=64)
         for u in range(2):
-            nc.vector.tensor_scalar(
-                early_factors[:, u * S : (u + 1) * S], weights[:], gains[u][:, 0:1], None, ALU.mult
+            nc.gpsimd.tensor_scalar(
+                early_factors[:, u * S : (u + 1) * S], weights[:], gains[u][:, 0:1], -0.0, ALU.mult, ALU.add
             )
         factors = [early_factors[:, 0:S], early_factors[:, S:], late_factors[0][:], late_factors[1][:]]
 
@@ -278,7 +278,7 @@ def tile_list_rod_checkpoint_kernel(
         wd_bf = keep.tile([P, PACK * N], BF16, name="wd_bf", align_bytes=64)
         respond(3, halves, [wd_bf[:].bitcast(F32)[:, 0:HALF], held[2][:, 0:HALF]], [resp[3][:, a:b] for a, b in halves])
         scatter(3, 0, S, resp[3][:])
-        nc.scalar.activation(warm[:, 0:1], rounded[1][:, T2 - 1 : T2], ACT.Sin, scale=0.0, bias=resp[3][:, S - 1 : S])
+        nc.scalar.activation(squares[:, S - 1 : S], one[:, 0:1], ACT.Sin)
         nc.scalar.copy(slot(2), page[2][:])
         nc.scalar.activation(
             wd_bf[:].rearrange("p (c i j) -> p c j i", i=4, j=PACK),

@@ -47,7 +47,7 @@ def tile_list_rod_checkpoint_kernel(
         pick = lists.tile([P, S // 16], U16, name="pick")
         put = lists.tile([P, S // 16], U16, name="put")
 
-        tab_sc = keep.tile([P, T], U8, name="tab_sc", align_bytes=64)
+        tab_sc = keep.tile([P, T], U8, name="tab_sc", align_bytes=256)
         nc.gpsimd.memset(tab_sc[:].bitcast(I32), 0)
 
         one = keep.tile([P, 8], F32, name="one")
@@ -55,25 +55,25 @@ def tile_list_rod_checkpoint_kernel(
         nc.vector.memset(one[:], 1.0)
         nc.scalar.activation(warm[:], one[:], ACT.Abs_reciprocal_sqrt)
 
-        wc_sc = keep.tile([P, N], U8, name="wc_sc", align_bytes=64)
+        wc_sc = keep.tile([P, N], U8, name="wc_sc", align_bytes=256)
         nc.vector.memset(wc_sc[:].bitcast(I32), 0)
 
-        tab = [keep.tile([P, T], U32, name=f"tab{a}", align_bytes=64) for a in range(PASSES)]
+        tab = [keep.tile([P, T], U32, name=f"tab{a}", align_bytes=256) for a in range(PASSES)]
         w1_raw = [
-            [keep.tile([P, PACK * W1_HALF], F32, name=f"w1_raw{g}{a}", align_bytes=64) for a in range(PASSES)]
+            [keep.tile([P, PACK * W1_HALF], F32, name=f"w1_raw{g}{a}", align_bytes=256) for a in range(PASSES)]
             for g in range(2)
         ]
         w1_rows = w1.rearrange("(a p j) c -> a p j c", p=P, j=PACK)
-        page = [keep.tile([P, T2], F32, name=f"page{u}") for u in range(TILES)]
-        weights = keep.tile([P, S], F32, name="weights", align_bytes=64)
-        late_factors = [keep.tile([P, S], F32, name=f"late_factor{e}", align_bytes=64) for e in range(2)]
-        rounded = [keep.tile([P, T2], BF16, name=f"rounded{g}", align_bytes=64) for g in range(2)]
-        third_weights = keep.tile([P, S], F32, name="third_weights", align_bytes=64)
+        page = [keep.tile([P, T2], F32, name=f"page{u}", align_bytes=256) for u in range(TILES)]
+        weights = keep.tile([P, S], F32, name="weights", align_bytes=256)
+        late_factors = [keep.tile([P, S], F32, name=f"late_factor{e}", align_bytes=256) for e in range(2)]
+        rounded = [keep.tile([P, T2], BF16, name=f"rounded{g}", align_bytes=256) for g in range(2)]
+        third_weights = keep.tile([P, S], F32, name="third_weights", align_bytes=256)
         late_weights = [third_weights[:], rounded[1][:].bitcast(F32)]
         gains = [keep.tile([P, 8], F32, name=f"gains{g}") for g in range(2)]
         late_gains = keep.tile([P, 8], F32, name="late_gains")
-        wc = keep.tile([P, 2 * N], U8, name="wc", align_bytes=64)
-        slots = keep.tile([P, 3 * T2 + 2 * PACK * N], BF16, name="slots", align_bytes=64)
+        wc = keep.tile([P, 2 * N], U8, name="wc", align_bytes=256)
+        slots = keep.tile([P, 3 * T2 + 2 * PACK * N], BF16, name="slots", align_bytes=256)
         wd_raw = slots[:, 3 * T2 :].bitcast(F32)
 
         def paired_rows(x):
@@ -153,8 +153,8 @@ def tile_list_rod_checkpoint_kernel(
         def entries(lst, j0, j1):
             return lst[:] if (j0, j1) == (0, S) else lst[:, j0 // 16 : j1 // 16]
 
-        paired_bf = [keep.tile([P, PASSES * P * PACK], BF16, name=f"paired_bf{g}", align_bytes=64) for g in range(2)]
-        late_bf = keep.tile([P, 2 * PASSES * P * PACK], BF16, name="late_bf", align_bytes=64)
+        paired_bf = [keep.tile([P, PASSES * P * PACK], BF16, name=f"paired_bf{g}", align_bytes=256) for g in range(2)]
+        late_bf = keep.tile([P, 2 * PASSES * P * PACK], BF16, name="late_bf", align_bytes=256)
 
         def round_paired(g, a):
             nc.scalar.copy(
@@ -172,13 +172,13 @@ def tile_list_rod_checkpoint_kernel(
 
         def quantise(bf, name, tag=None):
             width = bf.shape[1] // PACK
-            codes = keep.tile([P, width], U32, name=f"{name}_q", tag=tag or f"{name}_q", align_bytes=64)
-            bytes_ = keep.tile([P, width], U8, name=f"{name}_sc", align_bytes=64)
+            codes = keep.tile([P, width], U32, name=f"{name}_q", tag=tag or f"{name}_q", align_bytes=256)
+            bytes_ = keep.tile([P, width], U8, name=f"{name}_sc", align_bytes=256)
             nc.vector.quantize_mx(out=codes[:].bitcast(FP8X4), scales=bytes_[:], in_=bf[:])
             return codes, bytes_
 
-        v = [keep.tile([P, S], U32, name=f"v{a}", align_bytes=64) for a in range(PASSES)]
-        v_sc = keep.tile([P, S], U8, name="v_sc", align_bytes=64)
+        v = [keep.tile([P, S], U32, name=f"v{a}", align_bytes=256) for a in range(PASSES)]
+        v_sc = keep.tile([P, S], U8, name="v_sc", align_bytes=256)
         nc.vector.tensor_copy(v[0][:], tab[0][:].indirect(pick[:]))
         nc.vector.tensor_copy(v_sc[:], tab_sc[:].indirect(pick[:]))
         for a in range(PASSES):
@@ -187,7 +187,7 @@ def tile_list_rod_checkpoint_kernel(
         w1_q = [(codes[:], bytes_[:])]
         for j0, j1 in ((0, QUARTER), (QUARTER, HALF), (HALF, S)):
             nc.vector.tensor_copy(v[1][:, j0:j1], tab[1][:].indirect(entries(pick, j0, j1)))
-        early_factors = keep.tile([P, 2 * S], F32, name="early_factors", align_bytes=64)
+        early_factors = keep.tile([P, 2 * S], F32, name="early_factors", align_bytes=256)
         for u in range(2):
             nc.gpsimd.tensor_scalar(
                 early_factors[:, u * S : (u + 1) * S], weights[:], gains[u][:, 0:1], -0.0, ALU.mult, ALU.add
@@ -195,9 +195,9 @@ def tile_list_rod_checkpoint_kernel(
         factors = [early_factors[:, 0:S], early_factors[:, S:], late_factors[0][:], late_factors[1][:]]
 
 
-        squares = keep.tile([P, S], F32, name="squares", align_bytes=64)
-        roots = keep.tile([P, S], F32, name="roots", align_bytes=64)
-        resp = [keep.tile([P, S], F32, name=f"resp{u}", align_bytes=64) for u in range(TILES)]
+        squares = keep.tile([P, S], F32, name="squares", align_bytes=256)
+        roots = keep.tile([P, S], F32, name="roots", align_bytes=256)
+        resp = [keep.tile([P, S], F32, name=f"resp{u}", align_bytes=256) for u in range(TILES)]
 
         def slot(t, m0=0, m1=T2):
             return slots[:, t * T2 + m0 : t * T2 + m1]
@@ -275,7 +275,7 @@ def tile_list_rod_checkpoint_kernel(
         round_and_move(1)
         store_page(2)
 
-        wd_bf = keep.tile([P, PACK * N], BF16, name="wd_bf", align_bytes=64)
+        wd_bf = keep.tile([P, PACK * N], BF16, name="wd_bf", align_bytes=256)
         respond(3, halves, [wd_bf[:].bitcast(F32)[:, 0:HALF], held[2][:, 0:HALF]], [resp[3][:, a:b] for a, b in halves])
         scatter(3, 0, S, resp[3][:])
         nc.scalar.activation(squares[:, S - 1 : S], one[:, 0:1], ACT.Sin)
@@ -288,13 +288,13 @@ def tile_list_rod_checkpoint_kernel(
         )
         store_page(3)
 
-        words = keep.tile([P, T2], U32, name="words", align_bytes=64)
-        scales = keep.tile([P, T2], U8, name="scales", align_bytes=64)
+        words = keep.tile([P, T2], U32, name="words", align_bytes=256)
+        scales = keep.tile([P, T2], U8, name="scales", align_bytes=256)
         words_dst = out_2[0].rearrange("p m t -> p (m t)").bitcast(I32)
         slot_view = slots[:, 0 : PACK * T2].rearrange("p (t m) -> p t m", t=PACK)
 
         def regroup(m0, m1):
-            grouped = work.tile([P, (m1 - m0) * PACK], BF16, name="grouped", bufs=3, align_bytes=64)
+            grouped = work.tile([P, (m1 - m0) * PACK], BF16, name="grouped", bufs=3, align_bytes=256)
             nc.vector.tensor_copy(
                 grouped[:].rearrange("p (c i t) -> p c t i", i=4, t=PACK),
                 slot_view[:, :, m0:m1].rearrange("p t (c i) -> p c t i", i=4),
@@ -317,7 +317,7 @@ def tile_list_rod_checkpoint_kernel(
                 start=True,
                 stop=True,
             )
-            half_cos = work.tile([P, m1 - m0], F32, name="half_cos", bufs=4)
+            half_cos = work.tile([P, m1 - m0], F32, name="half_cos", bufs=4, align_bytes=256)
             nc.scalar.activation(half_cos[:], phase[:], ACT.Sin, scale=0.5, bias=math.pi / 2)
             return half_cos
 
@@ -334,18 +334,18 @@ def tile_list_rod_checkpoint_kernel(
                 stop=True,
             )
             if spent is None:
-                cos_tile = work.tile([P, m1 - m0], F32, name="cos_up", bufs=4)
+                cos_tile = work.tile([P, m1 - m0], F32, name="cos_up", bufs=4, align_bytes=256)
                 cos_up = cos_tile[:]
                 nc.scalar.activation(cos_up, half_cos[:], ACT.Square)
             else:
                 cos_up = spent
                 nc.gpsimd.tensor_tensor(cos_up, half_cos[:], half_cos[:], ALU.mult)
-            y = work.tile([P, m1 - m0], F32, name="y", bufs=8)
+            y = work.tile([P, m1 - m0], F32, name="y", bufs=8, align_bytes=256)
             nc.vector.scalar_tensor_tensor(y[:], cos_up, -0.5, value[:], ALU.add, ALU.mult)
             nc.sync.dma_start(out_0[n * P : (n + 1) * P, m0:m1], y[:])
 
-        wd_q = keep.tile([P, N], U32, name="wd_q", tag="resp3", align_bytes=64)
-        wd_sc = keep.tile([P, N], U8, name="wd_sc", align_bytes=64)
+        wd_q = keep.tile([P, N], U32, name="wd_q", tag="resp3", align_bytes=256)
+        wd_sc = keep.tile([P, N], U8, name="wd_sc", align_bytes=256)
         for n0, n1 in ((0, P), (P, N)):
             nc.vector.quantize_mx(
                 out=wd_q[:, n0:n1].bitcast(FP8X4), scales=wd_sc[:, n0:n1], in_=wd_bf[:, n0 * PACK : n1 * PACK]

@@ -117,7 +117,7 @@ def tile_list_rod_checkpoint_kernel(
         wgs_rows = wgs.rearrange("(q f) s -> q f s", f=PACK)
 
         def load_late_weights(u):
-            for c in range(QUADS):
+            for c in (0, 2, 1, 3):
                 nc.sync.dma_start(late_weights[u - 2][QUAD * c : QUAD * (c + 1), :], wgs_rows[:, u, :])
 
         nc.sync.dma_start(pick[:], offs)
@@ -296,8 +296,8 @@ def tile_list_rod_checkpoint_kernel(
         def regroup(m0, m1):
             grouped = work.tile([P, (m1 - m0) * PACK], BF16, name="grouped", bufs=3, align_bytes=256)
             nc.vector.tensor_copy(
-                grouped[:].rearrange("p (c i t) -> p c t i", i=4, t=PACK),
-                slot_view[:, :, m0:m1].rearrange("p t (c i) -> p c t i", i=4),
+                grouped[:].rearrange("p (c i t) -> p c t i", i=8, t=PACK),
+                slot_view[:, :, m0:m1].rearrange("p t (c i) -> p c t i", i=8),
             )
             return grouped
 

@@ -242,18 +242,19 @@ def tile_list_rod_checkpoint_kernel(
         scatter(0, 0, HALF, resp[0][:, 0:HALF])
         for a in range(PASSES):
             round_late(0, a)
-        for a in range(PASSES):
-            round_paired(1, a)
-            round_late(1, a)
+        round_paired(1, 0)
+        round_late(1, 0)
+        round_paired(1, 1)
         codes, bytes_ = quantise(paired_bf[1], "w1_1")
         w1_q.append((codes[:], bytes_[:]))
+        spent = w1_raw[1][0][:, 0:HALF]
+        respond(0, [(HALF, S)], [roots[:, HALF:S]], [spent])
+        scatter(0, HALF, S, spent)
+        round_late(1, 1)
         codes, bytes_ = quantise(late_bf, "w1_late")
         for e in range(2):
             cols = slice(e * PASSES * P, (e + 1) * PASSES * P)
             w1_q.append((codes[:, cols], bytes_[:, cols]))
-        spent = w1_raw[1][1][:, 0:HALF]
-        respond(0, [(HALF, S)], [roots[:, HALF:S]], [spent])
-        scatter(0, HALF, S, spent)
         store_page(0)
 
         held = [rounded[0][:].bitcast(F32), rounded[1][:].bitcast(F32), slot(2).bitcast(F32)]

@@ -30,6 +30,7 @@ QUARTER = S // 4
 HALF = S // 2
 PIECE = BANK // 2
 W1_HALF = H // 2
+FIRST = ((0, 256), (256, 384), (384, 512))
 ON_GPSIMD = (8, 10, 12)
 
 
@@ -185,7 +186,7 @@ def tile_list_rod_checkpoint_kernel(
             round_paired(0, a)
         codes, bytes_ = quantise(paired_bf[0], "w1_0")
         w1_q = [(codes[:], bytes_[:])]
-        for j0, j1 in ((0, QUARTER), (QUARTER, HALF), (HALF, S)):
+        for j0, j1 in FIRST + ((HALF, S),):
             nc.vector.tensor_copy(v[1][:, j0:j1], tab[1][:].indirect(entries(pick, j0, j1)))
         early_factors = keep.tile([P, 2 * S], F32, name="early_factors", align_bytes=256)
         for u in range(2):
@@ -202,19 +203,22 @@ def tile_list_rod_checkpoint_kernel(
         def slot(t, m0=0, m1=T2):
             return slots[:, t * T2 + m0 : t * T2 + m1]
 
+        def multiply(acc, u, a, j0, j1):
+            codes, bytes_ = w1_q[u]
+            nc.tensor.matmul_mx(
+                out=acc[:],
+                lhsT=codes[:, a * P : (a + 1) * P].bitcast(FP8X4),
+                lhsT_scale=bytes_[:, a * P : (a + 1) * P],
+                rhs=v[a][:, j0:j1].bitcast(FP8X4),
+                rhs_scale=v_sc[4 * a : P, j0:j1],
+                start=(a == 0),
+                stop=(a == PASSES - 1),
+            )
+
         def square(u, j0, j1):
             acc = psum.tile([P, j1 - j0], F32, name="phase", bufs=4)
-            codes, bytes_ = w1_q[u]
             for a in range(PASSES):
-                nc.tensor.matmul_mx(
-                    out=acc[:],
-                    lhsT=codes[:, a * P : (a + 1) * P].bitcast(FP8X4),
-                    lhsT_scale=bytes_[:, a * P : (a + 1) * P],
-                    rhs=v[a][:, j0:j1].bitcast(FP8X4),
-                    rhs_scale=v_sc[4 * a : P, j0:j1],
-                    start=(a == 0),
-                    stop=(a == PASSES - 1),
-                )
+                multiply(acc, u, a, j0, j1)
             nc.scalar.activation(squares[:, j0:j1], acc[:], ACT.Square)
 
         def respond(u, spans, root_at, resp_at):
@@ -235,10 +239,19 @@ def tile_list_rod_checkpoint_kernel(
                     p0 = 2 * QUAD * g + QUAD * c
                     nc.sync.dma_start(slot(e)[p0 : p0 + QUAD, :], rounded[g][2 * e + c : P : 4, :])
 
-        quarters = [(0, QUARTER), (QUARTER, HALF)]
         halves = [(0, HALF), (HALF, S)]
 
-        respond(0, quarters, [roots[:, a:b] for a, b in quarters], [resp[0][:, a:b] for a, b in quarters])
+        pieces = FIRST + ((HALF, S),)
+        sums = [psum.tile([P, j1 - j0], F32, name="phase", bufs=4) for j0, j1 in pieces]
+        for a in range(PASSES):
+            for acc, span in zip(sums, pieces):
+                multiply(acc, 0, a, *span)
+        for acc, (j0, j1) in zip(sums, FIRST):
+            nc.scalar.activation(squares[:, j0:j1], acc[:], ACT.Square)
+        for j0, j1 in FIRST:
+            nc.scalar.activation(roots[:, j0:j1], squares[:, j0:j1], ACT.Abs_reciprocal_sqrt, bias=1.0)
+        for j0, j1 in FIRST:
+            nc.scalar.activation(resp[0][:, j0:j1], roots[:, j0:j1], ACT.Square)
         scatter(0, 0, HALF, resp[0][:, 0:HALF])
         for a in range(PASSES):
             round_late(0, a)
@@ -248,7 +261,9 @@ def tile_list_rod_checkpoint_kernel(
         codes, bytes_ = quantise(paired_bf[1], "w1_1")
         w1_q.append((codes[:], bytes_[:]))
         spent = w1_raw[1][0][:, 0:HALF]
-        respond(0, [(HALF, S)], [roots[:, HALF:S]], [spent])
+        nc.scalar.activation(squares[:, HALF:S], sums[-1][:], ACT.Square)
+        nc.scalar.activation(roots[:, HALF:S], squares[:, HALF:S], ACT.Abs_reciprocal_sqrt, bias=1.0)
+        nc.scalar.activation(spent, roots[:, HALF:S], ACT.Square)
         scatter(0, HALF, S, spent)
         round_late(1, 1)
         codes, bytes_ = quantise(late_bf, "w1_late")

@@ -50,6 +50,8 @@ def tile_list_rod_checkpoint_kernel(
 
         tab_sc = keep.tile([P, T], U8, name="tab_sc", align_bytes=256)
         nc.gpsimd.memset(tab_sc[:].bitcast(I32), 0)
+        gain_rows = keep.tile([P, P], F32, name="gain_rows", align_bytes=256)
+        nc.vector.memset(gain_rows[:], 0.0)
 
         one = keep.tile([P, 8], F32, name="one")
         warm = keep.tile([P, 8], F32, name="warm")
@@ -71,7 +73,8 @@ def tile_list_rod_checkpoint_kernel(
         rounded = [keep.tile([P, T2], BF16, name=f"rounded{g}", align_bytes=256) for g in range(2)]
         third_weights = keep.tile([P, S], F32, name="third_weights", align_bytes=256)
         late_weights = [third_weights[:], rounded[1][:].bitcast(F32)]
-        gains = [keep.tile([P, 8], F32, name=f"gains{g}") for g in range(2)]
+        gain_dealt = keep.tile([P, 2 * QUAD], F32, name="gain_dealt", align_bytes=256)
+        gains = keep.tile([P, 2 * QUAD], F32, name="gains", align_bytes=256)
         late_gains = keep.tile([P, 8], F32, name="late_gains")
         wc = keep.tile([P, 2 * N], U8, name="wc", align_bytes=256)
         slots = keep.tile([P, 3 * T2 + 2 * PACK * N], BF16, name="slots", align_bytes=256)
@@ -109,12 +112,6 @@ def tile_list_rod_checkpoint_kernel(
             else:
                 nc.sync.dma_start(slot_rows(out_1)[:, u, :], page[u][:])
 
-        def load_gain(g):
-            rows = gain.rearrange("(g c q f o) -> g c q f o", g=2, c=2, f=PACK, o=1)
-            with nc.allow_non_contiguous_dma(reason="one gain for each partition"):
-                for c in range(2):
-                    nc.sync.dma_start(gains[g][c:P:2, 0:1], rows[g][c][:, 0:2, :])
-
         wgs_rows = wgs.rearrange("(q f) s -> q f s", f=PACK)
 
         def load_late_weights(u):
@@ -122,19 +119,22 @@ def tile_list_rod_checkpoint_kernel(
                 nc.sync.dma_start(late_weights[u - 2][QUAD * c : QUAD * (c + 1), :], wgs_rows[:, u, :])
 
         nc.sync.dma_start(pick[:], offs)
-        load_tab(0, (0, 768, 1408, T))
+        load_tab(0, (0, 256, 512, T))
         for q in range(QUADS):
             nc.sync.dma_start(
                 tab_sc[32 * q : 32 * q + 4 * PASSES, :].bitcast(I32),
                 tab_scales[:, 4 * q : 4 * q + 4, :].bitcast(I32),
             )
+        nc.sync.dma_start(
+            gain_rows[0:P:QUAD, :].rearrange("p (b i) -> p b i", i=QUAD),
+            gain.rearrange("(b p i) -> p b i", p=QUADS, i=QUAD),
+        )
         load_w1(0)
         load_tab(1)
-        load_gain(0)
         nc.sync.dma_start(put[:], offs2)
-        for c in range(2):
-            nc.sync.dma_start(weights[c:P:2, :], wgs_rows[:, 0:2, :])
-        load_gain(1)
+        for j0, j1 in ((0, HALF), (HALF, S - QUARTER), (S - QUARTER, S)):
+            for c in range(2):
+                nc.sync.dma_start(weights[c:P:2, j0:j1], wgs_rows[:, 0:2, j0:j1])
         load_page(0)
         load_w1(1)
         nc.sync.dma_start(late_gains[:, 0:2], gain.rearrange("(p t) -> p t", t=PACK)[:, 2:4])
@@ -150,6 +150,13 @@ def tile_list_rod_checkpoint_kernel(
                 wc_sc[32 * q : 32 * q + 4, :].bitcast(I32),
                 wc_scales[0, 4 * q : 4 * q + 4, :].bitcast(I32),
             )
+
+        nc.vector.tensor_copy(
+            gain_dealt[:, 0 : 2 * QUAD].rearrange("p (g q e c) -> p g q e c", g=2, e=2, c=2),
+            gain_rows[:, 0:P].rearrange("p (g c q f) -> p g q f c", g=2, c=2, f=PACK)[:, :, :, 0:2, :],
+        )
+        for g in range(2):
+            nc.vector.transpose(gains[:, g * QUAD : (g + 1) * QUAD], gain_dealt[:, g * QUAD : (g + 1) * QUAD])
 
         def entries(lst, j0, j1):
             return lst[:] if (j0, j1) == (0, S) else lst[:, j0 // 16 : j1 // 16]
@@ -191,7 +198,7 @@ def tile_list_rod_checkpoint_kernel(
         early_factors = keep.tile([P, 2 * S], F32, name="early_factors", align_bytes=256)
         for u in range(2):
             nc.gpsimd.tensor_scalar(
-                early_factors[:, u * S : (u + 1) * S], weights[:], gains[u][:, 0:1], -0.0, ALU.mult, ALU.add
+                early_factors[:, u * S : (u + 1) * S], weights[:], gains[:, u * QUAD : u * QUAD + 1], -0.0, ALU.mult, ALU.add
             )
         factors = [early_factors[:, 0:S], early_factors[:, S:], late_factors[0][:], late_factors[1][:]]
 

@@ -30,7 +30,14 @@ QUARTER = S // 4
 HALF = S // 2
 PIECE = BANK // 2
 W1_HALF = H // 2
+ALIGN = 256
+BANKS = 4
 FIRST = ((0, 256), (256, 384), (384, 512))
+TABLE_CUTS = (0, 256, 512, T)
+WGS_CUTS = (0, HALF, S - QUARTER, S)
+QUADRANT_ORDER = (0, 2, 1, 3)
+RUN = 8
+WD_RUN = 4
 ON_GPSIMD = (8, 10, 12)
 
 
@@ -48,9 +55,9 @@ def tile_list_rod_checkpoint_kernel(
         pick = lists.tile([P, S // 16], U16, name="pick")
         put = lists.tile([P, S // 16], U16, name="put")
 
-        tab_sc = keep.tile([P, T], U8, name="tab_sc", align_bytes=256)
+        tab_sc = keep.tile([P, T], U8, name="tab_sc", align_bytes=ALIGN)
         nc.gpsimd.memset(tab_sc[:].bitcast(I32), 0)
-        gain_rows = keep.tile([P, P], F32, name="gain_rows", align_bytes=256)
+        gain_rows = keep.tile([P, P], F32, name="gain_rows", align_bytes=ALIGN)
         nc.vector.memset(gain_rows[:], 0.0)
 
         one = keep.tile([P, 8], F32, name="one")
@@ -58,26 +65,26 @@ def tile_list_rod_checkpoint_kernel(
         nc.vector.memset(one[:], 1.0)
         nc.scalar.activation(warm[:], one[:], ACT.Abs_reciprocal_sqrt)
 
-        wc_sc = keep.tile([P, N], U8, name="wc_sc", align_bytes=256)
+        wc_sc = keep.tile([P, N], U8, name="wc_sc", align_bytes=ALIGN)
         nc.vector.memset(wc_sc[:].bitcast(I32), 0)
 
-        tab = [keep.tile([P, T], U32, name=f"tab{a}", align_bytes=256) for a in range(PASSES)]
+        tab = [keep.tile([P, T], U32, name=f"tab{a}", align_bytes=ALIGN) for a in range(PASSES)]
         w1_raw = [
-            [keep.tile([P, PACK * W1_HALF], F32, name=f"w1_raw{g}{a}", align_bytes=256) for a in range(PASSES)]
+            [keep.tile([P, PACK * W1_HALF], F32, name=f"w1_raw{g}{a}", align_bytes=ALIGN) for a in range(PASSES)]
             for g in range(2)
         ]
         w1_rows = w1.rearrange("(a p j) c -> a p j c", p=P, j=PACK)
-        page = [keep.tile([P, T2], F32, name=f"page{u}", align_bytes=256) for u in range(TILES)]
-        weights = keep.tile([P, S], F32, name="weights", align_bytes=256)
-        late_factors = [keep.tile([P, S], F32, name=f"late_factor{e}", align_bytes=256) for e in range(2)]
-        rounded = [keep.tile([P, T2], BF16, name=f"rounded{g}", align_bytes=256) for g in range(2)]
-        third_weights = keep.tile([P, S], F32, name="third_weights", align_bytes=256)
+        page = [keep.tile([P, T2], F32, name=f"page{u}", align_bytes=ALIGN) for u in range(TILES)]
+        weights = keep.tile([P, S], F32, name="weights", align_bytes=ALIGN)
+        late_factors = [keep.tile([P, S], F32, name=f"late_factor{e}", align_bytes=ALIGN) for e in range(2)]
+        rounded = [keep.tile([P, T2], BF16, name=f"rounded{g}", align_bytes=ALIGN) for g in range(2)]
+        third_weights = keep.tile([P, S], F32, name="third_weights", align_bytes=ALIGN)
         late_weights = [third_weights[:], rounded[1][:].bitcast(F32)]
-        gain_dealt = keep.tile([P, 2 * QUAD], F32, name="gain_dealt", align_bytes=256)
-        gains = keep.tile([P, 2 * QUAD], F32, name="gains", align_bytes=256)
+        gain_dealt = keep.tile([P, 2 * QUAD], F32, name="gain_dealt", align_bytes=ALIGN)
+        gains = keep.tile([P, 2 * QUAD], F32, name="gains", align_bytes=ALIGN)
         late_gains = keep.tile([P, 8], F32, name="late_gains")
-        wc = keep.tile([P, 2 * N], U8, name="wc", align_bytes=256)
-        slots = keep.tile([P, 3 * T2 + 2 * PACK * N], BF16, name="slots", align_bytes=256)
+        wc = keep.tile([P, 2 * N], U8, name="wc", align_bytes=ALIGN)
+        slots = keep.tile([P, 3 * T2 + 2 * PACK * N], BF16, name="slots", align_bytes=ALIGN)
         wd_raw = slots[:, 3 * T2 :].bitcast(F32)
 
         def paired_rows(x):
@@ -115,14 +122,14 @@ def tile_list_rod_checkpoint_kernel(
         wgs_rows = wgs.rearrange("(q f) s -> q f s", f=PACK)
 
         def load_late_weights(u):
-            for c in (0, 2, 1, 3):
+            for c in QUADRANT_ORDER:
                 nc.sync.dma_start(late_weights[u - 2][QUAD * c : QUAD * (c + 1), :], wgs_rows[:, u, :])
 
         nc.sync.dma_start(pick[:], offs)
-        load_tab(0, (0, 256, 512, T))
+        load_tab(0, TABLE_CUTS)
         for q in range(QUADS):
             nc.sync.dma_start(
-                tab_sc[32 * q : 32 * q + 4 * PASSES, :].bitcast(I32),
+                tab_sc[QUAD * q : QUAD * q + 4 * PASSES, :].bitcast(I32),
                 tab_scales[:, 4 * q : 4 * q + 4, :].bitcast(I32),
             )
         nc.sync.dma_start(
@@ -132,7 +139,7 @@ def tile_list_rod_checkpoint_kernel(
         load_w1(0)
         load_tab(1)
         nc.sync.dma_start(put[:], offs2)
-        for j0, j1 in ((0, HALF), (HALF, S - QUARTER), (S - QUARTER, S)):
+        for j0, j1 in zip(WGS_CUTS, WGS_CUTS[1:]):
             for c in range(2):
                 nc.sync.dma_start(weights[c:P:2, j0:j1], wgs_rows[:, 0:2, j0:j1])
         load_page(0)
@@ -147,13 +154,13 @@ def tile_list_rod_checkpoint_kernel(
         nc.sync.dma_start(wc[:].bitcast(I32), wc_words[0].bitcast(I32))
         for q in range(QUADS):
             nc.sync.dma_start(
-                wc_sc[32 * q : 32 * q + 4, :].bitcast(I32),
+                wc_sc[QUAD * q : QUAD * q + 4, :].bitcast(I32),
                 wc_scales[0, 4 * q : 4 * q + 4, :].bitcast(I32),
             )
 
-        nc.vector.tensor_copy(
-            gain_dealt[:, 0 : 2 * QUAD].rearrange("p (g q e c) -> p g q e c", g=2, e=2, c=2),
-            gain_rows[:, 0:P].rearrange("p (g c q f) -> p g q f c", g=2, c=2, f=PACK)[:, :, :, 0:2, :],
+        nc.scalar.copy(
+            gain_dealt[:].rearrange("p (g q e c) -> p g q e c", g=2, e=2, c=2),
+            gain_rows[:].rearrange("p (g c q f) -> p g q f c", g=2, c=2, f=PACK)[:, :, :, 0:2, :],
         )
         for g in range(2):
             nc.vector.transpose(gains[:, g * QUAD : (g + 1) * QUAD], gain_dealt[:, g * QUAD : (g + 1) * QUAD])
@@ -161,8 +168,8 @@ def tile_list_rod_checkpoint_kernel(
         def entries(lst, j0, j1):
             return lst[:] if (j0, j1) == (0, S) else lst[:, j0 // 16 : j1 // 16]
 
-        paired_bf = [keep.tile([P, PASSES * P * PACK], BF16, name=f"paired_bf{g}", align_bytes=256) for g in range(2)]
-        late_bf = keep.tile([P, 2 * PASSES * P * PACK], BF16, name="late_bf", align_bytes=256)
+        paired_bf = [keep.tile([P, PASSES * P * PACK], BF16, name=f"paired_bf{g}", align_bytes=ALIGN) for g in range(2)]
+        late_bf = keep.tile([P, 2 * PASSES * P * PACK], BF16, name="late_bf", align_bytes=ALIGN)
 
         def round_paired(g, a):
             nc.scalar.copy(
@@ -178,15 +185,15 @@ def tile_list_rod_checkpoint_kernel(
                 w1_raw[g][a][:].rearrange("p (j r f) -> p r j f", j=PACK, f=PACK)[:, :, :, 2:4],
             )
 
-        def quantise(bf, name, tag=None):
+        def quantise(bf, name):
             width = bf.shape[1] // PACK
-            codes = keep.tile([P, width], U32, name=f"{name}_q", tag=tag or f"{name}_q", align_bytes=256)
-            bytes_ = keep.tile([P, width], U8, name=f"{name}_sc", align_bytes=256)
+            codes = keep.tile([P, width], U32, name=f"{name}_q", align_bytes=ALIGN)
+            bytes_ = keep.tile([P, width], U8, name=f"{name}_sc", align_bytes=ALIGN)
             nc.vector.quantize_mx(out=codes[:].bitcast(FP8X4), scales=bytes_[:], in_=bf[:])
             return codes, bytes_
 
-        v = [keep.tile([P, S], U32, name=f"v{a}", align_bytes=256) for a in range(PASSES)]
-        v_sc = keep.tile([P, S], U8, name="v_sc", align_bytes=256)
+        v = [keep.tile([P, S], U32, name=f"v{a}", align_bytes=ALIGN) for a in range(PASSES)]
+        v_sc = keep.tile([P, S], U8, name="v_sc", align_bytes=ALIGN)
         nc.vector.tensor_copy(v[0][:], tab[0][:].indirect(pick[:]))
         nc.vector.tensor_copy(v_sc[:], tab_sc[:].indirect(pick[:]))
         for a in range(PASSES):
@@ -195,17 +202,15 @@ def tile_list_rod_checkpoint_kernel(
         w1_q = [(codes[:], bytes_[:])]
         for j0, j1 in FIRST + ((HALF, S),):
             nc.vector.tensor_copy(v[1][:, j0:j1], tab[1][:].indirect(entries(pick, j0, j1)))
-        early_factors = keep.tile([P, 2 * S], F32, name="early_factors", align_bytes=256)
+        early_factors = keep.tile([P, 2 * S], F32, name="early_factors", align_bytes=ALIGN)
         for u in range(2):
-            nc.gpsimd.tensor_scalar(
-                early_factors[:, u * S : (u + 1) * S], weights[:], gains[:, u * QUAD : u * QUAD + 1], -0.0, ALU.mult, ALU.add
-            )
+            column = gains[:, u * QUAD : u * QUAD + 1]
+            nc.gpsimd.tensor_scalar(early_factors[:, u * S : (u + 1) * S], weights[:], column, -0.0, ALU.mult, ALU.add)
         factors = [early_factors[:, 0:S], early_factors[:, S:], late_factors[0][:], late_factors[1][:]]
 
-
-        squares = keep.tile([P, S], F32, name="squares", align_bytes=256)
-        roots = keep.tile([P, S], F32, name="roots", align_bytes=256)
-        resp = [keep.tile([P, S], F32, name=f"resp{u}", align_bytes=256) for u in range(TILES)]
+        squares = keep.tile([P, S], F32, name="squares", align_bytes=ALIGN)
+        roots = keep.tile([P, S], F32, name="roots", align_bytes=ALIGN)
+        resp = [keep.tile([P, S], F32, name=f"resp{u}", align_bytes=ALIGN) for u in range(TILES)]
 
         def slot(t, m0=0, m1=T2):
             return slots[:, t * T2 + m0 : t * T2 + m1]
@@ -223,7 +228,7 @@ def tile_list_rod_checkpoint_kernel(
             )
 
         def square(u, j0, j1):
-            acc = psum.tile([P, j1 - j0], F32, name="phase", bufs=4)
+            acc = psum.tile([P, j1 - j0], F32, name="phase", bufs=BANKS)
             for a in range(PASSES):
                 multiply(acc, u, a, j0, j1)
             nc.scalar.activation(squares[:, j0:j1], acc[:], ACT.Square)
@@ -249,7 +254,7 @@ def tile_list_rod_checkpoint_kernel(
         halves = [(0, HALF), (HALF, S)]
 
         pieces = FIRST + ((HALF, S),)
-        sums = [psum.tile([P, j1 - j0], F32, name="phase", bufs=4) for j0, j1 in pieces]
+        sums = [psum.tile([P, j1 - j0], F32, name="phase", bufs=BANKS) for j0, j1 in pieces]
         for a in range(PASSES):
             for acc, span in zip(sums, pieces):
                 multiply(acc, 0, a, *span)
@@ -279,15 +284,15 @@ def tile_list_rod_checkpoint_kernel(
             w1_q.append((codes[:, cols], bytes_[:, cols]))
         store_page(0)
 
-        held = [rounded[0][:].bitcast(F32), rounded[1][:].bitcast(F32), slot(2).bitcast(F32)]
+        held = rounded[0][:].bitcast(F32)
         first = factors[2][:, 0:QUARTER]
-        respond(1, [(0, QUARTER)], [held[0][:, 0:QUARTER]], [first])
+        respond(1, [(0, QUARTER)], [held[:, 0:QUARTER]], [first])
         scatter(1, 0, QUARTER, first)
         nc.vector.tensor_scalar(factors[2], late_weights[0], late_gains[:, 0:1], None, ALU.mult)
         square(1, QUARTER, HALF)
         square(1, HALF, S)
-        nc.scalar.activation(held[0][:, QUARTER:S], squares[:, QUARTER:S], ACT.Abs_reciprocal_sqrt, bias=1.0)
-        nc.scalar.activation(resp[1][:, QUARTER:S], held[0][:, QUARTER:S], ACT.Square)
+        nc.scalar.activation(held[:, QUARTER:S], squares[:, QUARTER:S], ACT.Abs_reciprocal_sqrt, bias=1.0)
+        nc.scalar.activation(resp[1][:, QUARTER:S], held[:, QUARTER:S], ACT.Square)
         scatter(1, QUARTER, S, resp[1][:, QUARTER:S])
         round_and_move(0)
         store_page(1)
@@ -298,29 +303,30 @@ def tile_list_rod_checkpoint_kernel(
         round_and_move(1)
         store_page(2)
 
-        wd_bf = keep.tile([P, PACK * N], BF16, name="wd_bf", align_bytes=256)
-        respond(3, halves, [wd_bf[:].bitcast(F32)[:, 0:HALF], held[2][:, 0:HALF]], [resp[3][:, a:b] for a, b in halves])
+        wd_bf = keep.tile([P, PACK * N], BF16, name="wd_bf", align_bytes=ALIGN)
+        last_roots = [wd_bf[:].bitcast(F32)[:, 0:HALF], slot(2).bitcast(F32)[:, 0:HALF]]
+        respond(3, halves, last_roots, [resp[3][:, a:b] for a, b in halves])
         scatter(3, 0, S, resp[3][:])
         nc.scalar.activation(squares[:, S - 1 : S], one[:, 0:1], ACT.Sin)
         nc.scalar.copy(slot(2), page[2][:])
         nc.scalar.activation(
-            wd_bf[:].rearrange("p (c i j) -> p c j i", i=4, j=PACK),
-            wd_raw.rearrange("p (j c i) -> p c j i", i=4, j=PACK),
+            wd_bf[:].rearrange("p (c i j) -> p c j i", i=WD_RUN, j=PACK),
+            wd_raw.rearrange("p (j c i) -> p c j i", i=WD_RUN, j=PACK),
             ACT.Copy,
             scale=2.0,
         )
         store_page(3)
 
-        words = keep.tile([P, T2], U32, name="words", align_bytes=256)
-        scales = keep.tile([P, T2], U8, name="scales", align_bytes=256)
+        words = keep.tile([P, T2], U32, name="words", align_bytes=ALIGN)
+        scales = keep.tile([P, T2], U8, name="scales", align_bytes=ALIGN)
         words_dst = out_2[0].rearrange("p m t -> p (m t)").bitcast(I32)
         slot_view = slots[:, 0 : PACK * T2].rearrange("p (t m) -> p t m", t=PACK)
 
         def regroup(m0, m1):
-            grouped = work.tile([P, (m1 - m0) * PACK], BF16, name="grouped", bufs=3, align_bytes=256)
+            grouped = work.tile([P, (m1 - m0) * PACK], BF16, name="grouped", bufs=3, align_bytes=ALIGN)
             nc.vector.tensor_copy(
-                grouped[:].rearrange("p (c i t) -> p c t i", i=8, t=PACK),
-                slot_view[:, :, m0:m1].rearrange("p t (c i) -> p c t i", i=8),
+                grouped[:].rearrange("p (c i t) -> p c t i", i=RUN, t=PACK),
+                slot_view[:, :, m0:m1].rearrange("p t (c i) -> p c t i", i=RUN),
             )
             return grouped
 
@@ -330,7 +336,7 @@ def tile_list_rod_checkpoint_kernel(
                 nc.sync.dma_start(words_dst[:, m1 - BANK : m1], words[:, m1 - BANK : m1].bitcast(I32))
 
         def half_cosine(n, m0, m1):
-            phase = psum.tile([P, m1 - m0], F32, name="phase", bufs=4)
+            phase = psum.tile([P, m1 - m0], F32, name="phase", bufs=BANKS)
             nc.tensor.matmul_mx(
                 out=phase[:],
                 lhsT=wc[:, 2 * n * P : 2 * (n + 1) * P].bitcast(FP4X4),
@@ -340,12 +346,12 @@ def tile_list_rod_checkpoint_kernel(
                 start=True,
                 stop=True,
             )
-            half_cos = work.tile([P, m1 - m0], F32, name="half_cos", bufs=4, align_bytes=256)
+            half_cos = work.tile([P, m1 - m0], F32, name="half_cos", bufs=BANKS, align_bytes=ALIGN)
             nc.scalar.activation(half_cos[:], phase[:], ACT.Sin, scale=0.5, bias=math.pi / 2)
             return half_cos
 
-        def finish(half_cos, n, m0, m1, spent):
-            value = psum.tile([P, m1 - m0], F32, name="value", bufs=4)
+        def finish(half_cos, n, m0, m1, free):
+            value = psum.tile([P, m1 - m0], F32, name="value", bufs=BANKS)
             cols = slice(n * P, (n + 1) * P)
             nc.tensor.matmul_mx(
                 out=value[:],
@@ -356,19 +362,19 @@ def tile_list_rod_checkpoint_kernel(
                 start=True,
                 stop=True,
             )
-            if spent is None:
-                cos_tile = work.tile([P, m1 - m0], F32, name="cos_up", bufs=4, align_bytes=256)
+            if free is None:
+                cos_tile = work.tile([P, m1 - m0], F32, name="cos_up", bufs=BANKS, align_bytes=ALIGN)
                 cos_up = cos_tile[:]
                 nc.scalar.activation(cos_up, half_cos[:], ACT.Square)
             else:
-                cos_up = spent
+                cos_up = free
                 nc.gpsimd.tensor_tensor(cos_up, half_cos[:], half_cos[:], ALU.mult)
-            y = work.tile([P, m1 - m0], F32, name="y", bufs=8, align_bytes=256)
+            y = work.tile([P, m1 - m0], F32, name="y", bufs=2 * BANKS, align_bytes=ALIGN)
             nc.vector.scalar_tensor_tensor(y[:], cos_up, -0.5, value[:], ALU.add, ALU.mult)
             nc.sync.dma_start(out_0[n * P : (n + 1) * P, m0:m1], y[:])
 
-        wd_q = keep.tile([P, N], U32, name="wd_q", tag="resp3", align_bytes=256)
-        wd_sc = keep.tile([P, N], U8, name="wd_sc", align_bytes=256)
+        wd_q = keep.tile([P, N], U32, name="wd_q", tag="resp3", align_bytes=ALIGN)
+        wd_sc = keep.tile([P, N], U8, name="wd_sc", align_bytes=ALIGN)
         for n0, n1 in ((0, P), (P, N)):
             nc.vector.quantize_mx(
                 out=wd_q[:, n0:n1].bitcast(FP8X4), scales=wd_sc[:, n0:n1], in_=wd_bf[:, n0 * PACK : n1 * PACK]
@@ -376,30 +382,31 @@ def tile_list_rod_checkpoint_kernel(
         spans = [(0, PIECE), (PIECE, BANK)] + [(c * BANK, (c + 1) * BANK) for c in range(1, CHUNKS)]
         for m0, m1 in spans:
             nc.scalar.copy(slot(3, m0, m1), page[3][:, m0:m1])
-        for span in spans[0:3]:
+        ahead = 2
+        for span in spans[0 : ahead + 1]:
             quantise_page(regroup(*span), *span)
 
         behind = None
         count = 0
         for i, whole in enumerate(spans):
-            if 1 <= i <= 2:
-                last_grouped = regroup(*spans[i + 2])
-                quantise_page(last_grouped, *spans[i + 2])
-            if i == 2:
+            if 1 <= i < len(spans) - ahead:
+                last_grouped = regroup(*spans[i + ahead])
+                quantise_page(last_grouped, *spans[i + ahead])
+            if i + ahead + 1 == len(spans):
                 for q in range(QUADS):
                     nc.sync.dma_start(
                         out_3[0, 4 * q : 4 * q + 4, :].bitcast(I32),
-                        scales[32 * q : 32 * q + 4, :].bitcast(I32),
+                        scales[QUAD * q : QUAD * q + 4, :].bitcast(I32),
                     )
             for n in range(NT):
                 m0, m1 = whole
                 final = i + 1 == len(spans) and n + 1 == NT
                 for piece in ((m0, m1 - PIECE), (m1 - PIECE, m1)) if final else (whole,):
-                    spent = None
+                    free = None
                     if count in ON_GPSIMD:
                         at = ON_GPSIMD.index(count) % 2 * BANK
-                        spent = last_grouped[:].bitcast(F32)[:, at : at + BANK]
-                    now = (half_cosine(n, *piece), n, *piece, spent)
+                        free = last_grouped[:].bitcast(F32)[:, at : at + BANK]
+                    now = (half_cosine(n, *piece), n, *piece, free)
                     count = count + 1
                     if behind is not None:
                         finish(*behind)

import math
from contextlib import ExitStack

import concourse.mybir as mybir

K, T, S, T2, H, N = 1024, 2048, 1024, 2048, 512, 384
FLOPS = 2 * K * H * S + 2 * 2 * H * N * T2

F32 = mybir.dt.float32
BF16 = mybir.dt.bfloat16
I32 = mybir.dt.int32
U32 = mybir.dt.uint32
U16 = mybir.dt.uint16
U8 = mybir.dt.uint8
FP8X4 = mybir.dt.float8_e4m3fn_x4
FP4X4 = mybir.dt.float4_e2m1fn_x4
ACT = mybir.ActivationFunctionType
ALU = mybir.AluOpType

P = 128
PACK = 4
QUADS = 4
QUAD = 32
BANK = 512
PASSES = K // (P * PACK)
TILES = H // P
CHUNKS = T2 // BANK
NT = N // P
QUARTER = S // 4
HALF = S // 2
PIECE = BANK // 2
W1_HALF = H // 2
ALIGN = 256
BANKS = 4
FIRST = ((0, 256), (256, 384), (384, 512))
TABLE_CUTS = (0, 256, 512, T)
WGS_CUTS = (0, HALF, S - QUARTER, S)
QUADRANT_ORDER = (0, 2, 1, 3)
RUN = 8
WD_RUN = 4
ON_GPSIMD = (8, 10, 12)


def tile_list_rod_checkpoint_kernel(
    tc, tab_words, tab_scales, offs, w1, gain, page0, wgs, offs2, wc_words, wc_scales, wd,
    out_0, out_1, out_2, out_3,
):
    nc = tc.nc
    with ExitStack() as ctx:
        lists = ctx.enter_context(tc.tile_pool(name="lists", bufs=1))
        keep = ctx.enter_context(tc.tile_pool(name="keep", bufs=1))
        work = ctx.enter_context(tc.tile_pool(name="work", bufs=3))
        psum = ctx.enter_context(tc.psum_pool(name="psum", bufs=1))

        pick = lists.tile([P, S // 16], U16, name="pick")
        put = lists.tile([P, S // 16], U16, name="put")

        tab_sc = keep.tile([P, T], U8, name="tab_sc", align_bytes=ALIGN)
        nc.gpsimd.memset(tab_sc[:].bitcast(I32), 0)
        gain_rows = keep.tile([P, P], F32, name="gain_rows", align_bytes=ALIGN)
        nc.vector.memset(gain_rows[:], 0.0)

        one = keep.tile([P, 8], F32, name="one")
        warm = keep.tile([P, 8], F32, name="warm")
        nc.vector.memset(one[:], 1.0)
        nc.scalar.activation(warm[:], one[:], ACT.Abs_reciprocal_sqrt)

        wc_sc = keep.tile([P, N], U8, name="wc_sc", align_bytes=ALIGN)
        nc.vector.memset(wc_sc[:].bitcast(I32), 0)

        tab = [keep.tile([P, T], U32, name=f"tab{a}", align_bytes=ALIGN) for a in range(PASSES)]
        w1_raw = [
            [keep.tile([P, PACK * W1_HALF], F32, name=f"w1_raw{g}{a}", align_bytes=ALIGN) for a in range(PASSES)]
            for g in range(2)
        ]
        w1_rows = w1.rearrange("(a p j) c -> a p j c", p=P, j=PACK)
        page = [keep.tile([P, T2], F32, name=f"page{u}", align_bytes=ALIGN) for u in range(TILES)]
        weights = keep.tile([P, S], F32, name="weights", align_bytes=ALIGN)
        late_factors = [keep.tile([P, S], F32, name=f"late_factor{e}", align_bytes=ALIGN) for e in range(2)]
        rounded = [keep.tile([P, T2], BF16, name=f"rounded{g}", align_bytes=ALIGN) for g in range(2)]
        third_weights = keep.tile([P, S], F32, name="third_weights", align_bytes=ALIGN)
        late_weights = [third_weights[:], rounded[1][:].bitcast(F32)]
        gain_dealt = keep.tile([P, 2 * QUAD], F32, name="gain_dealt", align_bytes=ALIGN)
        gains = keep.tile([P, 2 * QUAD], F32, name="gains", align_bytes=ALIGN)
        late_gains = keep.tile([P, 8], F32, name="late_gains")
        wc = keep.tile([P, 2 * N], U8, name="wc", align_bytes=ALIGN)
        slots = keep.tile([P, 3 * T2 + 2 * PACK * N], BF16, name="slots", align_bytes=ALIGN)
        wd_raw = slots[:, 3 * T2 :].bitcast(F32)

        def paired_rows(x):
            return x.rearrange("(g c q f) m -> g c q f m", g=2, c=2, f=PACK)

        def slot_rows(x):
            return x.rearrange("(p t) m -> p t m", t=PACK)

        def load_tab(a, cuts=(0, T)):
            words_in = tab_words[a].rearrange("p t i -> p (t i)").bitcast(I32)
            for t0, t1 in zip(cuts, cuts[1:]):
                nc.sync.dma_start(tab[a][:, t0:t1].bitcast(I32), words_in[:, t0:t1])

        def load_w1(g):
            for a in range(PASSES):
                nc.sync.dma_start(
                    w1_raw[g][a][:].rearrange("p (j c) -> p j c", j=PACK),
                    w1_rows[a][:, :, g * W1_HALF : (g + 1) * W1_HALF],
                )

        def load_page(u):
            if u < 2:
                for c in range(2):
                    nc.sync.dma_start(page[u][c:P:2, :], paired_rows(page0)[u][c][:, 0:2, :])
            else:
                nc.sync.dma_start(page[u][:], slot_rows(page0)[:, u, :])

        def store_page(u):
            if u < 2:
                for c in range(2):
                    nc.sync.dma_start(paired_rows(out_1)[u][c][:, 0:2, :], page[u][c:P:2, :])
            else:
                nc.sync.dma_start(slot_rows(out_1)[:, u, :], page[u][:])

        wgs_rows = wgs.rearrange("(q f) s -> q f s", f=PACK)

        def load_late_weights(u):
            for c in QUADRANT_ORDER:
                nc.sync.dma_start(late_weights[u - 2][QUAD * c : QUAD * (c + 1), :], wgs_rows[:, u, :])

        nc.sync.dma_start(pick[:], offs)
        load_tab(0, TABLE_CUTS)
        for q in range(QUADS):
            nc.sync.dma_start(
                tab_sc[QUAD * q : QUAD * q + 4 * PASSES, :].bitcast(I32),
                tab_scales[:, 4 * q : 4 * q + 4, :].bitcast(I32),
            )
        nc.sync.dma_start(
            gain_rows[0:P:QUAD, :].rearrange("p (b i) -> p b i", i=QUAD),
            gain.rearrange("(b p i) -> p b i", p=QUADS, i=QUAD),
        )
        load_w1(0)
        load_tab(1)
        nc.sync.dma_start(put[:], offs2)
        for j0, j1 in zip(WGS_CUTS, WGS_CUTS[1:]):
            for c in range(2):
                nc.sync.dma_start(weights[c:P:2, j0:j1], wgs_rows[:, 0:2, j0:j1])
        load_page(0)
        load_w1(1)
        nc.sync.dma_start(late_gains[:, 0:2], gain.rearrange("(p t) -> p t", t=PACK)[:, 2:4])
        load_late_weights(2)
        load_page(1)
        load_late_weights(3)
        load_page(2)
        nc.sync.dma_start(wd_raw.rearrange("p (j n) -> p j n", j=PACK), wd.rearrange("(p j) n -> p j n", j=PACK))
        load_page(3)
        nc.sync.dma_start(wc[:].bitcast(I32), wc_words[0].bitcast(I32))
        for q in range(QUADS):
            nc.sync.dma_start(
                wc_sc[QUAD * q : QUAD * q + 4, :].bitcast(I32),
                wc_scales[0, 4 * q : 4 * q + 4, :].bitcast(I32),
            )

        nc.scalar.copy(
            gain_dealt[:].rearrange("p (g q e c) -> p g q e c", g=2, e=2, c=2),
            gain_rows[:].rearrange("p (g c q f) -> p g q f c", g=2, c=2, f=PACK)[:, :, :, 0:2, :],
        )
        for g in range(2):
            nc.vector.transpose(gains[:, g * QUAD : (g + 1) * QUAD], gain_dealt[:, g * QUAD : (g + 1) * QUAD])

        def entries(lst, j0, j1):
            return lst[:] if (j0, j1) == (0, S) else lst[:, j0 // 16 : j1 // 16]

        paired_bf = [keep.tile([P, PASSES * P * PACK], BF16, name=f"paired_bf{g}", align_bytes=ALIGN) for g in range(2)]
        late_bf = keep.tile([P, 2 * PASSES * P * PACK], BF16, name="late_bf", align_bytes=ALIGN)

        def round_paired(g, a):
            nc.scalar.copy(
                paired_bf[g][:, a * P * PACK : (a + 1) * P * PACK].rearrange(
                    "p (q e c j) -> p q c j e", e=2, c=2, j=PACK
                ),
                w1_raw[g][a][:].rearrange("p (j c q f) -> p q c j f", j=PACK, c=2, f=PACK)[:, :, :, :, 0:2],
            )

        def round_late(g, a):
            nc.scalar.copy(
                late_bf[:].rearrange("p (e a g r j) -> p a g r j e", e=2, a=PASSES, g=2, j=PACK)[:, a, g],
                w1_raw[g][a][:].rearrange("p (j r f) -> p r j f", j=PACK, f=PACK)[:, :, :, 2:4],
            )

        def quantise(bf, name):
            width = bf.shape[1] // PACK
            codes = keep.tile([P, width], U32, name=f"{name}_q", align_bytes=ALIGN)
            bytes_ = keep.tile([P, width], U8, name=f"{name}_sc", align_bytes=ALIGN)
            nc.vector.quantize_mx(out=codes[:].bitcast(FP8X4), scales=bytes_[:], in_=bf[:])
            return codes, bytes_

        v = [keep.tile([P, S], U32, name=f"v{a}", align_bytes=ALIGN) for a in range(PASSES)]
        v_sc = keep.tile([P, S], U8, name="v_sc", align_bytes=ALIGN)
        nc.vector.tensor_copy(v[0][:], tab[0][:].indirect(pick[:]))
        nc.vector.tensor_copy(v_sc[:], tab_sc[:].indirect(pick[:]))
        for a in range(PASSES):
            round_paired(0, a)
        codes, bytes_ = quantise(paired_bf[0], "w1_0")
        w1_q = [(codes[:], bytes_[:])]
        for j0, j1 in FIRST + ((HALF, S),):
            nc.vector.tensor_copy(v[1][:, j0:j1], tab[1][:].indirect(entries(pick, j0, j1)))
        early_factors = keep.tile([P, 2 * S], F32, name="early_factors", align_bytes=ALIGN)
        for u in range(2):
            column = gains[:, u * QUAD : u * QUAD + 1]
            nc.gpsimd.tensor_scalar(early_factors[:, u * S : (u + 1) * S], weights[:], column, -0.0, ALU.mult, ALU.add)
        factors = [early_factors[:, 0:S], early_factors[:, S:], late_factors[0][:], late_factors[1][:]]

        squares = keep.tile([P, S], F32, name="squares", align_bytes=ALIGN)
        roots = keep.tile([P, S], F32, name="roots", align_bytes=ALIGN)
        resp = [keep.tile([P, S], F32, name=f"resp{u}", align_bytes=ALIGN) for u in range(TILES)]

        def slot(t, m0=0, m1=T2):
            return slots[:, t * T2 + m0 : t * T2 + m1]

        def multiply(acc, u, a, j0, j1):
            codes, bytes_ = w1_q[u]
            nc.tensor.matmul_mx(
                out=acc[:],
                lhsT=codes[:, a * P : (a + 1) * P].bitcast(FP8X4),
                lhsT_scale=bytes_[:, a * P : (a + 1) * P],
                rhs=v[a][:, j0:j1].bitcast(FP8X4),
                rhs_scale=v_sc[4 * a : P, j0:j1],
                start=(a == 0),
                stop=(a == PASSES - 1),
            )

        def square(u, j0, j1):
            acc = psum.tile([P, j1 - j0], F32, name="phase", bufs=BANKS)
            for a in range(PASSES):
                multiply(acc, u, a, j0, j1)
            nc.scalar.activation(squares[:, j0:j1], acc[:], ACT.Square)

        def respond(u, spans, root_at, resp_at):
            for span in spans:
                square(u, *span)
            for (j0, j1), dst in zip(spans, root_at):
                nc.scalar.activation(dst, squares[:, j0:j1], ACT.Abs_reciprocal_sqrt, bias=1.0)
            for src, dst in zip(root_at, resp_at):
                nc.scalar.activation(dst, src, ACT.Square)

        def scatter(u, j0, j1, src):
            nc.vector.tensor_tensor(page[u][:].indirect(entries(put, j0, j1)), src, factors[u][:, j0:j1], ALU.mult)

        def round_and_move(g):
            nc.scalar.copy(rounded[g][:], page[g][:])
            for c in range(2):
                for e in range(2):
                    p0 = 2 * QUAD * g + QUAD * c
                    nc.sync.dma_start(slot(e)[p0 : p0 + QUAD, :], rounded[g][2 * e + c : P : 4, :])

        halves = [(0, HALF), (HALF, S)]

        pieces = FIRST + ((HALF, S),)
        sums = [psum.tile([P, j1 - j0], F32, name="phase", bufs=BANKS) for j0, j1 in pieces]
        for a in range(PASSES):
            for acc, span in zip(sums, pieces):
                multiply(acc, 0, a, *span)
        for acc, (j0, j1) in zip(sums, FIRST):
            nc.scalar.activation(squares[:, j0:j1], acc[:], ACT.Square)
        for j0, j1 in FIRST:
            nc.scalar.activation(roots[:, j0:j1], squares[:, j0:j1], ACT.Abs_reciprocal_sqrt, bias=1.0)
        for j0, j1 in FIRST:
            nc.scalar.activation(resp[0][:, j0:j1], roots[:, j0:j1], ACT.Square)
        scatter(0, 0, HALF, resp[0][:, 0:HALF])
        for a in range(PASSES):
            round_late(0, a)
        round_paired(1, 0)
        round_late(1, 0)
        round_paired(1, 1)
        codes, bytes_ = quantise(paired_bf[1], "w1_1")
        w1_q.append((codes[:], bytes_[:]))
        spent = w1_raw[1][0][:, 0:HALF]
        nc.scalar.activation(squares[:, HALF:S], sums[-1][:], ACT.Square)
        nc.scalar.activation(roots[:, HALF:S], squares[:, HALF:S], ACT.Abs_reciprocal_sqrt, bias=1.0)
        nc.scalar.activation(spent, roots[:, HALF:S], ACT.Square)
        scatter(0, HALF, S, spent)
        round_late(1, 1)
        codes, bytes_ = quantise(late_bf, "w1_late")
        for e in range(2):
            cols = slice(e * PASSES * P, (e + 1) * PASSES * P)
            w1_q.append((codes[:, cols], bytes_[:, cols]))
        store_page(0)

        held = rounded[0][:].bitcast(F32)
        first = factors[2][:, 0:QUARTER]
        respond(1, [(0, QUARTER)], [held[:, 0:QUARTER]], [first])
        scatter(1, 0, QUARTER, first)
        nc.vector.tensor_scalar(factors[2], late_weights[0], late_gains[:, 0:1], None, ALU.mult)
        square(1, QUARTER, HALF)
        square(1, HALF, S)
        nc.scalar.activation(held[:, QUARTER:S], squares[:, QUARTER:S], ACT.Abs_reciprocal_sqrt, bias=1.0)
        nc.scalar.activation(resp[1][:, QUARTER:S], held[:, QUARTER:S], ACT.Square)
        scatter(1, QUARTER, S, resp[1][:, QUARTER:S])
        round_and_move(0)
        store_page(1)

        respond(2, halves, [factors[3][:, a:b] for a, b in halves], [resp[2][:, a:b] for a, b in halves])
        nc.scalar.activation(factors[3], late_weights[1], ACT.Copy, scale=late_gains[:, 1:2])
        scatter(2, 0, S, resp[2][:])
        round_and_move(1)
        store_page(2)

        wd_bf = keep.tile([P, PACK * N], BF16, name="wd_bf", align_bytes=ALIGN)
        last_roots = [wd_bf[:].bitcast(F32)[:, 0:HALF], slot(2).bitcast(F32)[:, 0:HALF]]
        respond(3, halves, last_roots, [resp[3][:, a:b] for a, b in halves])
        scatter(3, 0, S, resp[3][:])
        nc.scalar.activation(squares[:, S - 1 : S], one[:, 0:1], ACT.Sin)
        nc.scalar.copy(slot(2), page[2][:])
        nc.scalar.activation(
            wd_bf[:].rearrange("p (c i j) -> p c j i", i=WD_RUN, j=PACK),
            wd_raw.rearrange("p (j c i) -> p c j i", i=WD_RUN, j=PACK),
            ACT.Copy,
            scale=2.0,
        )
        store_page(3)

        words = keep.tile([P, T2], U32, name="words", align_bytes=ALIGN)
        scales = keep.tile([P, T2], U8, name="scales", align_bytes=ALIGN)
        words_dst = out_2[0].rearrange("p m t -> p (m t)").bitcast(I32)
        slot_view = slots[:, 0 : PACK * T2].rearrange("p (t m) -> p t m", t=PACK)

        def regroup(m0, m1):
            grouped = work.tile([P, (m1 - m0) * PACK], BF16, name="grouped", bufs=3, align_bytes=ALIGN)
            nc.vector.tensor_copy(
                grouped[:].rearrange("p (c i t) -> p c t i", i=RUN, t=PACK),
                slot_view[:, :, m0:m1].rearrange("p t (c i) -> p c t i", i=RUN),
            )
            return grouped

        def quantise_page(grouped, m0, m1):
            nc.vector.quantize_mx(out=words[:, m0:m1].bitcast(FP8X4), scales=scales[:, m0:m1], in_=grouped[:])
            if m1 % BANK == 0:
                nc.sync.dma_start(words_dst[:, m1 - BANK : m1], words[:, m1 - BANK : m1].bitcast(I32))

        def half_cosine(n, m0, m1):
            phase = psum.tile([P, m1 - m0], F32, name="phase", bufs=BANKS)
            nc.tensor.matmul_mx(
                out=phase[:],
                lhsT=wc[:, 2 * n * P : 2 * (n + 1) * P].bitcast(FP4X4),
                lhsT_scale=wc_sc[:, n * P : (n + 1) * P],
                rhs=words[:, m0:m1].bitcast(FP8X4),
                rhs_scale=scales[:, m0:m1],
                start=True,
                stop=True,
            )
            half_cos = work.tile([P, m1 - m0], F32, name="half_cos", bufs=BANKS, align_bytes=ALIGN)
            nc.scalar.activation(half_cos[:], phase[:], ACT.Sin, scale=0.5, bias=math.pi / 2)
            return half_cos

        def finish(half_cos, n, m0, m1, free):
            value = psum.tile([P, m1 - m0], F32, name="value", bufs=BANKS)
            cols = slice(n * P, (n + 1) * P)
            nc.tensor.matmul_mx(
                out=value[:],
                lhsT=wd_q[:, cols].bitcast(FP8X4),
                lhsT_scale=wd_sc[:, cols],
                rhs=words[:, m0:m1].bitcast(FP8X4),
                rhs_scale=scales[:, m0:m1],
                start=True,
                stop=True,
            )
            if free is None:
                cos_tile = work.tile([P, m1 - m0], F32, name="cos_up", bufs=BANKS, align_bytes=ALIGN)
                cos_up = cos_tile[:]
                nc.scalar.activation(cos_up, half_cos[:], ACT.Square)
            else:
                cos_up = free
                nc.gpsimd.tensor_tensor(cos_up, half_cos[:], half_cos[:], ALU.mult)
            y = work.tile([P, m1 - m0], F32, name="y", bufs=2 * BANKS, align_bytes=ALIGN)
            nc.vector.scalar_tensor_tensor(y[:], cos_up, -0.5, value[:], ALU.add, ALU.mult)
            nc.sync.dma_start(out_0[n * P : (n + 1) * P, m0:m1], y[:])

        wd_q = keep.tile([P, N], U32, name="wd_q", tag="resp3", align_bytes=ALIGN)
        wd_sc = keep.tile([P, N], U8, name="wd_sc", align_bytes=ALIGN)
        for n0, n1 in ((0, P), (P, N)):
            nc.vector.quantize_mx(
                out=wd_q[:, n0:n1].bitcast(FP8X4), scales=wd_sc[:, n0:n1], in_=wd_bf[:, n0 * PACK : n1 * PACK]
            )
        spans = [(0, PIECE), (PIECE, BANK)] + [(c * BANK, (c + 1) * BANK) for c in range(1, CHUNKS)]
        for m0, m1 in spans:
            nc.scalar.copy(slot(3, m0, m1), page[3][:, m0:m1])
        ahead = 2
        for span in spans[0 : ahead + 1]:
            quantise_page(regroup(*span), *span)

        behind = None
        count = 0
        for i, whole in enumerate(spans):
            if 1 <= i < len(spans) - ahead:
                last_grouped = regroup(*spans[i + ahead])
                quantise_page(last_grouped, *spans[i + ahead])
            if i + ahead + 1 == len(spans):
                for q in range(QUADS):
                    nc.sync.dma_start(
                        out_3[0, 4 * q : 4 * q + 4, :].bitcast(I32),
                        scales[QUAD * q : QUAD * q + 4, :].bitcast(I32),
                    )
            for n in range(NT):
                m0, m1 = whole
                final = i + 1 == len(spans) and n + 1 == NT
                for piece in ((m0, m1 - PIECE), (m1 - PIECE, m1)) if final else (whole,):
                    free = None
                    if count in ON_GPSIMD:
                        at = ON_GPSIMD.index(count) % 2 * BANK
                        free = last_grouped[:].bitcast(F32)[:, at : at + BANK]
                    now = (half_cosine(n, *piece), n, *piece, free)
                    count = count + 1
                    if behind is not None:
                        finish(*behind)
                    behind = now
        finish(*behind)
